import numpy as np
import ml_dtypes


def mxq(x, axis, fmt="e4m3"):
    dtype, down = {"e4m3": (ml_dtypes.float8_e4m3fn, 7), "e5m2": (ml_dtypes.float8_e5m2, 14)}[fmt]
    v = np.moveaxis(np.asarray(x, np.float32).astype(ml_dtypes.bfloat16).astype(np.float64), axis, -1)
    blocks = v.reshape(v.shape[:-1] + (-1, 32))
    amax = np.abs(blocks).max(-1, keepdims=True)
    byte = np.maximum(np.where(amax > 0, np.frexp(amax)[1] - 1 + 127, 0) - down, 1)
    scale = np.exp2(byte - 127.0)
    codes = (blocks / scale).astype(np.float32).astype(dtype).astype(np.float64)
    return np.moveaxis((codes * scale).reshape(v.shape), -1, axis)


WIDE = False


def mx_kscale(k):
    if not WIDE:
        return np.ones(k)
    levels = np.array([18, -18])
    if k % 512:
        return np.exp2(np.random.permutation(np.resize(levels, k // 32))).repeat(32)
    a = np.empty((k // 512, 16))
    for p in range(k // 512):
        a[p, :8] = np.random.permutation(np.resize(levels, 8))
        for g in range(8):
            far = levels[np.abs(levels - a[p, g]) >= 10]
            a[p, g + 8] = far[np.random.randint(len(far))]
    return np.exp2(a.ravel()).repeat(32)


def f64(x):
    return np.asarray(x).astype(np.float64)


def striped(idx):
    return np.tile(np.asarray(idx).reshape(-1, 16).T, (8, 1)).astype(np.uint16)


def unstriped(offs):
    return offs[:16].T.reshape(-1).astype(np.int64)


E2M1 = np.array([0.0, 0.5, 1.0, 1.5, 2.0, 3.0, 4.0, 6.0, -0.0, -0.5, -1.0, -1.5, -2.0, -3.0, -4.0, -6.0])


def pack_weight(w, fmt):
    k, n = w.shape
    w = f64(np.asarray(w, np.float32).astype(ml_dtypes.bfloat16)).reshape(k // 32, 32, n)
    amax = np.abs(w).max(1)
    if fmt == "e4m3":
        byte = np.frexp(amax)[1] - 1 + 127 - 7
    else:
        mant, ex = np.frexp(amax / 6.0)
        byte = np.where(mant > 0.5, ex, ex - 1) + 127
    byte = np.clip(np.where(amax > 0, byte, 1), 1, 254)
    scaled = (w * np.exp2(127.0 - byte)[:, None, :]).reshape(k, n).astype(np.float32)
    by_word = np.ascontiguousarray(scaled.reshape(k // 512, 128, 4, n).transpose(0, 1, 3, 2))
    if fmt == "e4m3":
        words = by_word.astype(ml_dtypes.float8_e4m3fn).view(np.uint8)
    else:
        c = by_word.astype(ml_dtypes.float4_e2m1fn).view(np.uint8) & 0xF
        words = (c[..., 0::2] | (c[..., 1::2] << 4)).reshape(k // 512, 128, 2 * n)
    return np.ascontiguousarray(words), np.ascontiguousarray(byte.astype(np.uint8).reshape(k // 512, 16, n))


def unpack_weight(words, scales, fmt):
    g, _, n = scales.shape
    words = np.ascontiguousarray(words).reshape(g, 128, n, -1)
    if fmt == "e4m3":
        vals = words.view(ml_dtypes.float8_e4m3fn).astype(np.float64)
    else:
        nib = np.empty((g, 128, n, 4), np.uint8)
        nib[..., 0::2] = words & 0xF
        nib[..., 1::2] = words >> 4
        vals = E2M1[nib]
    vals = vals * np.repeat(np.exp2(scales.astype(np.float64) - 127.0), 8, axis=1)[..., None]
    return vals.transpose(0, 1, 3, 2).reshape(g * 512, n)


N, T, D, V = 512, 2048, 512, 512


def setup_inputs():
    n = np.random.standard_normal
    idx = np.random.permutation(T)[:N]
    s = mx_kscale(D)[:, None]
    z = mx_kscale(V)[:, None]
    w = n((D, V)) / np.sqrt(D)
    wd, wv = pack_weight(w * s, "e2m1"), pack_weight(w.T / z, "e2m1")
    return {
        "xT": (n((D, T)) / s).astype(np.float32),
        "wd_words": wd[0],
        "wd_scales": wd[1],
        "wv_words": wv[0],
        "wv_scales": wv[1],
        "y": np.random.randint(0, 2, (V, N)).astype(np.float32),
        "cw": (np.random.uniform(0.5, 1.5, (V, 1)) / np.sqrt(V) * z).astype(np.float32),
        "rw": np.tile(np.random.uniform(0.5, 1.5, N), (128, 1)).astype(np.float32),
        "offs": striped(idx),
    }


def reference(xT, wd_words, wd_scales, wv_words, wv_scales, y, cw, rw, offs):
    idx = unstriped(offs)
    a = unpack_weight(wd_words, wd_scales, "e2m1").T @ mxq(f64(xT)[:, idx], 0, "e4m3")
    g = f64(cw) * f64(rw)[:1] * (1.0 / (1.0 + np.exp(-a)) - f64(y))
    dx = unpack_weight(wv_words, wv_scales, "e2m1").T @ mxq(g, 0, "e5m2")
    gx = np.zeros((D, T))
    gx[:, idx] = dx
    return gx

@@ -1,0 +1,194 @@
+from contextlib import ExitStack
+
+import concourse.mybir as mybir
+from concourse.masks import make_identity
+
+N, T, D, V = 512, 2048, 512, 512
+FLOPS = 2 * 2 * N * D * V
+
+F32 = mybir.dt.float32
+BF16 = mybir.dt.bfloat16
+I32 = mybir.dt.int32
+U32 = mybir.dt.uint32
+U16 = mybir.dt.uint16
+U8 = mybir.dt.uint8
+E4M3X4 = mybir.dt.float8_e4m3fn_x4
+E5M2X4 = mybir.dt.float8_e5m2_x4
+E2M1X4 = mybir.dt.float4_e2m1fn_x4
+ACT = mybir.ActivationFunctionType
+ALU = mybir.AluOpType
+
+P = 128
+PACK = 4
+HALF = N // 2
+LIST_COLS = HALF // 16
+EARLY_TILES = 2
+
+
+def load_scale_rows(queue, tile, scales):
+    for q in range(4):
+        queue.dma_start(
+            out=tile[32 * q : 32 * q + 4, :].bitcast(I32),
+            in_=scales[0, 4 * q : 4 * q + 4, :].bitcast(I32),
+        )
+
+
+def tile_attend_gml_nce_kernel(tc, xT, wd_words, wd_scales, wv_words, wv_scales, y, cw, rw, offs, out):
+    nc = tc.nc
+    with ExitStack() as ctx:
+        sb = ctx.enter_context(tc.tile_pool(name="sb", bufs=1))
+        ps = ctx.enter_context(tc.psum_pool(name="ps", bufs=1))
+
+        x_rows = xT.rearrange("(p t) n -> p t n", t=PACK)
+        y_rows = y.rearrange("(p r) n -> p r n", r=PACK)
+        x_plane = [sb.tile([P, T], F32, name=f"x_plane{t}") for t in range(PACK)]
+        y_half = [sb.tile([P, PACK, HALF], F32, name=f"y_half{h}") for h in range(2)]
+        offsets = sb.tile([P, N // 16], U16, name="offsets")
+        cw4 = sb.tile([P, PACK], F32, name="cw4")
+        rw4 = sb.tile([P, PACK], F32, name="rw4")
+        wd_raw = sb.tile([P, 2 * V], U8, name="wd_raw", align_bytes=64)
+        wd_scale_raw = sb.tile([P, V], U8, name="wd_scale_raw", align_bytes=64)
+        wv_codes = sb.tile([P, 2 * D], U8, name="wv_codes", align_bytes=64)
+        wv_scale = sb.tile([P, D], U8, name="wv_scale", align_bytes=64)
+        g_codes = sb.tile([P, HALF + N], U32, name="g_codes", align_bytes=64)
+        g_scale = sb.tile([P, HALF + N], U8, name="g_scale", align_bytes=64)
+        ident = sb.tile([P, P], F32, name="ident")
+
+        nc.gpsimd.memset(wd_scale_raw[:].bitcast(I32), 0)
+        nc.gpsimd.memset(wv_scale[:].bitcast(I32), 0)
+        nc.gpsimd.memset(g_codes[:, 0:HALF], 0)
+        nc.gpsimd.memset(g_scale[:, 0:HALF].bitcast(I32), 0)
+        make_identity(nc, ident[:])
+
+        nc.sync.dma_start(out=x_plane[0][:], in_=x_rows[:, 0, :])
+        nc.sync.dma_start(offsets[:], offs)
+        nc.scalar.dma_start(out=rw4[:], in_=rw[0].rearrange("(p j) -> p j", j=PACK))
+        nc.scalar.dma_start(out=cw4[:], in_=cw.rearrange("(p r) o -> p (r o)", r=PACK))
+        nc.scalar.dma_start(out=wd_raw[:].bitcast(I32), in_=wd_words[0].bitcast(I32))
+        load_scale_rows(nc.scalar, wd_scale_raw, wd_scales)
+        for t in range(1, PACK):
+            nc.sync.dma_start(out=x_plane[t][:], in_=x_rows[:, t, :])
+        nc.sync.dma_start(out=y_half[0][:], in_=y_rows[:, :, 0:HALF])
+        nc.sync.dma_start(out=wv_codes[:].bitcast(I32), in_=wv_words[0].bitcast(I32))
+        load_scale_rows(nc.sync, wv_scale, wv_scales)
+        nc.sync.dma_start(out=y_half[1][:], in_=y_rows[:, :, HALF:N])
+
+        window = [sb.tile([P, T], F32, name=f"window{j}") for j in range(PACK)]
+        for j in range(PACK):
+            nc.vector.memset(window[j][:], 0.0)
+
+        warm = sb.tile([P, 1], F32, name="warm")
+        nc.scalar.activation(out=warm[:], in_=ident[:, 0:1], func=ACT.Sigmoid)
+
+        rw_bank = ps.tile([P, PACK, P], F32, name="rw_bank", tag="bank7")
+        for j in range(PACK):
+            nc.tensor.transpose(rw_bank[:, j, :], rw4[:, j : j + 1].to_broadcast([P, P]), ident[:])
+        weight = sb.tile([P, PACK, N], F32, name="weight")
+        for r in range(PACK):
+            nc.scalar.activation(
+                out=weight[:, r, :].rearrange("q (p j) -> q p j", j=PACK),
+                in_=rw_bank[:].rearrange("q j p -> q p j"),
+                func=ACT.Copy,
+                scale=cw4[:, r : r + 1],
+            )
+
+        wd_codes = sb.tile([P, 2 * V], U8, name="wd_codes", align_bytes=64)
+        wd_scale = sb.tile([P, V], U8, name="wd_scale", align_bytes=64)
+
+        x_words = [sb.tile([P, HALF, PACK], BF16, name=f"x_words{h}", align_bytes=64) for h in range(2)]
+        x_codes = [sb.tile([P, HALF], U32, name=f"x_codes{h}", align_bytes=64) for h in range(2)]
+        x_scale = [sb.tile([P, HALF], U8, name=f"x_scale{h}", align_bytes=64) for h in range(2)]
+
+        def half_list(h):
+            return offsets[:, h * LIST_COLS : (h + 1) * LIST_COLS]
+
+        def gather(t, h):
+            nc.vector.tensor_copy(out=x_words[h][:, :, t], in_=x_plane[t][:].indirect(half_list(h)))
+
+        for t in range(PACK - 1):
+            for h in range(2):
+                gather(t, h)
+            if t == 0:
+                nc.vector.tensor_copy(
+                    out=wd_codes[:].bitcast(U16).rearrange("p (r s) -> p s r", r=PACK),
+                    in_=wd_raw[:].bitcast(U16).rearrange("p (s r) -> p s r", r=PACK),
+                )
+                nc.vector.tensor_copy(
+                    out=wd_scale[:].rearrange("p (r s) -> p s r", r=PACK),
+                    in_=wd_scale_raw[:].rearrange("p (s r) -> p s r", r=PACK),
+                )
+
+        sig = [sb.tile([P, PACK, HALF], F32, name=f"sig{h}") for h in range(2)]
+        for h in range(2):
+            gather(PACK - 1, h)
+            nc.vector.quantize_mx(
+                out=x_codes[h][:].bitcast(E4M3X4), scales=x_scale[h][:], in_=x_words[h][:].rearrange("p n t -> p (n t)")
+            )
+            for b in range(2):
+                score = ps.tile([P, 2, HALF], F32, name=f"score{h}{b}", tag=f"bank{2 * h + b}")
+                for u in range(2):
+                    r = 2 * b + u
+                    nc.tensor.matmul_mx(
+                        out=score[:, u, :],
+                        lhsT=wd_codes[:, 2 * P * r : 2 * P * (r + 1)].bitcast(E2M1X4),
+                        lhsT_scale=wd_scale[:, P * r : P * (r + 1)],
+                        rhs=x_codes[h][:].bitcast(E4M3X4),
+                        rhs_scale=x_scale[h][:],
+                        start=True,
+                        stop=True,
+                    )
+                nc.scalar.activation(out=sig[h][:, 2 * b : 2 * b + 2, :], in_=score[:], func=ACT.Sigmoid)
+
+        def back(j, first, bank):
+            acc = ps.tile([P, N], F32, name=f"acc{j}_{first}", tag=f"bank{bank}")
+            nc.tensor.matmul_mx(
+                out=acc[:],
+                lhsT=wv_codes[:, 2 * P * j : 2 * P * (j + 1)].bitcast(E2M1X4),
+                lhsT_scale=wv_scale[:, P * j : P * (j + 1)],
+                rhs=g_codes[:, first : first + N].bitcast(E5M2X4),
+                rhs_scale=g_scale[:, first : first + N],
+                start=True,
+                stop=True,
+            )
+            return acc
+
+        def gradient(h):
+            diff = sb.tile([P, PACK, HALF], F32, name=f"diff{h}")
+            for b in range(2):
+                planes = slice(2 * b, 2 * b + 2)
+                nc.vector.tensor_tensor(diff[:, planes, :], sig[h][:, planes, :], y_half[h][:, planes, :], ALU.subtract)
+            g_words = sb.tile([P, HALF, PACK], BF16, name=f"g_words{h}", align_bytes=64)
+            nc.vector.tensor_tensor(
+                g_words[:].rearrange("p (c i) r -> p c r i", i=4),
+                diff[:].rearrange("p r (c i) -> p c r i", i=4),
+                weight[:, :, h * HALF : (h + 1) * HALF].rearrange("p r (c i) -> p c r i", i=4),
+                ALU.mult,
+            )
+            cols = slice((h + 1) * HALF, (h + 2) * HALF)
+            nc.vector.quantize_mx(
+                out=g_codes[:, cols].bitcast(E5M2X4), scales=g_scale[:, cols], in_=g_words[:].rearrange("p n r -> p (n r)")
+            )
+
+        pieces = []
+        gradient(0)
+        for j in range(EARLY_TILES):
+            acc = back(j, 0, 4 + j)
+            dx = sb.tile([P, HALF], F32, name=f"dx_early{j}")
+            nc.scalar.copy(out=dx[:], in_=acc[:, HALF:N])
+            pieces.append((j, dx, half_list(0), False))
+        gradient(1)
+        for j in range(PACK):
+            acc = back(j, HALF, (6 + j) % 8)
+            if j < EARLY_TILES:
+                dx = sb.tile([P, HALF], F32, name=f"dx_late{j}")
+                nc.scalar.copy(out=dx[:], in_=acc[:, HALF:N])
+                pieces.append((j, dx, half_list(1), True))
+            else:
+                dx = sb.tile([P, N], F32, name=f"dx_whole{j}")
+                nc.scalar.copy(out=dx[:], in_=acc[:])
+                pieces.append((j, dx, offsets[:], True))
+
+        for j, dx, entries, last in pieces:
+            nc.vector.tensor_copy(out=window[j][:].indirect(entries), in_=dx[:])
+            if last:
+                nc.sync.dma_start(out=out[P * j : P * (j + 1), :], in_=window[j][:])

@@ -23,14 +23,14 @@ PACK = 4
 HALF = N // 2
 LIST_COLS = HALF // 16
 EARLY_TILES = 2
+OVERLAP = 32
 
 
-def load_scale_rows(queue, tile, scales):
-    for q in range(4):
-        queue.dma_start(
-            out=tile[32 * q : 32 * q + 4, :].bitcast(I32),
-            in_=scales[0, 4 * q : 4 * q + 4, :].bitcast(I32),
-        )
+def load_scale_rows(queue, tile, scales, q):
+    queue.dma_start(
+        out=tile[32 * q : 32 * q + 4, :].bitcast(I32),
+        in_=scales[0, 4 * q : 4 * q + 4, :].bitcast(I32),
+    )
 
 
 def tile_attend_gml_nce_kernel(tc, xT, wd_words, wd_scales, wv_words, wv_scales, y, cw, rw, offs, out):
@@ -41,7 +41,7 @@ def tile_attend_gml_nce_kernel(tc, xT, wd_words, wd_scales, wv_words, wv_scales,
 
         x_rows = xT.rearrange("(p t) n -> p t n", t=PACK)
         y_rows = y.rearrange("(p r) n -> p r n", r=PACK)
-        x_plane = [sb.tile([P, T], F32, name=f"x_plane{t}") for t in range(PACK)]
+        x_plane = [sb.tile([P, T], F32, name=f"x_plane{t}", tag=f"wide{t}", align_bytes=64) for t in range(PACK)]
         y_half = [sb.tile([P, PACK, HALF], F32, name=f"y_half{h}") for h in range(2)]
         offsets = sb.tile([P, N // 16], U16, name="offsets")
         cw4 = sb.tile([P, PACK], F32, name="cw4")
@@ -61,21 +61,24 @@ def tile_attend_gml_nce_kernel(tc, xT, wd_words, wd_scales, wv_words, wv_scales,
         make_identity(nc, ident[:])
 
         nc.sync.dma_start(out=x_plane[0][:], in_=x_rows[:, 0, :])
-        nc.sync.dma_start(offsets[:], offs)
-        nc.scalar.dma_start(out=rw4[:], in_=rw[0].rearrange("(p j) -> p j", j=PACK))
-        nc.scalar.dma_start(out=cw4[:], in_=cw.rearrange("(p r) o -> p (r o)", r=PACK))
         nc.scalar.dma_start(out=wd_raw[:].bitcast(I32), in_=wd_words[0].bitcast(I32))
-        load_scale_rows(nc.scalar, wd_scale_raw, wd_scales)
-        for t in range(1, PACK):
-            nc.sync.dma_start(out=x_plane[t][:], in_=x_rows[:, t, :])
+        for q in range(4):
+            load_scale_rows(nc.scalar, wd_scale_raw, wd_scales, q)
+        nc.sync.dma_start(offsets[:], offs)
+        nc.sync.dma_start(out=x_plane[1][:], in_=x_rows[:, 1, :])
+        nc.sync.dma_start(out=rw4[:], in_=rw[0].rearrange("(p j) -> p j", j=PACK))
+        nc.sync.dma_start(out=cw4[:], in_=cw.rearrange("(p r) o -> p (r o)", r=PACK))
+        nc.sync.dma_start(out=x_plane[2][:], in_=x_rows[:, 2, :])
+        nc.sync.dma_start(out=x_plane[3][:], in_=x_rows[:, 3, :])
         nc.sync.dma_start(out=y_half[0][:], in_=y_rows[:, :, 0:HALF])
-        nc.sync.dma_start(out=wv_codes[:].bitcast(I32), in_=wv_words[0].bitcast(I32))
-        load_scale_rows(nc.sync, wv_scale, wv_scales)
         nc.sync.dma_start(out=y_half[1][:], in_=y_rows[:, :, HALF:N])
+        nc.sync.dma_start(out=wv_codes[:].bitcast(I32), in_=wv_words[0].bitcast(I32))
+        for q in range(4):
+            load_scale_rows(nc.sync, wv_scale, wv_scales, q)
 
         window = [sb.tile([P, T], F32, name=f"window{j}") for j in range(PACK)]
         for j in range(PACK):
-            nc.vector.memset(window[j][:], 0.0)
+            (nc.vector if j < 2 else nc.gpsimd).memset(window[j][:].bitcast(I32), 0)
 
         warm = sb.tile([P, 1], F32, name="warm")
         nc.scalar.activation(out=warm[:], in_=ident[:, 0:1], func=ACT.Sigmoid)
@@ -92,42 +95,45 @@ def tile_attend_gml_nce_kernel(tc, xT, wd_words, wd_scales, wv_words, wv_scales,
                 scale=cw4[:, r : r + 1],
             )
 
-        wd_codes = sb.tile([P, 2 * V], U8, name="wd_codes", align_bytes=64)
-        wd_scale = sb.tile([P, V], U8, name="wd_scale", align_bytes=64)
 
-        x_words = [sb.tile([P, HALF, PACK], BF16, name=f"x_words{h}", align_bytes=64) for h in range(2)]
+        x_words = sb.tile([P, N, PACK], BF16, name="x_words", align_bytes=64)
         x_codes = [sb.tile([P, HALF], U32, name=f"x_codes{h}", align_bytes=64) for h in range(2)]
         x_scale = [sb.tile([P, HALF], U8, name=f"x_scale{h}", align_bytes=64) for h in range(2)]
 
         def half_list(h):
             return offsets[:, h * LIST_COLS : (h + 1) * LIST_COLS]
 
-        def gather(t, h):
-            nc.vector.tensor_copy(out=x_words[h][:, :, t], in_=x_plane[t][:].indirect(half_list(h)))
+        def gather(t, first, end):
+            nc.vector.tensor_copy(
+                out=x_words[:, first:end, t], in_=x_plane[t][:].indirect(offsets[:, first // 16 : end // 16])
+            )
 
         for t in range(PACK - 1):
-            for h in range(2):
-                gather(t, h)
-            if t == 0:
+            gather(t, 0, N)
+            if t == 1:
+                wd_dealt = sb.tile([P, 3 * V], U8, name="wd_dealt", tag="wide1", align_bytes=64)
+                wd_codes = wd_dealt[:, 0 : 2 * V]
+                wd_scale = wd_dealt[:, 2 * V : 3 * V]
                 nc.vector.tensor_copy(
-                    out=wd_codes[:].bitcast(U16).rearrange("p (r s) -> p s r", r=PACK),
+                    out=wd_codes.bitcast(U16).rearrange("p (r s) -> p s r", r=PACK),
                     in_=wd_raw[:].bitcast(U16).rearrange("p (s r) -> p s r", r=PACK),
                 )
                 nc.vector.tensor_copy(
-                    out=wd_scale[:].rearrange("p (r s) -> p s r", r=PACK),
+                    out=wd_scale.rearrange("p (r s) -> p s r", r=PACK),
                     in_=wd_scale_raw[:].rearrange("p (s r) -> p s r", r=PACK),
                 )
 
         sig = [sb.tile([P, PACK, HALF], F32, name=f"sig{h}") for h in range(2)]
         for h in range(2):
-            gather(PACK - 1, h)
+            gather(PACK - 1, h * (HALF - OVERLAP), (h + 1) * HALF)
             nc.vector.quantize_mx(
-                out=x_codes[h][:].bitcast(E4M3X4), scales=x_scale[h][:], in_=x_words[h][:].rearrange("p n t -> p (n t)")
+                out=x_codes[h][:].bitcast(E4M3X4), scales=x_scale[h][:], in_=x_words[:, h * HALF : (h + 1) * HALF, :].rearrange("p n t -> p (n t)")
             )
-            for b in range(2):
-                score = ps.tile([P, 2, HALF], F32, name=f"score{h}{b}", tag=f"bank{2 * h + b}")
-                for u in range(2):
-                    r = 2 * b + u
+            per_bank = 1 + h
+            for b in range(PACK // per_bank):
+                score = ps.tile([P, per_bank, HALF], F32, name=f"score{h}{b}", tag=f"bank{PACK * h + b}")
+                for u in range(per_bank):
+                    r = per_bank * b + u
                     nc.tensor.matmul_mx(
                         out=score[:, u, :],
                         lhsT=wd_codes[:, 2 * P * r : 2 * P * (r + 1)].bitcast(E2M1X4),
@@ -137,7 +143,8 @@ def tile_attend_gml_nce_kernel(tc, xT, wd_words, wd_scales, wv_words, wv_scales,
                         start=True,
                         stop=True,
                     )
-                nc.scalar.activation(out=sig[h][:, 2 * b : 2 * b + 2, :], in_=score[:], func=ACT.Sigmoid)
+                nc.scalar.activation(out=sig[h][:, per_bank * b : per_bank * (b + 1), :], in_=score[:], func=ACT.Sigmoid)
+
 
         def back(j, first, bank):
             acc = ps.tile([P, N], F32, name=f"acc{j}_{first}", tag=f"bank{bank}")
@@ -152,43 +159,51 @@ def tile_attend_gml_nce_kernel(tc, xT, wd_words, wd_scales, wv_words, wv_scales,
             )
             return acc
 
-        def gradient(h):
-            diff = sb.tile([P, PACK, HALF], F32, name=f"diff{h}")
-            for b in range(2):
-                planes = slice(2 * b, 2 * b + 2)
-                nc.vector.tensor_tensor(diff[:, planes, :], sig[h][:, planes, :], y_half[h][:, planes, :], ALU.subtract)
-            g_words = sb.tile([P, HALF, PACK], BF16, name=f"g_words{h}", align_bytes=64)
+        diff = [sb.tile([P, PACK, HALF], F32, name=f"diff{h}") for h in range(2)]
+        g_words = [sb.tile([P, HALF, PACK], BF16, name=f"g_words{h}", align_bytes=64) for h in range(2)]
+
+        def subtract(h, planes):
+            nc.vector.tensor_tensor(diff[h][:, planes, :], sig[h][:, planes, :], y_half[h][:, planes, :], ALU.subtract)
+
+        def weigh(h):
             nc.vector.tensor_tensor(
-                g_words[:].rearrange("p (c i) r -> p c r i", i=4),
-                diff[:].rearrange("p r (c i) -> p c r i", i=4),
+                g_words[h][:].rearrange("p (c i) r -> p c r i", i=4),
+                diff[h][:].rearrange("p r (c i) -> p c r i", i=4),
                 weight[:, :, h * HALF : (h + 1) * HALF].rearrange("p r (c i) -> p c r i", i=4),
                 ALU.mult,
             )
+
+        def quantize_g(h):
             cols = slice((h + 1) * HALF, (h + 2) * HALF)
             nc.vector.quantize_mx(
-                out=g_codes[:, cols].bitcast(E5M2X4), scales=g_scale[:, cols], in_=g_words[:].rearrange("p n r -> p (n r)")
+                out=g_codes[:, cols].bitcast(E5M2X4), scales=g_scale[:, cols], in_=g_words[h][:].rearrange("p n r -> p (n r)")
             )
 
+        for r in range(PACK):
+            subtract(0, slice(r, r + 1))
+        subtract(1, slice(0, 2))
+        weigh(0)
+        subtract(1, slice(2, 4))
+        quantize_g(0)
+        early = [back(j, 0, 6 + j) for j in range(EARLY_TILES)]
+        weigh(1)
+        quantize_g(1)
         pieces = []
-        gradient(0)
-        for j in range(EARLY_TILES):
-            acc = back(j, 0, 4 + j)
-            dx = sb.tile([P, HALF], F32, name=f"dx_early{j}")
-            nc.scalar.copy(out=dx[:], in_=acc[:, HALF:N])
-            pieces.append((j, dx, half_list(0), False))
-        gradient(1)
+        for j, spent in enumerate((sig[1], diff[1])):
+            nc.scalar.copy(out=spent[:, PACK - 1, :], in_=early[j][:, HALF:N])
+            pieces.append((j, spent[:, PACK - 1, :], half_list(0), False))
         for j in range(PACK):
-            acc = back(j, HALF, (6 + j) % 8)
+            acc = back(j, HALF, j)
             if j < EARLY_TILES:
                 dx = sb.tile([P, HALF], F32, name=f"dx_late{j}")
                 nc.scalar.copy(out=dx[:], in_=acc[:, HALF:N])
-                pieces.append((j, dx, half_list(1), True))
+                pieces.append((j, dx[:], half_list(1), True))
             else:
                 dx = sb.tile([P, N], F32, name=f"dx_whole{j}")
                 nc.scalar.copy(out=dx[:], in_=acc[:])
-                pieces.append((j, dx, offsets[:], True))
+                pieces.append((j, dx[:], offsets[:], True))
 
         for j, dx, entries, last in pieces:
-            nc.vector.tensor_copy(out=window[j][:].indirect(entries), in_=dx[:])
+            nc.vector.tensor_copy(out=window[j][:].indirect(entries), in_=dx)
             if last:
                 nc.sync.dma_start(out=out[P * j : P * (j + 1), :], in_=window[j][:])

@@ -123,28 +123,35 @@ def tile_attend_gml_nce_kernel(tc, xT, wd_words, wd_scales, wv_words, wv_scales,
                     in_=wd_scale_raw[:].rearrange("p (s r) -> p s r", r=PACK),
                 )
 
-        sig = [sb.tile([P, PACK, HALF], F32, name=f"sig{h}") for h in range(2)]
-        for h in range(2):
-            gather(PACK - 1, h * (HALF - OVERLAP), (h + 1) * HALF)
+        def quantize_x(h):
             nc.vector.quantize_mx(
-                out=x_codes[h][:].bitcast(E4M3X4), scales=x_scale[h][:], in_=x_words[:, h * HALF : (h + 1) * HALF, :].rearrange("p n t -> p (n t)")
+                out=x_codes[h][:].bitcast(E4M3X4),
+                scales=x_scale[h][:],
+                in_=x_words[:, HALF * h : HALF * (h + 1), :].rearrange("p n t -> p (n t)"),
             )
-            per_bank = 1 + h
-            for b in range(PACK // per_bank):
-                score = ps.tile([P, per_bank, HALF], F32, name=f"score{h}{b}", tag=f"bank{PACK * h + b}")
-                for u in range(per_bank):
-                    r = per_bank * b + u
-                    nc.tensor.matmul_mx(
-                        out=score[:, u, :],
-                        lhsT=wd_codes[:, 2 * P * r : 2 * P * (r + 1)].bitcast(E2M1X4),
-                        lhsT_scale=wd_scale[:, P * r : P * (r + 1)],
-                        rhs=x_codes[h][:].bitcast(E4M3X4),
-                        rhs_scale=x_scale[h][:],
-                        start=True,
-                        stop=True,
-                    )
-                nc.scalar.activation(out=sig[h][:, per_bank * b : per_bank * (b + 1), :], in_=score[:], func=ACT.Sigmoid)
 
+        def scores(h, planes, bank):
+            score = ps.tile([P, len(planes), HALF], F32, name=f"score{bank}", tag=f"bank{bank}")
+            for u, r in enumerate(planes):
+                nc.tensor.matmul_mx(
+                    out=score[:, u, :],
+                    lhsT=wd_codes[:, 2 * P * r : 2 * P * (r + 1)].bitcast(E2M1X4),
+                    lhsT_scale=wd_scale[:, P * r : P * (r + 1)],
+                    rhs=x_codes[h][:].bitcast(E4M3X4),
+                    rhs_scale=x_scale[h][:],
+                    start=True,
+                    stop=True,
+                )
+            sig = sb.tile([P, len(planes), HALF], F32, name=f"sig{bank}")
+            nc.scalar.activation(out=sig[:], in_=score[:], func=ACT.Sigmoid)
+            return sig
+
+        gather(PACK - 1, 0, HALF)
+        quantize_x(0)
+        sig_first = [scores(0, [r], r) for r in range(PACK)]
+        gather(PACK - 1, HALF - OVERLAP, N)
+        quantize_x(1)
+        sig_second = [scores(1, [2 * b, 2 * b + 1], 4 + b) for b in range(2)]
 
         def back(j, first, bank):
             acc = ps.tile([P, N], F32, name=f"acc{j}_{first}", tag=f"bank{bank}")
@@ -159,39 +166,58 @@ def tile_attend_gml_nce_kernel(tc, xT, wd_words, wd_scales, wv_words, wv_scales,
             )
             return acc
 
-        diff = [sb.tile([P, PACK, HALF], F32, name=f"diff{h}") for h in range(2)]
-        g_words = [sb.tile([P, HALF, PACK], BF16, name=f"g_words{h}", align_bytes=64) for h in range(2)]
+        diff = [sb.tile([P, 2, PACK, P], F32, name=f"diff{h}") for h in range(2)]
+        g_words = [sb.tile([P, 2, P * PACK], BF16, name=f"g_words{h}", align_bytes=64) for h in range(2)]
 
-        def subtract(h, planes):
-            nc.vector.tensor_tensor(diff[h][:, planes, :], sig[h][:, planes, :], y_half[h][:, planes, :], ALU.subtract)
-
-        def weigh(h):
+        def subtract_plane(r, chunks):
             nc.vector.tensor_tensor(
-                g_words[h][:].rearrange("p (c i) r -> p c r i", i=4),
-                diff[h][:].rearrange("p r (c i) -> p c r i", i=4),
-                weight[:, :, h * HALF : (h + 1) * HALF].rearrange("p r (c i) -> p c r i", i=4),
+                diff[0][:, chunks, r, :],
+                sig_first[r][:, 0, :].rearrange("p (c i) -> p c i", i=P)[:, chunks, :],
+                y_half[0][:, r, :].rearrange("p (c i) -> p c i", i=P)[:, chunks, :],
+                ALU.subtract,
+            )
+
+        def subtract_pair(b, chunks):
+            nc.vector.tensor_tensor(
+                diff[1][:, chunks, 2 * b : 2 * b + 2, :],
+                sig_second[b][:].rearrange("p r (c i) -> p c r i", i=P)[:, chunks, :, :],
+                y_half[1][:, 2 * b : 2 * b + 2, :].rearrange("p r (c i) -> p c r i", i=P)[:, chunks, :, :],
+                ALU.subtract,
+            )
+
+        def weigh(h, c):
+            first = HALF * h + P * c
+            nc.vector.tensor_tensor(
+                g_words[h][:, c, :].rearrange("p (k i r) -> p k r i", i=4, r=PACK),
+                diff[h][:, c, :, :].rearrange("p r (k i) -> p k r i", i=4),
+                weight[:, :, first : first + P].rearrange("p r (k i) -> p k r i", i=4),
                 ALU.mult,
             )
 
-        def quantize_g(h):
-            cols = slice((h + 1) * HALF, (h + 2) * HALF)
-            nc.vector.quantize_mx(
-                out=g_codes[:, cols].bitcast(E5M2X4), scales=g_scale[:, cols], in_=g_words[h][:].rearrange("p n r -> p (n r)")
-            )
+        def quantize_g(words, first, end):
+            cols = slice(HALF + first, HALF + end)
+            nc.vector.quantize_mx(out=g_codes[:, cols].bitcast(E5M2X4), scales=g_scale[:, cols], in_=words)
 
-        for r in range(PACK):
-            subtract(0, slice(r, r + 1))
-        subtract(1, slice(0, 2))
-        weigh(0)
-        subtract(1, slice(2, 4))
-        quantize_g(0)
+        for r in range(PACK - 1):
+            subtract_plane(r, slice(0, 2))
+        for c in range(2):
+            subtract_plane(PACK - 1, slice(c, c + 1))
+        for c in range(2):
+            weigh(0, c)
+        for c in range(2):
+            quantize_g(g_words[0][:, c, :], P * c, P * (c + 1))
         early = [back(j, 0, 6 + j) for j in range(EARLY_TILES)]
-        weigh(1)
-        quantize_g(1)
+        subtract_pair(0, slice(0, 2))
+        for c in range(2):
+            subtract_pair(1, slice(c, c + 1))
+        for c in range(2):
+            weigh(1, c)
         pieces = []
-        for j, spent in enumerate((sig[1], diff[1])):
-            nc.scalar.copy(out=spent[:, PACK - 1, :], in_=early[j][:, HALF:N])
-            pieces.append((j, spent[:, PACK - 1, :], half_list(0), False))
+        for j, dx in enumerate((sig_second[1][:, 0, :], diff[1][:, 1, 0:2, :].rearrange("p r i -> p (r i)"))):
+            nc.scalar.copy(out=dx, in_=early[j][:, HALF:N])
+            pieces.append((j, dx, half_list(0), False))
+        nc.vector.tensor_copy(out=window[0][:].indirect(pieces[0][2]), in_=pieces[0][1])
+        quantize_g(g_words[1][:].rearrange("p c n -> p (c n)"), HALF, N)
         for j in range(PACK):
             acc = back(j, HALF, j)
             if j < EARLY_TILES:
@@ -203,7 +229,7 @@ def tile_attend_gml_nce_kernel(tc, xT, wd_words, wd_scales, wv_words, wv_scales,
                 nc.scalar.copy(out=dx[:], in_=acc[:])
                 pieces.append((j, dx[:], offsets[:], True))
 
-        for j, dx, entries, last in pieces:
+        for j, dx, entries, last in pieces[1:]:
             nc.vector.tensor_copy(out=window[j][:].indirect(entries), in_=dx)
             if last:
                 nc.sync.dma_start(out=out[P * j : P * (j + 1), :], in_=window[j][:])

@@ -24,6 +24,7 @@ HALF = N // 2
 LIST_COLS = HALF // 16
 EARLY_TILES = 2
 OVERLAP = 32
+SLOT = (0, 2, 1, 3)
 
 
 def load_scale_rows(queue, tile, scales, q):
@@ -71,10 +72,10 @@ def tile_attend_gml_nce_kernel(tc, xT, wd_words, wd_scales, wv_words, wv_scales,
         nc.sync.dma_start(out=x_plane[2][:], in_=x_rows[:, 2, :])
         nc.sync.dma_start(out=x_plane[3][:], in_=x_rows[:, 3, :])
         nc.sync.dma_start(out=y_half[0][:], in_=y_rows[:, :, 0:HALF])
-        nc.sync.dma_start(out=y_half[1][:], in_=y_rows[:, :, HALF:N])
         nc.sync.dma_start(out=wv_codes[:].bitcast(I32), in_=wv_words[0].bitcast(I32))
         for q in range(4):
             load_scale_rows(nc.sync, wv_scale, wv_scales, q)
+        nc.sync.dma_start(out=y_half[1][:], in_=y_rows[:, :, HALF:N])
 
         window = [sb.tile([P, T], F32, name=f"window{j}") for j in range(PACK)]
         for j in range(PACK):
@@ -86,14 +87,29 @@ def tile_attend_gml_nce_kernel(tc, xT, wd_words, wd_scales, wv_words, wv_scales,
         rw_bank = ps.tile([P, PACK, P], F32, name="rw_bank", tag="bank7")
         for j in range(PACK):
             nc.tensor.transpose(rw_bank[:, j, :], rw4[:, j : j + 1].to_broadcast([P, P]), ident[:])
-        weight = sb.tile([P, PACK, N], F32, name="weight")
-        for r in range(PACK):
+        weight = [sb.tile([P, PACK, HALF], F32, name=f"weight{h}") for h in range(2)]
+        for h in (1, 0):
+            for r in range(PACK):
+                nc.scalar.activation(
+                    out=weight[h][:, r, :].rearrange("q (p j) -> q p j", j=PACK),
+                    in_=rw_bank[:, :, 64 * h : 64 * (h + 1)].rearrange("q j p -> q p j"),
+                    func=ACT.Copy,
+                    scale=cw4[:, r : r + 1],
+                )
+
+        turned_weight = []
+        for c in range(2):
+            bank = ps.tile([P, PACK, P], F32, name=f"weight_bank{c}", tag=f"bank{4 + c}")
+            for r in range(PACK):
+                nc.tensor.transpose(bank[:, SLOT[r], :], weight[1][:, r, P * c : P * (c + 1)], ident[:])
+            turned = sb.tile([P, V], F32, name=f"turned_weight{c}")
             nc.scalar.activation(
-                out=weight[:, r, :].rearrange("q (p j) -> q p j", j=PACK),
-                in_=rw_bank[:].rearrange("q j p -> q p j"),
+                out=turned[:].rearrange("q (k e) -> q k e", e=2),
+                in_=bank[:].rearrange("q (e u) p -> q (u p) e", e=2),
                 func=ACT.Copy,
-                scale=cw4[:, r : r + 1],
+                scale=-1.0,
             )
+            turned_weight.append(turned)
 
 
         x_words = sb.tile([P, N, PACK], BF16, name="x_words", align_bytes=64)
@@ -143,7 +159,7 @@ def tile_attend_gml_nce_kernel(tc, xT, wd_words, wd_scales, wv_words, wv_scales,
                     stop=True,
                 )
             sig = sb.tile([P, len(planes), HALF], F32, name=f"sig{bank}")
-            nc.scalar.activation(out=sig[:], in_=score[:], func=ACT.Sigmoid)
+            nc.scalar.activation(out=sig[:], in_=score[:], func=ACT.Sigmoid, scale=-1.0 if h else 1.0)
             return sig
 
         gather(PACK - 1, 0, HALF)
@@ -166,7 +182,7 @@ def tile_attend_gml_nce_kernel(tc, xT, wd_words, wd_scales, wv_words, wv_scales,
             )
             return acc
 
-        diff = [sb.tile([P, 2, PACK, P], F32, name=f"diff{h}") for h in range(2)]
+        diff = [sb.tile([P, 2, PACK, P], F32, name="diff0")]
         g_words = [sb.tile([P, 2, P * PACK], BF16, name=f"g_words{h}", align_bytes=64) for h in range(2)]
 
         def subtract_plane(r, chunks):
@@ -177,26 +193,37 @@ def tile_attend_gml_nce_kernel(tc, xT, wd_words, wd_scales, wv_words, wv_scales,
                 ALU.subtract,
             )
 
-        def subtract_pair(b, chunks):
-            nc.vector.tensor_tensor(
-                diff[1][:, chunks, 2 * b : 2 * b + 2, :],
-                sig_second[b][:].rearrange("p r (c i) -> p c r i", i=P)[:, chunks, :, :],
-                y_half[1][:, 2 * b : 2 * b + 2, :].rearrange("p r (c i) -> p c r i", i=P)[:, chunks, :, :],
-                ALU.subtract,
-            )
-
         def weigh(h, c):
             first = HALF * h + P * c
             nc.vector.tensor_tensor(
                 g_words[h][:, c, :].rearrange("p (k i r) -> p k r i", i=4, r=PACK),
                 diff[h][:, c, :, :].rearrange("p r (k i) -> p k r i", i=4),
-                weight[:, :, first : first + P].rearrange("p r (k i) -> p k r i", i=4),
+                weight[0][:, :, first : first + P].rearrange("p r (k i) -> p k r i", i=4),
                 ALU.mult,
             )
 
         def quantize_g(words, first, end):
             cols = slice(HALF + first, HALF + end)
             nc.vector.quantize_mx(out=g_codes[:, cols].bitcast(E5M2X4), scales=g_scale[:, cols], in_=words)
+
+        sums = [ps.tile([P, PACK, P], F32, name=f"sums{c}", tag=f"bank{c}") for c in range(2)]
+        for c in range(2):
+            for r in range(PACK):
+                nc.tensor.matmul(
+                    sums[c][:, SLOT[r], :], y_half[1][:, r, P * c : P * (c + 1)], ident[:], is_transpose=True, start=r == 0, stop=False
+                )
+        for b in range(2):
+            for c in range(2):
+                for u in range(2):
+                    r = 2 * b + u
+                    nc.tensor.matmul(
+                        sums[c][:, SLOT[r], :],
+                        sig_second[b][:, u, P * c : P * (c + 1)],
+                        ident[:],
+                        is_transpose=True,
+                        start=False,
+                        stop=r == PACK - 1,
+                    )
 
         for r in range(PACK - 1):
             subtract_plane(r, slice(0, 2))
@@ -207,19 +234,32 @@ def tile_attend_gml_nce_kernel(tc, xT, wd_words, wd_scales, wv_words, wv_scales,
         for c in range(2):
             quantize_g(g_words[0][:, c, :], P * c, P * (c + 1))
         early = [back(j, 0, 6 + j) for j in range(EARLY_TILES)]
-        subtract_pair(0, slice(0, 2))
+        g_turned = []
         for c in range(2):
-            subtract_pair(1, slice(c, c + 1))
-        for c in range(2):
-            weigh(1, c)
+            turned = g_words[0][:, 1 - c, :]
+            nc.vector.scalar_tensor_tensor(
+                turned.rearrange("q (k e) -> q k e", e=2),
+                sums[c][:].rearrange("q (e u) p -> q (u p) e", e=2),
+                -1.0,
+                turned_weight[c][:].rearrange("q (k e) -> q k e", e=2),
+                ALU.add,
+                ALU.mult,
+            )
+            g_turned.append(turned)
+            pairs = ps.tile([P, 2, P], F32, name=f"pairs{c}", tag=f"bank{2 + c}")
+            for u in range(2):
+                nc.tensor.transpose(pairs[:, u, :], turned.bitcast(F32)[:, P * u : P * (u + 1)], ident[:])
+            nc.scalar.copy(
+                out=g_words[1][:, c, :].bitcast(F32).rearrange("p (i u) -> p i u", u=2), in_=pairs[:].rearrange("p u i -> p i u")
+            )
         pieces = []
-        for j, dx in enumerate((sig_second[1][:, 0, :], diff[1][:, 1, 0:2, :].rearrange("p r i -> p (r i)"))):
+        for j, dx in enumerate((turned_weight[0][:, 0:HALF], g_turned[1].bitcast(F32))):
             nc.scalar.copy(out=dx, in_=early[j][:, HALF:N])
             pieces.append((j, dx, half_list(0), False))
         nc.vector.tensor_copy(out=window[0][:].indirect(pieces[0][2]), in_=pieces[0][1])
         quantize_g(g_words[1][:].rearrange("p c n -> p (c n)"), HALF, N)
         for j in range(PACK):
-            acc = back(j, HALF, j)
+            acc = back(j, HALF, (4 + j) % 6)
             if j < EARLY_TILES:
                 dx = sb.tile([P, HALF], F32, name=f"dx_late{j}")
                 nc.scalar.copy(out=dx[:], in_=acc[:, HALF:N])

@@ -46,73 +46,89 @@ def tile_attend_gml_nce_kernel(tc, xT, wd_words, wd_scales, wv_words, wv_scales,
         y_half = [sb.tile([P, PACK, HALF], F32, name=f"y_half{h}") for h in range(2)]
         offsets = sb.tile([P, N // 16], U16, name="offsets")
         cw4 = sb.tile([P, PACK], F32, name="cw4")
-        rw4 = sb.tile([P, PACK], F32, name="rw4")
-        wd_raw = sb.tile([P, 2 * V], U8, name="wd_raw", align_bytes=64)
-        wd_scale_raw = sb.tile([P, V], U8, name="wd_scale_raw", align_bytes=64)
+        rw_rows = sb.tile([P, P], F32, name="rw_rows", tag="late")
+        wd_in = sb.tile([P, 3 * V], U8, name="wd_in", tag="words", align_bytes=64)
+        wd_raw = wd_in[:, 0 : 2 * V]
+        wd_scale_raw = wd_in[:, 2 * V : 3 * V]
         wv_codes = sb.tile([P, 2 * D], U8, name="wv_codes", align_bytes=64)
         wv_scale = sb.tile([P, D], U8, name="wv_scale", align_bytes=64)
         g_codes = sb.tile([P, HALF + N], U32, name="g_codes", align_bytes=64)
         g_scale = sb.tile([P, HALF + N], U8, name="g_scale", align_bytes=64)
         ident = sb.tile([P, P], F32, name="ident")
 
-        nc.gpsimd.memset(wd_scale_raw[:].bitcast(I32), 0)
+        nc.vector.memset(wd_scale_raw.bitcast(I32), 0)
+        nc.gpsimd.memset(rw_rows[:], 0.0)
+        make_identity(nc, ident[:])
         nc.gpsimd.memset(wv_scale[:].bitcast(I32), 0)
         nc.gpsimd.memset(g_codes[:, 0:HALF], 0)
         nc.gpsimd.memset(g_scale[:, 0:HALF].bitcast(I32), 0)
-        make_identity(nc, ident[:])
 
         nc.sync.dma_start(out=x_plane[0][:], in_=x_rows[:, 0, :])
-        nc.scalar.dma_start(out=wd_raw[:].bitcast(I32), in_=wd_words[0].bitcast(I32))
+        nc.scalar.dma_start(out=wd_raw.bitcast(I32), in_=wd_words[0].bitcast(I32))
         for q in range(4):
-            load_scale_rows(nc.scalar, wd_scale_raw, wd_scales, q)
+            load_scale_rows(nc.sync, wd_scale_raw, wd_scales, q)
         nc.sync.dma_start(offsets[:], offs)
         nc.sync.dma_start(out=x_plane[1][:], in_=x_rows[:, 1, :])
-        nc.sync.dma_start(out=rw4[:], in_=rw[0].rearrange("(p j) -> p j", j=PACK))
+        nc.sync.dma_start(out=rw_rows[0:PACK, :], in_=rw[0].rearrange("(c q) -> c q", c=PACK))
         nc.sync.dma_start(out=cw4[:], in_=cw.rearrange("(p r) o -> p (r o)", r=PACK))
         nc.sync.dma_start(out=x_plane[2][:], in_=x_rows[:, 2, :])
         nc.sync.dma_start(out=x_plane[3][:], in_=x_rows[:, 3, :])
         nc.sync.dma_start(out=y_half[0][:], in_=y_rows[:, :, 0:HALF])
+        nc.sync.dma_start(out=y_half[1][:], in_=y_rows[:, :, HALF:N])
         nc.sync.dma_start(out=wv_codes[:].bitcast(I32), in_=wv_words[0].bitcast(I32))
         for q in range(4):
             load_scale_rows(nc.sync, wv_scale, wv_scales, q)
-        nc.sync.dma_start(out=y_half[1][:], in_=y_rows[:, :, HALF:N])
 
-        window = [sb.tile([P, T], F32, name=f"window{j}") for j in range(PACK)]
-        for j in range(PACK):
-            (nc.vector if j < 2 else nc.gpsimd).memset(window[j][:].bitcast(I32), 0)
+        window = [sb.tile([P, T], F32, name=f"window{j}") for j in range(2)]
+        for j in range(2):
+            nc.vector.memset(window[j][:].bitcast(I32), 0)
 
-        warm = sb.tile([P, 1], F32, name="warm")
-        nc.scalar.activation(out=warm[:], in_=ident[:, 0:1], func=ACT.Sigmoid)
 
-        rw_bank = ps.tile([P, PACK, P], F32, name="rw_bank", tag="bank7")
-        for j in range(PACK):
-            nc.tensor.transpose(rw_bank[:, j, :], rw4[:, j : j + 1].to_broadcast([P, P]), ident[:])
-        weight = [sb.tile([P, PACK, HALF], F32, name=f"weight{h}") for h in range(2)]
-        for h in (1, 0):
-            for r in range(PACK):
-                nc.scalar.activation(
-                    out=weight[h][:, r, :].rearrange("q (p j) -> q p j", j=PACK),
-                    in_=rw_bank[:, :, 64 * h : 64 * (h + 1)].rearrange("q j p -> q p j"),
-                    func=ACT.Copy,
-                    scale=cw4[:, r : r + 1],
-                )
-
+        rw_turned = ps.tile([P, P], F32, name="rw_turned", tag="bank5")
+        nc.tensor.transpose(rw_turned[:], rw_rows[:], ident[:])
+        minus_rw = sb.tile([P, PACK], F32, name="minus_rw")
+        nc.scalar.activation(out=minus_rw[:], in_=rw_turned[:, 0:PACK], func=ACT.Copy, scale=-1.0)
+        rw_bank = ps.tile([P, 2, P], F32, name="rw_bank", tag="bank7")
+        for c in range(2):
+            nc.tensor.transpose(rw_bank[:, c, :], minus_rw[:, c : c + 1].to_broadcast([P, P]), ident[:])
+        cw_bank = ps.tile([P, PACK, P], F32, name="cw_bank", tag="bank6")
+        for r in range(PACK):
+            nc.tensor.transpose(cw_bank[:, SLOT[r], :], cw4[:, r : r + 1].to_broadcast([P, P]), ident[:])
+        window.append(sb.tile([P, T], F32, name="window2", tag="late"))
+        nc.gpsimd.memset(window[2][:].bitcast(I32), 0)
+        window.append(window[0])
+        weight = sb.tile([P, PACK, HALF], F32, name="weight")
+        for r in range(PACK):
+            nc.scalar.activation(
+                out=weight[:, r, :],
+                in_=rw_bank[:].rearrange("q c i -> q (c i)"),
+                func=ACT.Copy,
+                scale=cw4[:, r : r + 1],
+            )
         turned_weight = []
         for c in range(2):
-            bank = ps.tile([P, PACK, P], F32, name=f"weight_bank{c}", tag=f"bank{4 + c}")
-            for r in range(PACK):
-                nc.tensor.transpose(bank[:, SLOT[r], :], weight[1][:, r, P * c : P * (c + 1)], ident[:])
             turned = sb.tile([P, V], F32, name=f"turned_weight{c}")
             nc.scalar.activation(
                 out=turned[:].rearrange("q (k e) -> q k e", e=2),
-                in_=bank[:].rearrange("q (e u) p -> q (u p) e", e=2),
+                in_=cw_bank[:].rearrange("q (e u) p -> q (u p) e", e=2),
                 func=ACT.Copy,
-                scale=-1.0,
+                scale=minus_rw[:, 2 + c : 3 + c],
             )
             turned_weight.append(turned)
 
+        wd_dealt = sb.tile([P, 3 * V], U8, name="wd_dealt", align_bytes=64)
+        wd_codes = wd_dealt[:, 0 : 2 * V]
+        wd_scale = wd_dealt[:, 2 * V : 3 * V]
+        nc.vector.tensor_copy(
+            out=wd_codes.bitcast(U16).rearrange("p (r s) -> p s r", r=PACK),
+            in_=wd_raw.bitcast(U16).rearrange("p (s r) -> p s r", r=PACK),
+        )
+        nc.vector.tensor_copy(
+            out=wd_scale.rearrange("p (r s) -> p s r", r=PACK),
+            in_=wd_scale_raw.rearrange("p (s r) -> p s r", r=PACK),
+        )
 
-        x_words = sb.tile([P, N, PACK], BF16, name="x_words", align_bytes=64)
+        x_words = sb.tile([P, N, PACK], BF16, name="x_words", tag="words", align_bytes=64)
         x_codes = [sb.tile([P, HALF], U32, name=f"x_codes{h}", align_bytes=64) for h in range(2)]
         x_scale = [sb.tile([P, HALF], U8, name=f"x_scale{h}", align_bytes=64) for h in range(2)]
 
@@ -126,18 +142,6 @@ def tile_attend_gml_nce_kernel(tc, xT, wd_words, wd_scales, wv_words, wv_scales,
 
         for t in range(PACK - 1):
             gather(t, 0, N)
-            if t == 1:
-                wd_dealt = sb.tile([P, 3 * V], U8, name="wd_dealt", tag="wide1", align_bytes=64)
-                wd_codes = wd_dealt[:, 0 : 2 * V]
-                wd_scale = wd_dealt[:, 2 * V : 3 * V]
-                nc.vector.tensor_copy(
-                    out=wd_codes.bitcast(U16).rearrange("p (r s) -> p s r", r=PACK),
-                    in_=wd_raw[:].bitcast(U16).rearrange("p (s r) -> p s r", r=PACK),
-                )
-                nc.vector.tensor_copy(
-                    out=wd_scale.rearrange("p (r s) -> p s r", r=PACK),
-                    in_=wd_scale_raw[:].rearrange("p (s r) -> p s r", r=PACK),
-                )
 
         def quantize_x(h):
             nc.vector.quantize_mx(
@@ -188,8 +192,8 @@ def tile_attend_gml_nce_kernel(tc, xT, wd_words, wd_scales, wv_words, wv_scales,
         def subtract_plane(r, chunks):
             nc.vector.tensor_tensor(
                 diff[0][:, chunks, r, :],
-                sig_first[r][:, 0, :].rearrange("p (c i) -> p c i", i=P)[:, chunks, :],
                 y_half[0][:, r, :].rearrange("p (c i) -> p c i", i=P)[:, chunks, :],
+                sig_first[r][:, 0, :].rearrange("p (c i) -> p c i", i=P)[:, chunks, :],
                 ALU.subtract,
             )
 
@@ -198,7 +202,7 @@ def tile_attend_gml_nce_kernel(tc, xT, wd_words, wd_scales, wv_words, wv_scales,
             nc.vector.tensor_tensor(
                 g_words[h][:, c, :].rearrange("p (k i r) -> p k r i", i=4, r=PACK),
                 diff[h][:, c, :, :].rearrange("p r (k i) -> p k r i", i=4),
-                weight[0][:, :, first : first + P].rearrange("p r (k i) -> p k r i", i=4),
+                weight[:, :, first : first + P].rearrange("p r (k i) -> p k r i", i=4),
                 ALU.mult,
             )
 
@@ -246,16 +250,17 @@ def tile_attend_gml_nce_kernel(tc, xT, wd_words, wd_scales, wv_words, wv_scales,
                 ALU.mult,
             )
             g_turned.append(turned)
-            pairs = ps.tile([P, 2, P], F32, name=f"pairs{c}", tag=f"bank{2 + c}")
+        dx_early = [turned_weight[0][:, 0:HALF], g_turned[1].bitcast(F32)]
+        nc.scalar.copy(out=dx_early[0], in_=early[0][:, HALF:N])
+        pairs = ps.tile([P, 2, 2, P], F32, name="pairs", tag="bank6")
+        for c in range(2):
             for u in range(2):
-                nc.tensor.transpose(pairs[:, u, :], turned.bitcast(F32)[:, P * u : P * (u + 1)], ident[:])
-            nc.scalar.copy(
-                out=g_words[1][:, c, :].bitcast(F32).rearrange("p (i u) -> p i u", u=2), in_=pairs[:].rearrange("p u i -> p i u")
-            )
-        pieces = []
-        for j, dx in enumerate((turned_weight[0][:, 0:HALF], g_turned[1].bitcast(F32))):
-            nc.scalar.copy(out=dx, in_=early[j][:, HALF:N])
-            pieces.append((j, dx, half_list(0), False))
+                nc.tensor.transpose(pairs[:, c, u, :], g_turned[c].bitcast(F32)[:, P * u : P * (u + 1)], ident[:])
+        nc.scalar.copy(
+            out=g_words[1][:].bitcast(F32).rearrange("p c (i u) -> p c i u", u=2), in_=pairs[:].rearrange("p c u i -> p c i u")
+        )
+        nc.scalar.copy(out=dx_early[1], in_=early[1][:, HALF:N])
+        pieces = [(j, dx_early[j], half_list(0), False) for j in range(EARLY_TILES)]
         nc.vector.tensor_copy(out=window[0][:].indirect(pieces[0][2]), in_=pieces[0][1])
         quantize_g(g_words[1][:].rearrange("p c n -> p (c n)"), HALF, N)
         for j in range(PACK):

@@ -21,17 +21,21 @@ ALU = mybir.AluOpType
 P = 128
 PACK = 4
 HALF = N // 2
-LIST_COLS = HALF // 16
+ENTRIES = 16
 EARLY_TILES = 2
 OVERLAP = 32
-SLOT = (0, 2, 1, 3)
+RUN = 4
+PLACE = (0, 2, 1, 3)
+CHUNK = (slice(0, P), slice(P, HALF))
+BOTH = slice(0, HALF)
 
 
-def load_scale_rows(queue, tile, scales, q):
-    queue.dma_start(
-        out=tile[32 * q : 32 * q + 4, :].bitcast(I32),
-        in_=scales[0, 4 * q : 4 * q + 4, :].bitcast(I32),
-    )
+def load_scale_rows(nc, tile, scales):
+    for q in range(4):
+        nc.sync.dma_start(
+            out=tile[32 * q : 32 * q + 4, :].bitcast(I32),
+            in_=scales[0, 4 * q : 4 * q + 4, :].bitcast(I32),
+        )
 
 
 def tile_attend_gml_nce_kernel(tc, xT, wd_words, wd_scales, wv_words, wv_scales, y, cw, rw, offs, out):
@@ -40,23 +44,26 @@ def tile_attend_gml_nce_kernel(tc, xT, wd_words, wd_scales, wv_words, wv_scales,
         sb = ctx.enter_context(tc.tile_pool(name="sb", bufs=1))
         ps = ctx.enter_context(tc.psum_pool(name="ps", bufs=1))
 
+        def bank(number, shape, name):
+            return ps.tile(shape, F32, name=name, tag=f"bank{number}")
+
         x_rows = xT.rearrange("(p t) n -> p t n", t=PACK)
         y_rows = y.rearrange("(p r) n -> p r n", r=PACK)
-        x_plane = [sb.tile([P, T], F32, name=f"x_plane{t}", tag=f"wide{t}", align_bytes=64) for t in range(PACK)]
+        x_plane = [sb.tile([P, T], F32, name=f"x_plane{t}", align_bytes=64) for t in range(PACK)]
         y_half = [sb.tile([P, PACK, HALF], F32, name=f"y_half{h}") for h in range(2)]
-        offsets = sb.tile([P, N // 16], U16, name="offsets")
+        offsets = sb.tile([P, N // ENTRIES], U16, name="offsets")
         cw4 = sb.tile([P, PACK], F32, name="cw4")
-        rw_rows = sb.tile([P, P], F32, name="rw_rows", tag="late")
-        wd_in = sb.tile([P, 3 * V], U8, name="wd_in", tag="words", align_bytes=64)
-        wd_raw = wd_in[:, 0 : 2 * V]
-        wd_scale_raw = wd_in[:, 2 * V : 3 * V]
+        rw_rows = sb.tile([P, P], F32, name="rw_rows", tag="rw_then_window")
+        wd_in = sb.tile([P, 3 * V], U8, name="wd_in", tag="wd_then_x", align_bytes=64)
+        wd_in_words = wd_in[:, 0 : 2 * V]
+        wd_in_scale = wd_in[:, 2 * V : 3 * V]
         wv_codes = sb.tile([P, 2 * D], U8, name="wv_codes", align_bytes=64)
         wv_scale = sb.tile([P, D], U8, name="wv_scale", align_bytes=64)
         g_codes = sb.tile([P, HALF + N], U32, name="g_codes", align_bytes=64)
         g_scale = sb.tile([P, HALF + N], U8, name="g_scale", align_bytes=64)
         ident = sb.tile([P, P], F32, name="ident")
 
-        nc.vector.memset(wd_scale_raw.bitcast(I32), 0)
+        nc.vector.memset(wd_in_scale.bitcast(I32), 0)
         nc.gpsimd.memset(rw_rows[:], 0.0)
         make_identity(nc, ident[:])
         nc.gpsimd.memset(wv_scale[:].bitcast(I32), 0)
@@ -64,117 +71,165 @@ def tile_attend_gml_nce_kernel(tc, xT, wd_words, wd_scales, wv_words, wv_scales,
         nc.gpsimd.memset(g_scale[:, 0:HALF].bitcast(I32), 0)
 
         nc.sync.dma_start(out=x_plane[0][:], in_=x_rows[:, 0, :])
-        nc.scalar.dma_start(out=wd_raw.bitcast(I32), in_=wd_words[0].bitcast(I32))
-        for q in range(4):
-            load_scale_rows(nc.sync, wd_scale_raw, wd_scales, q)
+        nc.scalar.dma_start(out=wd_in_words.bitcast(I32), in_=wd_words[0].bitcast(I32))
+        load_scale_rows(nc, wd_in_scale, wd_scales)
         nc.sync.dma_start(offsets[:], offs)
         nc.sync.dma_start(out=x_plane[1][:], in_=x_rows[:, 1, :])
-        nc.sync.dma_start(out=rw_rows[0:PACK, :], in_=rw[0].rearrange("(c q) -> c q", c=PACK))
+        nc.sync.dma_start(out=rw_rows[0 : N // P, :], in_=rw[0].rearrange("(c q) -> c q", q=P))
         nc.sync.dma_start(out=cw4[:], in_=cw.rearrange("(p r) o -> p (r o)", r=PACK))
         nc.sync.dma_start(out=x_plane[2][:], in_=x_rows[:, 2, :])
         nc.sync.dma_start(out=x_plane[3][:], in_=x_rows[:, 3, :])
         nc.sync.dma_start(out=y_half[0][:], in_=y_rows[:, :, 0:HALF])
         nc.sync.dma_start(out=y_half[1][:], in_=y_rows[:, :, HALF:N])
         nc.sync.dma_start(out=wv_codes[:].bitcast(I32), in_=wv_words[0].bitcast(I32))
-        for q in range(4):
-            load_scale_rows(nc.sync, wv_scale, wv_scales, q)
+        load_scale_rows(nc, wv_scale, wv_scales)
 
         window = [sb.tile([P, T], F32, name=f"window{j}") for j in range(2)]
         for j in range(2):
             nc.vector.memset(window[j][:].bitcast(I32), 0)
 
-
-        rw_turned = ps.tile([P, P], F32, name="rw_turned", tag="bank5")
+        rw_turned = bank(5, [P, P], "rw_turned")
         nc.tensor.transpose(rw_turned[:], rw_rows[:], ident[:])
-        minus_rw = sb.tile([P, PACK], F32, name="minus_rw")
-        nc.scalar.activation(out=minus_rw[:], in_=rw_turned[:, 0:PACK], func=ACT.Copy, scale=-1.0)
-        rw_bank = ps.tile([P, 2, P], F32, name="rw_bank", tag="bank7")
+        minus_rw = sb.tile([P, N // P], F32, name="minus_rw")
+        nc.scalar.activation(out=minus_rw[:], in_=rw_turned[:, 0 : N // P], func=ACT.Copy, scale=-1.0)
+        rw_spread = bank(7, [P, 2, P], "rw_spread")
         for c in range(2):
-            nc.tensor.transpose(rw_bank[:, c, :], minus_rw[:, c : c + 1].to_broadcast([P, P]), ident[:])
-        cw_bank = ps.tile([P, PACK, P], F32, name="cw_bank", tag="bank6")
+            nc.tensor.transpose(rw_spread[:, c, :], minus_rw[:, c : c + 1].to_broadcast([P, P]), ident[:])
+        cw_spread = bank(6, [P, PACK, P], "cw_spread")
         for r in range(PACK):
-            nc.tensor.transpose(cw_bank[:, SLOT[r], :], cw4[:, r : r + 1].to_broadcast([P, P]), ident[:])
-        window.append(sb.tile([P, T], F32, name="window2", tag="late"))
+            nc.tensor.transpose(cw_spread[:, PLACE[r], :], cw4[:, r : r + 1].to_broadcast([P, P]), ident[:])
+        window.append(sb.tile([P, T], F32, name="window2", tag="rw_then_window"))
         nc.gpsimd.memset(window[2][:].bitcast(I32), 0)
         window.append(window[0])
         weight = sb.tile([P, PACK, HALF], F32, name="weight")
         for r in range(PACK):
             nc.scalar.activation(
                 out=weight[:, r, :],
-                in_=rw_bank[:].rearrange("q c i -> q (c i)"),
+                in_=rw_spread[:].rearrange("q c i -> q (c i)"),
                 func=ACT.Copy,
                 scale=cw4[:, r : r + 1],
             )
         turned_weight = []
         for c in range(2):
-            turned = sb.tile([P, V], F32, name=f"turned_weight{c}")
+            turned_weight.append(sb.tile([P, V], F32, name=f"turned_weight{c}"))
             nc.scalar.activation(
-                out=turned[:].rearrange("q (k e) -> q k e", e=2),
-                in_=cw_bank[:].rearrange("q (e u) p -> q (u p) e", e=2),
+                out=turned_weight[c][:].rearrange("q (k e) -> q k e", e=2),
+                in_=cw_spread[:].rearrange("q (e u) p -> q (u p) e", e=2),
                 func=ACT.Copy,
                 scale=minus_rw[:, 2 + c : 3 + c],
             )
-            turned_weight.append(turned)
 
         wd_dealt = sb.tile([P, 3 * V], U8, name="wd_dealt", align_bytes=64)
         wd_codes = wd_dealt[:, 0 : 2 * V]
         wd_scale = wd_dealt[:, 2 * V : 3 * V]
         nc.vector.tensor_copy(
             out=wd_codes.bitcast(U16).rearrange("p (r s) -> p s r", r=PACK),
-            in_=wd_raw.bitcast(U16).rearrange("p (s r) -> p s r", r=PACK),
+            in_=wd_in_words.bitcast(U16).rearrange("p (s r) -> p s r", r=PACK),
         )
         nc.vector.tensor_copy(
             out=wd_scale.rearrange("p (r s) -> p s r", r=PACK),
-            in_=wd_scale_raw.rearrange("p (s r) -> p s r", r=PACK),
+            in_=wd_in_scale.rearrange("p (s r) -> p s r", r=PACK),
         )
 
-        x_words = sb.tile([P, N, PACK], BF16, name="x_words", tag="words", align_bytes=64)
+        x_words = sb.tile([P, N, PACK], BF16, name="x_words", tag="wd_then_x", align_bytes=64)
         x_codes = [sb.tile([P, HALF], U32, name=f"x_codes{h}", align_bytes=64) for h in range(2)]
         x_scale = [sb.tile([P, HALF], U8, name=f"x_scale{h}", align_bytes=64) for h in range(2)]
 
-        def half_list(h):
-            return offsets[:, h * LIST_COLS : (h + 1) * LIST_COLS]
+        def entries(first, end):
+            return offsets[:, first // ENTRIES : end // ENTRIES]
 
         def gather(t, first, end):
-            nc.vector.tensor_copy(
-                out=x_words[:, first:end, t], in_=x_plane[t][:].indirect(offsets[:, first // 16 : end // 16])
-            )
+            nc.vector.tensor_copy(out=x_words[:, first:end, t], in_=x_plane[t][:].indirect(entries(first, end)))
 
-        for t in range(PACK - 1):
-            gather(t, 0, N)
-
-        def quantize_x(h):
+        def quantize_x(h, cols):
             nc.vector.quantize_mx(
-                out=x_codes[h][:].bitcast(E4M3X4),
-                scales=x_scale[h][:],
-                in_=x_words[:, HALF * h : HALF * (h + 1), :].rearrange("p n t -> p (n t)"),
+                out=x_codes[h][:, cols].bitcast(E4M3X4),
+                scales=x_scale[h][:, cols],
+                in_=x_words[:, HALF * h : HALF * (h + 1), :][:, cols, :].rearrange("p n t -> p (n t)"),
             )
 
-        def scores(h, planes, bank):
-            score = ps.tile([P, len(planes), HALF], F32, name=f"score{bank}", tag=f"bank{bank}")
+        def sigmoid_of_scores(h, planes, cols, number, sign):
+            shape = [P, len(planes), cols.stop - cols.start]
+            score = bank(number, shape, f"score{number}")
             for u, r in enumerate(planes):
                 nc.tensor.matmul_mx(
                     out=score[:, u, :],
                     lhsT=wd_codes[:, 2 * P * r : 2 * P * (r + 1)].bitcast(E2M1X4),
                     lhsT_scale=wd_scale[:, P * r : P * (r + 1)],
-                    rhs=x_codes[h][:].bitcast(E4M3X4),
-                    rhs_scale=x_scale[h][:],
+                    rhs=x_codes[h][:, cols].bitcast(E4M3X4),
+                    rhs_scale=x_scale[h][:, cols],
                     start=True,
                     stop=True,
                 )
-            sig = sb.tile([P, len(planes), HALF], F32, name=f"sig{bank}")
-            nc.scalar.activation(out=sig[:], in_=score[:], func=ACT.Sigmoid, scale=-1.0 if h else 1.0)
+            sig = sb.tile(shape, F32, name=f"sig{number}")
+            nc.scalar.activation(out=sig[:], in_=score[:], func=ACT.Sigmoid, scale=sign)
             return sig
 
-        gather(PACK - 1, 0, HALF)
-        quantize_x(0)
-        sig_first = [scores(0, [r], r) for r in range(PACK)]
-        gather(PACK - 1, HALF - OVERLAP, N)
-        quantize_x(1)
-        sig_second = [scores(1, [2 * b, 2 * b + 1], 4 + b) for b in range(2)]
+        for t in range(PACK - 1):
+            gather(t, 0, N)
 
-        def back(j, first, bank):
-            acc = ps.tile([P, N], F32, name=f"acc{j}_{first}", tag=f"bank{bank}")
+        gather(PACK - 1, 0, HALF)
+        quantize_x(0, CHUNK[1])
+        sig_plane0 = {1: sigmoid_of_scores(0, [0], CHUNK[1], 7, 1.0)}
+        quantize_x(0, CHUNK[0])
+        sig_plane0[0] = sigmoid_of_scores(0, [0], CHUNK[0], 0, 1.0)
+        sig_first = {r: sigmoid_of_scores(0, [r], BOTH, r, 1.0) for r in range(1, PACK)}
+        gather(PACK - 1, HALF - OVERLAP, N)
+        quantize_x(1, BOTH)
+        sig_second = [sigmoid_of_scores(1, [2 * b, 2 * b + 1], BOTH, 4 + b, -1.0) for b in range(2)]
+
+        diff = sb.tile([P, 2, PACK, P], F32, name="diff")
+        g_words = [sb.tile([P, 2, P * PACK], BF16, name=f"g_words{h}", align_bytes=64) for h in range(2)]
+
+        sums = [bank(c, [P, PACK, P], f"sums{c}") for c in range(2)]
+        for c in range(2):
+            for r in range(PACK):
+                nc.tensor.matmul(
+                    sums[c][:, PLACE[r], :], y_half[1][:, r, CHUNK[c]], ident[:], is_transpose=True, start=r == 0, stop=False
+                )
+        for b in range(2):
+            for c in range(2):
+                for u in range(2):
+                    r = 2 * b + u
+                    nc.tensor.matmul(
+                        sums[c][:, PLACE[r], :],
+                        sig_second[b][:, u, CHUNK[c]],
+                        ident[:],
+                        is_transpose=True,
+                        start=False,
+                        stop=r == PACK - 1,
+                    )
+
+        def subtract_plane(r, chunks):
+            nc.vector.tensor_tensor(
+                diff[:, chunks, r, :],
+                y_half[0][:, r, :].rearrange("p (c i) -> p c i", i=P)[:, chunks, :],
+                sig_first[r][:, 0, :].rearrange("p (c i) -> p c i", i=P)[:, chunks, :],
+                ALU.subtract,
+            )
+
+        def quantize_g(words, first, end):
+            cols = slice(HALF + first, HALF + end)
+            nc.vector.quantize_mx(out=g_codes[:, cols].bitcast(E5M2X4), scales=g_scale[:, cols], in_=words)
+
+        for c in (1, 0):
+            nc.vector.tensor_tensor(diff[:, c, 0, :], y_half[0][:, 0, CHUNK[c]], sig_plane0[c][:, 0, :], ALU.subtract)
+        for r in range(1, PACK - 1):
+            subtract_plane(r, slice(0, 2))
+        for c in range(2):
+            subtract_plane(PACK - 1, slice(c, c + 1))
+        for c in range(2):
+            nc.vector.tensor_tensor(
+                g_words[0][:, c, :].rearrange("p (k i r) -> p k r i", i=RUN, r=PACK),
+                diff[:, c, :, :].rearrange("p r (k i) -> p k r i", i=RUN),
+                weight[:, :, CHUNK[c]].rearrange("p r (k i) -> p k r i", i=RUN),
+                ALU.mult,
+            )
+        for c in range(2):
+            quantize_g(g_words[0][:, c, :], P * c, P * (c + 1))
+
+        def back(j, first, number):
+            acc = bank(number, [P, N], f"acc{j}_{first}")
             nc.tensor.matmul_mx(
                 out=acc[:],
                 lhsT=wv_codes[:, 2 * P * j : 2 * P * (j + 1)].bitcast(E2M1X4),
@@ -186,95 +241,45 @@ def tile_attend_gml_nce_kernel(tc, xT, wd_words, wd_scales, wv_words, wv_scales,
             )
             return acc
 
-        diff = [sb.tile([P, 2, PACK, P], F32, name="diff0")]
-        g_words = [sb.tile([P, 2, P * PACK], BF16, name=f"g_words{h}", align_bytes=64) for h in range(2)]
-
-        def subtract_plane(r, chunks):
-            nc.vector.tensor_tensor(
-                diff[0][:, chunks, r, :],
-                y_half[0][:, r, :].rearrange("p (c i) -> p c i", i=P)[:, chunks, :],
-                sig_first[r][:, 0, :].rearrange("p (c i) -> p c i", i=P)[:, chunks, :],
-                ALU.subtract,
-            )
-
-        def weigh(h, c):
-            first = HALF * h + P * c
-            nc.vector.tensor_tensor(
-                g_words[h][:, c, :].rearrange("p (k i r) -> p k r i", i=4, r=PACK),
-                diff[h][:, c, :, :].rearrange("p r (k i) -> p k r i", i=4),
-                weight[:, :, first : first + P].rearrange("p r (k i) -> p k r i", i=4),
-                ALU.mult,
-            )
-
-        def quantize_g(words, first, end):
-            cols = slice(HALF + first, HALF + end)
-            nc.vector.quantize_mx(out=g_codes[:, cols].bitcast(E5M2X4), scales=g_scale[:, cols], in_=words)
-
-        sums = [ps.tile([P, PACK, P], F32, name=f"sums{c}", tag=f"bank{c}") for c in range(2)]
-        for c in range(2):
-            for r in range(PACK):
-                nc.tensor.matmul(
-                    sums[c][:, SLOT[r], :], y_half[1][:, r, P * c : P * (c + 1)], ident[:], is_transpose=True, start=r == 0, stop=False
-                )
-        for b in range(2):
-            for c in range(2):
-                for u in range(2):
-                    r = 2 * b + u
-                    nc.tensor.matmul(
-                        sums[c][:, SLOT[r], :],
-                        sig_second[b][:, u, P * c : P * (c + 1)],
-                        ident[:],
-                        is_transpose=True,
-                        start=False,
-                        stop=r == PACK - 1,
-                    )
-
-        for r in range(PACK - 1):
-            subtract_plane(r, slice(0, 2))
-        for c in range(2):
-            subtract_plane(PACK - 1, slice(c, c + 1))
-        for c in range(2):
-            weigh(0, c)
-        for c in range(2):
-            quantize_g(g_words[0][:, c, :], P * c, P * (c + 1))
         early = [back(j, 0, 6 + j) for j in range(EARLY_TILES)]
-        g_turned = []
+
+        g_turned = [g_words[0][:, c, :] for c in range(2)]
         for c in range(2):
-            turned = g_words[0][:, 1 - c, :]
             nc.vector.scalar_tensor_tensor(
-                turned.rearrange("q (k e) -> q k e", e=2),
+                g_turned[c].rearrange("q (k e) -> q k e", e=2),
                 sums[c][:].rearrange("q (e u) p -> q (u p) e", e=2),
                 -1.0,
                 turned_weight[c][:].rearrange("q (k e) -> q k e", e=2),
                 ALU.add,
                 ALU.mult,
             )
-            g_turned.append(turned)
+
         dx_early = [turned_weight[0][:, 0:HALF], g_turned[1].bitcast(F32)]
         nc.scalar.copy(out=dx_early[0], in_=early[0][:, HALF:N])
-        pairs = ps.tile([P, 2, 2, P], F32, name="pairs", tag="bank6")
+        pairs = bank(6, [P, 2, 2, P], "pairs")
         for c in range(2):
             for u in range(2):
                 nc.tensor.transpose(pairs[:, c, u, :], g_turned[c].bitcast(F32)[:, P * u : P * (u + 1)], ident[:])
         nc.scalar.copy(
-            out=g_words[1][:].bitcast(F32).rearrange("p c (i u) -> p c i u", u=2), in_=pairs[:].rearrange("p c u i -> p c i u")
+            out=g_words[1][:].bitcast(F32).rearrange("p c (q u) -> p c q u", u=2), in_=pairs[:].rearrange("p c u q -> p c q u")
         )
         nc.scalar.copy(out=dx_early[1], in_=early[1][:, HALF:N])
-        pieces = [(j, dx_early[j], half_list(0), False) for j in range(EARLY_TILES)]
-        nc.vector.tensor_copy(out=window[0][:].indirect(pieces[0][2]), in_=pieces[0][1])
-        quantize_g(g_words[1][:].rearrange("p c n -> p (c n)"), HALF, N)
-        for j in range(PACK):
-            acc = back(j, HALF, (4 + j) % 6)
-            if j < EARLY_TILES:
-                dx = sb.tile([P, HALF], F32, name=f"dx_late{j}")
-                nc.scalar.copy(out=dx[:], in_=acc[:, HALF:N])
-                pieces.append((j, dx[:], half_list(1), True))
-            else:
-                dx = sb.tile([P, N], F32, name=f"dx_whole{j}")
-                nc.scalar.copy(out=dx[:], in_=acc[:])
-                pieces.append((j, dx[:], offsets[:], True))
 
-        for j, dx, entries, last in pieces[1:]:
-            nc.vector.tensor_copy(out=window[j][:].indirect(entries), in_=dx)
-            if last:
-                nc.sync.dma_start(out=out[P * j : P * (j + 1), :], in_=window[j][:])
+        def scatter(j, dx, first, end):
+            nc.vector.tensor_copy(out=window[j][:].indirect(entries(first, end)), in_=dx)
+
+        scatter(0, dx_early[0], 0, HALF)
+        quantize_g(g_words[1][:].rearrange("p c n -> p (c n)"), HALF, N)
+
+        dx_late = []
+        for j, number in enumerate((4, 5, 0, 1)):
+            acc = back(j, HALF, number)
+            first = HALF if j < EARLY_TILES else 0
+            dx = sb.tile([P, N - first], F32, name=f"dx_late{j}")
+            nc.scalar.copy(out=dx[:], in_=acc[:, first:N])
+            dx_late.append((dx, first))
+
+        scatter(1, dx_early[1], 0, HALF)
+        for j, (dx, first) in enumerate(dx_late):
+            scatter(j, dx[:], first, N)
+            nc.sync.dma_start(out=out[P * j : P * (j + 1), :], in_=window[j][:])

@@ -79,10 +79,10 @@ def tile_attend_gml_nce_kernel(tc, xT, wd_words, wd_scales, wv_words, wv_scales,
         nc.sync.dma_start(out=cw4[:], in_=cw.rearrange("(p r) o -> p (r o)", r=PACK))
         nc.sync.dma_start(out=x_plane[2][:], in_=x_rows[:, 2, :])
         nc.sync.dma_start(out=x_plane[3][:], in_=x_rows[:, 3, :])
+        load_scale_rows(nc, wv_scale, wv_scales)
         nc.sync.dma_start(out=y_half[0][:], in_=y_rows[:, :, 0:HALF])
         nc.sync.dma_start(out=y_half[1][:], in_=y_rows[:, :, HALF:N])
         nc.sync.dma_start(out=wv_codes[:].bitcast(I32), in_=wv_words[0].bitcast(I32))
-        load_scale_rows(nc, wv_scale, wv_scales)
 
         window = [sb.tile([P, T], F32, name=f"window{j}") for j in range(2)]
         for j in range(2):
@@ -92,16 +92,16 @@ def tile_attend_gml_nce_kernel(tc, xT, wd_words, wd_scales, wv_words, wv_scales,
         nc.tensor.transpose(rw_turned[:], rw_rows[:], ident[:])
         minus_rw = sb.tile([P, N // P], F32, name="minus_rw")
         nc.scalar.activation(out=minus_rw[:], in_=rw_turned[:, 0 : N // P], func=ACT.Copy, scale=-1.0)
-        rw_spread = bank(7, [P, 2, P], "rw_spread")
-        for c in range(2):
-            nc.tensor.transpose(rw_spread[:, c, :], minus_rw[:, c : c + 1].to_broadcast([P, P]), ident[:])
+        rw_spread = bank(7, [P, 3, P], "rw_spread")
+        for k, c in enumerate((0, 1, 3)):
+            nc.tensor.transpose(rw_spread[:, k, :], minus_rw[:, c : c + 1].to_broadcast([P, P]), ident[:])
         cw_spread = bank(6, [P, PACK, P], "cw_spread")
         for r in range(PACK):
             nc.tensor.transpose(cw_spread[:, PLACE[r], :], cw4[:, r : r + 1].to_broadcast([P, P]), ident[:])
         window.append(sb.tile([P, T], F32, name="window2", tag="rw_then_window"))
         nc.gpsimd.memset(window[2][:].bitcast(I32), 0)
         window.append(window[0])
-        weight = sb.tile([P, PACK, HALF], F32, name="weight")
+        weight = sb.tile([P, PACK, 3 * P], F32, name="weight")
         for r in range(PACK):
             nc.scalar.activation(
                 out=weight[:, r, :],
@@ -110,7 +110,7 @@ def tile_attend_gml_nce_kernel(tc, xT, wd_words, wd_scales, wv_words, wv_scales,
                 scale=cw4[:, r : r + 1],
             )
         turned_weight = []
-        for c in range(2):
+        for c in range(1):
             turned_weight.append(sb.tile([P, V], F32, name=f"turned_weight{c}"))
             nc.scalar.activation(
                 out=turned_weight[c][:].rearrange("q (k e) -> q k e", e=2),
@@ -148,7 +148,7 @@ def tile_attend_gml_nce_kernel(tc, xT, wd_words, wd_scales, wv_words, wv_scales,
                 in_=x_words[:, HALF * h : HALF * (h + 1), :][:, cols, :].rearrange("p n t -> p (n t)"),
             )
 
-        def sigmoid_of_scores(h, planes, cols, number, sign):
+        def sigmoid_of_scores(h, planes, cols, number, sign, sig=None):
             shape = [P, len(planes), cols.stop - cols.start]
             score = bank(number, shape, f"score{number}")
             for u, r in enumerate(planes):
@@ -161,8 +161,9 @@ def tile_attend_gml_nce_kernel(tc, xT, wd_words, wd_scales, wv_words, wv_scales,
                     start=True,
                     stop=True,
                 )
-            sig = sb.tile(shape, F32, name=f"sig{number}")
-            nc.scalar.activation(out=sig[:], in_=score[:], func=ACT.Sigmoid, scale=sign)
+            if sig is None:
+                sig = sb.tile(shape, F32, name=f"sig{number}")[:]
+            nc.scalar.activation(out=sig, in_=score[:], func=ACT.Sigmoid, scale=sign)
             return sig
 
         for t in range(PACK - 1):
@@ -176,29 +177,19 @@ def tile_attend_gml_nce_kernel(tc, xT, wd_words, wd_scales, wv_words, wv_scales,
         sig_first = {r: sigmoid_of_scores(0, [r], BOTH, r, 1.0) for r in range(1, PACK)}
         gather(PACK - 1, HALF - OVERLAP, N)
         quantize_x(1, BOTH)
-        sig_second = [sigmoid_of_scores(1, [2 * b, 2 * b + 1], BOTH, 4 + b, -1.0) for b in range(2)]
+        sig_turned = sigmoid_of_scores(1, range(PACK), CHUNK[0], 4, -1.0)
+        sig_last = sigmoid_of_scores(1, range(PACK), CHUNK[1], 5, 1.0)
 
         diff = sb.tile([P, 2, PACK, P], F32, name="diff")
-        g_words = [sb.tile([P, 2, P * PACK], BF16, name=f"g_words{h}", align_bytes=64) for h in range(2)]
+        g_words = [sb.tile([P, 3 - h, P * PACK], BF16, name=f"g_words{h}", align_bytes=64) for h in range(2)]
 
-        sums = [bank(c, [P, PACK, P], f"sums{c}") for c in range(2)]
-        for c in range(2):
-            for r in range(PACK):
-                nc.tensor.matmul(
-                    sums[c][:, PLACE[r], :], y_half[1][:, r, CHUNK[c]], ident[:], is_transpose=True, start=r == 0, stop=False
-                )
-        for b in range(2):
-            for c in range(2):
-                for u in range(2):
-                    r = 2 * b + u
-                    nc.tensor.matmul(
-                        sums[c][:, PLACE[r], :],
-                        sig_second[b][:, u, CHUNK[c]],
-                        ident[:],
-                        is_transpose=True,
-                        start=False,
-                        stop=r == PACK - 1,
-                    )
+        sums = [bank(0, [P, PACK, P], "sums0")]
+        for r in range(PACK):
+            nc.tensor.matmul(sums[0][:, PLACE[r], :], y_half[1][:, r, CHUNK[0]], ident[:], is_transpose=True, start=r == 0, stop=False)
+        for r in range(PACK):
+            nc.tensor.matmul(
+                sums[0][:, PLACE[r], :], sig_turned[:, r, :], ident[:], is_transpose=True, start=False, stop=r == PACK - 1
+            )
 
         def subtract_plane(r, chunks):
             nc.vector.tensor_tensor(
@@ -220,13 +211,13 @@ def tile_attend_gml_nce_kernel(tc, xT, wd_words, wd_scales, wv_words, wv_scales,
             subtract_plane(PACK - 1, slice(c, c + 1))
         for c in range(2):
             nc.vector.tensor_tensor(
-                g_words[0][:, c, :].rearrange("p (k i r) -> p k r i", i=RUN, r=PACK),
+                g_words[0][:, 1 + c, :].rearrange("p (k i r) -> p k r i", i=RUN, r=PACK),
                 diff[:, c, :, :].rearrange("p r (k i) -> p k r i", i=RUN),
                 weight[:, :, CHUNK[c]].rearrange("p r (k i) -> p k r i", i=RUN),
                 ALU.mult,
             )
         for c in range(2):
-            quantize_g(g_words[0][:, c, :], P * c, P * (c + 1))
+            quantize_g(g_words[0][:, 1 + c, :], P * c, P * (c + 1))
 
         def back(j, first, number):
             acc = bank(number, [P, N], f"acc{j}_{first}")
@@ -243,8 +234,16 @@ def tile_attend_gml_nce_kernel(tc, xT, wd_words, wd_scales, wv_words, wv_scales,
 
         early = [back(j, 0, 6 + j) for j in range(EARLY_TILES)]
 
-        g_turned = [g_words[0][:, c, :] for c in range(2)]
-        for c in range(2):
+        diff_last = g_words[0][:, 0:2, :].rearrange("p c n -> p (c n)").bitcast(F32).rearrange("p (r i) -> p r i", i=P)
+        nc.vector.tensor_tensor(diff_last, y_half[1][:, :, CHUNK[1]], sig_last, ALU.subtract)
+        nc.gpsimd.tensor_tensor(
+            g_words[1][:, 1, :].rearrange("p (k i r) -> p k r i", i=RUN, r=PACK),
+            diff_last.rearrange("p r (k i) -> p k r i", i=RUN),
+            weight[:, :, HALF : HALF + P].rearrange("p r (k i) -> p k r i", i=RUN),
+            ALU.mult,
+        )
+        g_turned = [g_words[0][:, 2, :]]
+        for c in range(1):
             nc.vector.scalar_tensor_tensor(
                 g_turned[c].rearrange("q (k e) -> q k e", e=2),
                 sums[c][:].rearrange("q (e u) p -> q (u p) e", e=2),
@@ -254,14 +253,14 @@ def tile_attend_gml_nce_kernel(tc, xT, wd_words, wd_scales, wv_words, wv_scales,
                 ALU.mult,
             )
 
-        dx_early = [turned_weight[0][:, 0:HALF], g_turned[1].bitcast(F32)]
+        dx_first = sb.tile([P, HALF], F32, name="dx_first")
+        dx_early = [dx_first[:], g_turned[0].bitcast(F32)]
         nc.scalar.copy(out=dx_early[0], in_=early[0][:, HALF:N])
-        pairs = bank(6, [P, 2, 2, P], "pairs")
-        for c in range(2):
-            for u in range(2):
-                nc.tensor.transpose(pairs[:, c, u, :], g_turned[c].bitcast(F32)[:, P * u : P * (u + 1)], ident[:])
+        pairs = bank(6, [P, 2, P], "pairs")
+        for u in range(2):
+            nc.tensor.transpose(pairs[:, u, :], g_turned[0].bitcast(F32)[:, P * u : P * (u + 1)], ident[:])
         nc.scalar.copy(
-            out=g_words[1][:].bitcast(F32).rearrange("p c (q u) -> p c q u", u=2), in_=pairs[:].rearrange("p c u q -> p c q u")
+            out=g_words[1][:, 0, :].bitcast(F32).rearrange("p (q u) -> p q u", u=2), in_=pairs[:].rearrange("p u q -> p q u")
         )
         nc.scalar.copy(out=dx_early[1], in_=early[1][:, HALF:N])
 

@@ -28,6 +28,7 @@ RUN = 4
 PLACE = (0, 2, 1, 3)
 CHUNK = (slice(0, P), slice(P, HALF))
 BOTH = slice(0, HALF)
+SHARE = 32
 
 
 def load_scale_rows(nc, tile, scales):
@@ -92,20 +93,27 @@ def tile_attend_gml_nce_kernel(tc, xT, wd_words, wd_scales, wv_words, wv_scales,
         nc.tensor.transpose(rw_turned[:], rw_rows[:], ident[:])
         minus_rw = sb.tile([P, N // P], F32, name="minus_rw")
         nc.scalar.activation(out=minus_rw[:], in_=rw_turned[:, 0 : N // P], func=ACT.Copy, scale=-1.0)
-        rw_spread = bank(7, [P, 3, P], "rw_spread")
-        for k, c in enumerate((0, 1, 3)):
+        rw_spread = bank(7, [P, 2, P], "rw_spread")
+        for k, c in enumerate((1, 3)):
             nc.tensor.transpose(rw_spread[:, k, :], minus_rw[:, c : c + 1].to_broadcast([P, P]), ident[:])
-        cw_spread = bank(6, [P, PACK, P], "cw_spread")
+        cw_spread = bank(4, [P, PACK, P], "cw_spread")
         for r in range(PACK):
             nc.tensor.transpose(cw_spread[:, PLACE[r], :], cw4[:, r : r + 1].to_broadcast([P, P]), ident[:])
         window.append(sb.tile([P, T], F32, name="window2", tag="rw_then_window"))
         nc.gpsimd.memset(window[2][:].bitcast(I32), 0)
         window.append(window[0])
-        weight = sb.tile([P, PACK, 3 * P], F32, name="weight")
+        bank_weight = []
+        for c in range(2):
+            rows = sb.tile([P, PACK, P], F32, name=f"weight_rows{c}")
+            nc.scalar.activation(out=rows[:], in_=cw_spread[:], func=ACT.Copy, scale=minus_rw[:, c : c + 1])
+            bank_weight.append(bank(5 + c, [P, PACK, P], f"bank_weight{c}"))
+            for r in range(PACK):
+                nc.tensor.transpose(bank_weight[c][:, r, :], rows[:, PLACE[r], :], ident[:])
+        weight = sb.tile([P, PACK, SHARE + P], F32, name="weight")
         for r in range(PACK):
             nc.scalar.activation(
                 out=weight[:, r, :],
-                in_=rw_spread[:].rearrange("q c i -> q (c i)"),
+                in_=rw_spread[:].rearrange("q c i -> q (c i)")[:, P - SHARE : 2 * P],
                 func=ACT.Copy,
                 scale=cw4[:, r : r + 1],
             )
@@ -148,7 +156,7 @@ def tile_attend_gml_nce_kernel(tc, xT, wd_words, wd_scales, wv_words, wv_scales,
                 in_=x_words[:, HALF * h : HALF * (h + 1), :][:, cols, :].rearrange("p n t -> p (n t)"),
             )
 
-        def sigmoid_of_scores(h, planes, cols, number, sign, sig=None):
+        def sigmoid_of_scores(h, planes, cols, number, sign, parts=(slice(None),), sig=None):
             shape = [P, len(planes), cols.stop - cols.start]
             score = bank(number, shape, f"score{number}")
             for u, r in enumerate(planes):
@@ -162,8 +170,9 @@ def tile_attend_gml_nce_kernel(tc, xT, wd_words, wd_scales, wv_words, wv_scales,
                     stop=True,
                 )
             if sig is None:
-                sig = sb.tile(shape, F32, name=f"sig{number}")[:]
-            nc.scalar.activation(out=sig, in_=score[:], func=ACT.Sigmoid, scale=sign)
+                sig = sb.tile(shape, F32, name=f"sig{h}_{number}")[:]
+            for part in parts:
+                nc.scalar.activation(out=sig[:, :, part], in_=score[:, :, part], func=ACT.Sigmoid, scale=sign)
             return sig
 
         for t in range(PACK - 1):
@@ -171,14 +180,20 @@ def tile_attend_gml_nce_kernel(tc, xT, wd_words, wd_scales, wv_words, wv_scales,
 
         gather(PACK - 1, 0, HALF)
         quantize_x(0, CHUNK[1])
-        sig_plane0 = {1: sigmoid_of_scores(0, [0], CHUNK[1], 7, 1.0)}
+        sig_plane0 = sb.tile([P, 1, HALF], F32, name="sig_plane0")
+        sigmoid_of_scores(0, [0], CHUNK[1], 7, 1.0, sig=sig_plane0[:, :, CHUNK[1]])
         quantize_x(0, CHUNK[0])
-        sig_plane0[0] = sigmoid_of_scores(0, [0], CHUNK[0], 0, 1.0)
-        sig_first = {r: sigmoid_of_scores(0, [r], BOTH, r, 1.0) for r in range(1, PACK)}
+        sigmoid_of_scores(0, [0], CHUNK[0], 0, 1.0, sig=sig_plane0[:, :, CHUNK[0]])
+        sig_first = {r: sigmoid_of_scores(0, [r], BOTH, r, 1.0) for r in range(1, PACK - 1)}
+        sig_first[0] = sig_plane0[:]
+        sig_first[PACK - 1] = sigmoid_of_scores(0, [PACK - 1], BOTH, PACK - 1, 1.0, (CHUNK[1], CHUNK[0]))
         gather(PACK - 1, HALF - OVERLAP, N)
         quantize_x(1, BOTH)
-        sig_turned = sigmoid_of_scores(1, range(PACK), CHUNK[0], 4, -1.0)
-        sig_last = sigmoid_of_scores(1, range(PACK), CHUNK[1], 5, 1.0)
+        sig_second = sb.tile([P, PACK, HALF], F32, name="sig_second")
+        sigmoid_of_scores(1, [0, 1], BOTH, 4, -1.0, sig=sig_second[:, 0:2, :])
+        sigmoid_of_scores(1, [2, 3], BOTH, 7, -1.0, CHUNK, sig_second[:, 2:4, :])
+        sig_turned = sig_second[:, :, CHUNK[0]]
+        sig_last = sig_second[:, :, CHUNK[1]]
 
         diff = sb.tile([P, 2, PACK, P], F32, name="diff")
         g_words = [sb.tile([P, 3 - h, P * PACK], BF16, name=f"g_words{h}", align_bytes=64) for h in range(2)]
@@ -203,21 +218,25 @@ def tile_attend_gml_nce_kernel(tc, xT, wd_words, wd_scales, wv_words, wv_scales,
             cols = slice(HALF + first, HALF + end)
             nc.vector.quantize_mx(out=g_codes[:, cols].bitcast(E5M2X4), scales=g_scale[:, cols], in_=words)
 
-        for c in (1, 0):
-            nc.vector.tensor_tensor(diff[:, c, 0, :], y_half[0][:, 0, CHUNK[c]], sig_plane0[c][:, 0, :], ALU.subtract)
-        for r in range(1, PACK - 1):
+        for r in range(PACK - 1):
             subtract_plane(r, slice(0, 2))
-        for c in range(2):
+        for c in (1, 0):
             subtract_plane(PACK - 1, slice(c, c + 1))
-        for c in range(2):
-            nc.vector.tensor_tensor(
-                g_words[0][:, 1 + c, :].rearrange("p (k i r) -> p k r i", i=RUN, r=PACK),
-                diff[:, c, :, :].rearrange("p r (k i) -> p k r i", i=RUN),
-                weight[:, :, CHUNK[c]].rearrange("p r (k i) -> p k r i", i=RUN),
+
+        def weigh(engine, words, differences, weights):
+            engine.tensor_tensor(
+                words.rearrange("p (k i r) -> p k r i", i=RUN, r=PACK),
+                differences.rearrange("p r (k i) -> p k r i", i=RUN),
+                weights.rearrange("p r (k i) -> p k r i", i=RUN),
                 ALU.mult,
             )
-        for c in range(2):
-            quantize_g(g_words[0][:, 1 + c, :], P * c, P * (c + 1))
+
+        own = P - SHARE
+        weigh(nc.gpsimd, g_words[0][:, 1, PACK * own :], diff[:, 1, :, own:P], weight[:, :, 0:SHARE])
+        weigh(nc.vector, g_words[0][:, 1, 0 : PACK * own], diff[:, 1, :, 0:own], bank_weight[1][:, :, 0:own])
+        weigh(nc.vector, g_words[0][:, 2, :], diff[:, 0, :, :], bank_weight[0][:])
+        for c in (1, 0):
+            quantize_g(g_words[0][:, 2 - c, :], P * c, P * (c + 1))
 
         def back(j, first, number):
             acc = bank(number, [P, N], f"acc{j}_{first}")
@@ -232,14 +251,14 @@ def tile_attend_gml_nce_kernel(tc, xT, wd_words, wd_scales, wv_words, wv_scales,
             )
             return acc
 
-        early = [back(j, 0, 6 + j) for j in range(EARLY_TILES)]
+        early = [back(j, 0, 1 + j) for j in range(EARLY_TILES)]
 
         diff_last = g_words[0][:, 0:2, :].rearrange("p c n -> p (c n)").bitcast(F32).rearrange("p (r i) -> p r i", i=P)
-        nc.vector.tensor_tensor(diff_last, y_half[1][:, :, CHUNK[1]], sig_last, ALU.subtract)
+        nc.vector.scalar_tensor_tensor(diff_last, sig_last, -1.0, y_half[1][:, :, CHUNK[1]], ALU.add, ALU.add)
         nc.gpsimd.tensor_tensor(
             g_words[1][:, 1, :].rearrange("p (k i r) -> p k r i", i=RUN, r=PACK),
             diff_last.rearrange("p r (k i) -> p k r i", i=RUN),
-            weight[:, :, HALF : HALF + P].rearrange("p r (k i) -> p k r i", i=RUN),
+            weight[:, :, SHARE : SHARE + P].rearrange("p r (k i) -> p k r i", i=RUN),
             ALU.mult,
         )
         g_turned = [g_words[0][:, 2, :]]
@@ -256,7 +275,7 @@ def tile_attend_gml_nce_kernel(tc, xT, wd_words, wd_scales, wv_words, wv_scales,
         dx_first = sb.tile([P, HALF], F32, name="dx_first")
         dx_early = [dx_first[:], g_turned[0].bitcast(F32)]
         nc.scalar.copy(out=dx_early[0], in_=early[0][:, HALF:N])
-        pairs = bank(6, [P, 2, P], "pairs")
+        pairs = bank(1, [P, 2, P], "pairs")
         for u in range(2):
             nc.tensor.transpose(pairs[:, u, :], g_turned[0].bitcast(F32)[:, P * u : P * (u + 1)], ident[:])
         nc.scalar.copy(
@@ -271,7 +290,7 @@ def tile_attend_gml_nce_kernel(tc, xT, wd_words, wd_scales, wv_words, wv_scales,
         quantize_g(g_words[1][:].rearrange("p c n -> p (c n)"), HALF, N)
 
         dx_late = []
-        for j, number in enumerate((4, 5, 0, 1)):
+        for j, number in enumerate((3, 4, 5, 6)):
             acc = back(j, HALF, number)
             first = HALF if j < EARLY_TILES else 0
             dx = sb.tile([P, N - first], F32, name=f"dx_late{j}")

@@ -25,10 +25,10 @@ ENTRIES = 16
 EARLY_TILES = 2
 OVERLAP = 32
 RUN = 4
+SHARE = 40
+OWN = P - SHARE
 PLACE = (0, 2, 1, 3)
-CHUNK = (slice(0, P), slice(P, HALF))
-BOTH = slice(0, HALF)
-SHARE = 32
+LOW, HIGH, BOTH = slice(0, P), slice(P, HALF), slice(0, HALF)
 
 
 def load_scale_rows(nc, tile, scales):
@@ -55,16 +55,15 @@ def tile_attend_gml_nce_kernel(tc, xT, wd_words, wd_scales, wv_words, wv_scales,
         offsets = sb.tile([P, N // ENTRIES], U16, name="offsets")
         cw4 = sb.tile([P, PACK], F32, name="cw4")
         rw_rows = sb.tile([P, P], F32, name="rw_rows", tag="rw_then_window")
-        wd_in = sb.tile([P, 3 * V], U8, name="wd_in", tag="wd_then_x", align_bytes=64)
-        wd_in_words = wd_in[:, 0 : 2 * V]
-        wd_in_scale = wd_in[:, 2 * V : 3 * V]
+        wd_in_words = sb.tile([P, 2 * V], U8, name="wd_in_words", align_bytes=64)
+        wd_in_scale = sb.tile([P, V], U8, name="wd_in_scale", tag="scale_then_x", align_bytes=64)
         wv_codes = sb.tile([P, 2 * D], U8, name="wv_codes", align_bytes=64)
         wv_scale = sb.tile([P, D], U8, name="wv_scale", align_bytes=64)
         g_codes = sb.tile([P, HALF + N], U32, name="g_codes", align_bytes=64)
         g_scale = sb.tile([P, HALF + N], U8, name="g_scale", align_bytes=64)
         ident = sb.tile([P, P], F32, name="ident")
 
-        nc.vector.memset(wd_in_scale.bitcast(I32), 0)
+        nc.vector.memset(wd_in_scale[:].bitcast(I32), 0)
         nc.gpsimd.memset(rw_rows[:], 0.0)
         make_identity(nc, ident[:])
         nc.gpsimd.memset(wv_scale[:].bitcast(I32), 0)
@@ -72,7 +71,6 @@ def tile_attend_gml_nce_kernel(tc, xT, wd_words, wd_scales, wv_words, wv_scales,
         nc.gpsimd.memset(g_scale[:, 0:HALF].bitcast(I32), 0)
 
         nc.sync.dma_start(out=x_plane[0][:], in_=x_rows[:, 0, :])
-        nc.scalar.dma_start(out=wd_in_words.bitcast(I32), in_=wd_words[0].bitcast(I32))
         load_scale_rows(nc, wd_in_scale, wd_scales)
         nc.sync.dma_start(offsets[:], offs)
         nc.sync.dma_start(out=x_plane[1][:], in_=x_rows[:, 1, :])
@@ -80,6 +78,7 @@ def tile_attend_gml_nce_kernel(tc, xT, wd_words, wd_scales, wv_words, wv_scales,
         nc.sync.dma_start(out=cw4[:], in_=cw.rearrange("(p r) o -> p (r o)", r=PACK))
         nc.sync.dma_start(out=x_plane[2][:], in_=x_rows[:, 2, :])
         nc.sync.dma_start(out=x_plane[3][:], in_=x_rows[:, 3, :])
+        nc.sync.dma_start(out=wd_in_words[:].bitcast(I32), in_=wd_words[0].bitcast(I32))
         load_scale_rows(nc, wv_scale, wv_scales)
         nc.sync.dma_start(out=y_half[0][:], in_=y_rows[:, :, 0:HALF])
         nc.sync.dma_start(out=y_half[1][:], in_=y_rows[:, :, HALF:N])
@@ -109,39 +108,33 @@ def tile_attend_gml_nce_kernel(tc, xT, wd_words, wd_scales, wv_words, wv_scales,
             bank_weight.append(bank(5 + c, [P, PACK, P], f"bank_weight{c}"))
             for r in range(PACK):
                 nc.tensor.transpose(bank_weight[c][:, r, :], rows[:, PLACE[r], :], ident[:])
-        weight = sb.tile([P, PACK, SHARE + P], F32, name="weight")
+        gpsimd_weight = sb.tile([P, PACK, SHARE + P], F32, name="gpsimd_weight")
         for r in range(PACK):
             nc.scalar.activation(
-                out=weight[:, r, :],
-                in_=rw_spread[:].rearrange("q c i -> q (c i)")[:, P - SHARE : 2 * P],
+                out=gpsimd_weight[:, r, :],
+                in_=rw_spread[:].rearrange("q c i -> q (c i)")[:, OWN : 2 * P],
                 func=ACT.Copy,
                 scale=cw4[:, r : r + 1],
             )
-        turned_weight = []
-        for c in range(1):
-            turned_weight.append(sb.tile([P, V], F32, name=f"turned_weight{c}"))
-            nc.scalar.activation(
-                out=turned_weight[c][:].rearrange("q (k e) -> q k e", e=2),
-                in_=cw_spread[:].rearrange("q (e u) p -> q (u p) e", e=2),
-                func=ACT.Copy,
-                scale=minus_rw[:, 2 + c : 3 + c],
-            )
+        turned_weight = sb.tile([P, V], F32, name="turned_weight")
+        nc.scalar.activation(
+            out=turned_weight[:].rearrange("q (k e) -> q k e", e=2),
+            in_=cw_spread[:].rearrange("q (e u) p -> q (u p) e", e=2),
+            func=ACT.Copy,
+            scale=minus_rw[:, 2:3],
+        )
 
         wd_dealt = sb.tile([P, 3 * V], U8, name="wd_dealt", align_bytes=64)
         wd_codes = wd_dealt[:, 0 : 2 * V]
         wd_scale = wd_dealt[:, 2 * V : 3 * V]
         nc.vector.tensor_copy(
-            out=wd_codes.bitcast(U16).rearrange("p (r s) -> p s r", r=PACK),
-            in_=wd_in_words.bitcast(U16).rearrange("p (s r) -> p s r", r=PACK),
-        )
-        nc.vector.tensor_copy(
             out=wd_scale.rearrange("p (r s) -> p s r", r=PACK),
-            in_=wd_in_scale.rearrange("p (s r) -> p s r", r=PACK),
+            in_=wd_in_scale[:].rearrange("p (s r) -> p s r", r=PACK),
         )
 
-        x_words = sb.tile([P, N, PACK], BF16, name="x_words", tag="wd_then_x", align_bytes=64)
+        x_words = sb.tile([P, N, PACK], BF16, name="x_words", tag="scale_then_x", align_bytes=64)
         x_codes = [sb.tile([P, HALF], U32, name=f"x_codes{h}", align_bytes=64) for h in range(2)]
-        x_scale = [sb.tile([P, HALF], U8, name=f"x_scale{h}", align_bytes=64) for h in range(2)]
+        x_scale = [wd_in_words[:, 2 * V - HALF :], sb.tile([P, HALF], U8, name="x_scale1", align_bytes=64)]
 
         def entries(first, end):
             return offsets[:, first // ENTRIES : end // ENTRIES]
@@ -156,9 +149,8 @@ def tile_attend_gml_nce_kernel(tc, xT, wd_words, wd_scales, wv_words, wv_scales,
                 in_=x_words[:, HALF * h : HALF * (h + 1), :][:, cols, :].rearrange("p n t -> p (n t)"),
             )
 
-        def sigmoid_of_scores(h, planes, cols, number, sign, parts=(slice(None),), sig=None):
-            shape = [P, len(planes), cols.stop - cols.start]
-            score = bank(number, shape, f"score{number}")
+        def scores(h, planes, cols, number):
+            score = bank(number, [P, len(planes), cols.stop - cols.start], f"score{number}")
             for u, r in enumerate(planes):
                 nc.tensor.matmul_mx(
                     out=score[:, u, :],
@@ -169,49 +161,64 @@ def tile_attend_gml_nce_kernel(tc, xT, wd_words, wd_scales, wv_words, wv_scales,
                     start=True,
                     stop=True,
                 )
-            if sig is None:
-                sig = sb.tile(shape, F32, name=f"sig{h}_{number}")[:]
-            for part in parts:
-                nc.scalar.activation(out=sig[:, :, part], in_=score[:, :, part], func=ACT.Sigmoid, scale=sign)
-            return sig
+            return score
+
+        def sigmoid(result, score, sign):
+            nc.scalar.activation(out=result, in_=score, func=ACT.Sigmoid, scale=sign)
 
         for t in range(PACK - 1):
             gather(t, 0, N)
 
         gather(PACK - 1, 0, HALF)
-        quantize_x(0, CHUNK[1])
-        sig_plane0 = sb.tile([P, 1, HALF], F32, name="sig_plane0")
-        sigmoid_of_scores(0, [0], CHUNK[1], 7, 1.0, sig=sig_plane0[:, :, CHUNK[1]])
-        quantize_x(0, CHUNK[0])
-        sigmoid_of_scores(0, [0], CHUNK[0], 0, 1.0, sig=sig_plane0[:, :, CHUNK[0]])
-        sig_first = {r: sigmoid_of_scores(0, [r], BOTH, r, 1.0) for r in range(1, PACK - 1)}
-        sig_first[0] = sig_plane0[:]
-        sig_first[PACK - 1] = sigmoid_of_scores(0, [PACK - 1], BOTH, PACK - 1, 1.0, (CHUNK[1], CHUNK[0]))
+        under_chunk1 = P - P // (2 * PACK)
+        for s in (slice(under_chunk1, P), slice(0, under_chunk1)):
+            nc.vector.tensor_copy(
+                out=wd_codes.bitcast(U16).rearrange("p (r s) -> p r s", r=PACK)[:, :, s],
+                in_=wd_in_words[:].bitcast(U16).rearrange("p (s r) -> p r s", r=PACK)[:, :, s],
+            )
+        sig_first = [sb.tile([P, HALF], F32, name=f"sig_first{r}") for r in range(PACK)]
+        for cols, number in ((HIGH, 7), (LOW, 0)):
+            quantize_x(0, cols)
+            sigmoid(sig_first[0][:, cols], scores(0, [0], cols, number)[:, 0, :], 1.0)
+        for r in range(1, PACK - 1):
+            sigmoid(sig_first[r][:], scores(0, [r], BOTH, r)[:, 0, :], 1.0)
+        score = scores(0, [PACK - 1], BOTH, PACK - 1)
+        for cols in (HIGH, LOW):
+            sigmoid(sig_first[PACK - 1][:, cols], score[:, 0, cols], 1.0)
         gather(PACK - 1, HALF - OVERLAP, N)
         quantize_x(1, BOTH)
         sig_second = sb.tile([P, PACK, HALF], F32, name="sig_second")
-        sigmoid_of_scores(1, [0, 1], BOTH, 4, -1.0, sig=sig_second[:, 0:2, :])
-        sigmoid_of_scores(1, [2, 3], BOTH, 7, -1.0, CHUNK, sig_second[:, 2:4, :])
-        sig_turned = sig_second[:, :, CHUNK[0]]
-        sig_last = sig_second[:, :, CHUNK[1]]
+        sigmoid(sig_second[:, 0:2, :], scores(1, [0, 1], BOTH, 4)[:], -1.0)
+        score = scores(1, [2, 3], BOTH, 7)
+        for cols in (LOW, HIGH):
+            sigmoid(sig_second[:, 2:4, cols], score[:, :, cols], -1.0)
 
         diff = sb.tile([P, 2, PACK, P], F32, name="diff")
-        g_words = [sb.tile([P, 3 - h, P * PACK], BF16, name=f"g_words{h}", align_bytes=64) for h in range(2)]
+        g_first = sb.tile([P, 3, P * PACK], BF16, name="g_first", align_bytes=64)
+        g_second = sb.tile([P, 2, P * PACK], BF16, name="g_second", align_bytes=64)
 
-        sums = [bank(0, [P, PACK, P], "sums0")]
+        sums = bank(0, [P, PACK, P], "sums")
         for r in range(PACK):
-            nc.tensor.matmul(sums[0][:, PLACE[r], :], y_half[1][:, r, CHUNK[0]], ident[:], is_transpose=True, start=r == 0, stop=False)
+            nc.tensor.matmul(sums[:, PLACE[r], :], y_half[1][:, r, LOW], ident[:], is_transpose=True, start=r == 0, stop=False)
         for r in range(PACK):
             nc.tensor.matmul(
-                sums[0][:, PLACE[r], :], sig_turned[:, r, :], ident[:], is_transpose=True, start=False, stop=r == PACK - 1
+                sums[:, PLACE[r], :], sig_second[:, r, LOW], ident[:], is_transpose=True, start=False, stop=r == PACK - 1
             )
 
         def subtract_plane(r, chunks):
             nc.vector.tensor_tensor(
                 diff[:, chunks, r, :],
                 y_half[0][:, r, :].rearrange("p (c i) -> p c i", i=P)[:, chunks, :],
-                sig_first[r][:, 0, :].rearrange("p (c i) -> p c i", i=P)[:, chunks, :],
+                sig_first[r][:].rearrange("p (c i) -> p c i", i=P)[:, chunks, :],
                 ALU.subtract,
+            )
+
+        def weigh(engine, words, differences, weights):
+            engine.tensor_tensor(
+                words.rearrange("p (k i r) -> p k r i", i=RUN, r=PACK),
+                differences.rearrange("p r (k i) -> p k r i", i=RUN),
+                weights.rearrange("p r (k i) -> p k r i", i=RUN),
+                ALU.mult,
             )
 
         def quantize_g(words, first, end):
@@ -222,21 +229,11 @@ def tile_attend_gml_nce_kernel(tc, xT, wd_words, wd_scales, wv_words, wv_scales,
             subtract_plane(r, slice(0, 2))
         for c in (1, 0):
             subtract_plane(PACK - 1, slice(c, c + 1))
-
-        def weigh(engine, words, differences, weights):
-            engine.tensor_tensor(
-                words.rearrange("p (k i r) -> p k r i", i=RUN, r=PACK),
-                differences.rearrange("p r (k i) -> p k r i", i=RUN),
-                weights.rearrange("p r (k i) -> p k r i", i=RUN),
-                ALU.mult,
-            )
-
-        own = P - SHARE
-        weigh(nc.gpsimd, g_words[0][:, 1, PACK * own :], diff[:, 1, :, own:P], weight[:, :, 0:SHARE])
-        weigh(nc.vector, g_words[0][:, 1, 0 : PACK * own], diff[:, 1, :, 0:own], bank_weight[1][:, :, 0:own])
-        weigh(nc.vector, g_words[0][:, 2, :], diff[:, 0, :, :], bank_weight[0][:])
+        weigh(nc.gpsimd, g_first[:, 1, PACK * OWN :], diff[:, 1, :, OWN:P], gpsimd_weight[:, :, 0:SHARE])
+        weigh(nc.vector, g_first[:, 1, 0 : PACK * OWN], diff[:, 1, :, 0:OWN], bank_weight[1][:, :, 0:OWN])
+        weigh(nc.vector, g_first[:, 2, :], diff[:, 0, :, :], bank_weight[0][:])
         for c in (1, 0):
-            quantize_g(g_words[0][:, 2 - c, :], P * c, P * (c + 1))
+            quantize_g(g_first[:, 2 - c, :], P * c, P * (c + 1))
 
         def back(j, first, number):
             acc = bank(number, [P, N], f"acc{j}_{first}")
@@ -253,33 +250,27 @@ def tile_attend_gml_nce_kernel(tc, xT, wd_words, wd_scales, wv_words, wv_scales,
 
         early = [back(j, 0, 1 + j) for j in range(EARLY_TILES)]
 
-        diff_last = g_words[0][:, 0:2, :].rearrange("p c n -> p (c n)").bitcast(F32).rearrange("p (r i) -> p r i", i=P)
-        nc.vector.scalar_tensor_tensor(diff_last, sig_last, -1.0, y_half[1][:, :, CHUNK[1]], ALU.add, ALU.add)
-        nc.gpsimd.tensor_tensor(
-            g_words[1][:, 1, :].rearrange("p (k i r) -> p k r i", i=RUN, r=PACK),
-            diff_last.rearrange("p r (k i) -> p k r i", i=RUN),
-            weight[:, :, SHARE : SHARE + P].rearrange("p r (k i) -> p k r i", i=RUN),
+        diff_last = g_first[:, 0:2, :].rearrange("p c n -> p (c n)").bitcast(F32).rearrange("p (r i) -> p r i", i=P)
+        nc.vector.scalar_tensor_tensor(diff_last, sig_second[:, :, HIGH], -1.0, y_half[1][:, :, HIGH], ALU.add, ALU.add)
+        weigh(nc.gpsimd, g_second[:, 1, :], diff_last, gpsimd_weight[:, :, SHARE:])
+        g_turned = g_first[:, 2, :]
+        nc.vector.scalar_tensor_tensor(
+            g_turned.rearrange("q (k e) -> q k e", e=2),
+            sums[:].rearrange("q (e u) p -> q (u p) e", e=2),
+            -1.0,
+            turned_weight[:].rearrange("q (k e) -> q k e", e=2),
+            ALU.add,
             ALU.mult,
         )
-        g_turned = [g_words[0][:, 2, :]]
-        for c in range(1):
-            nc.vector.scalar_tensor_tensor(
-                g_turned[c].rearrange("q (k e) -> q k e", e=2),
-                sums[c][:].rearrange("q (e u) p -> q (u p) e", e=2),
-                -1.0,
-                turned_weight[c][:].rearrange("q (k e) -> q k e", e=2),
-                ALU.add,
-                ALU.mult,
-            )
 
         dx_first = sb.tile([P, HALF], F32, name="dx_first")
-        dx_early = [dx_first[:], g_turned[0].bitcast(F32)]
+        dx_early = [dx_first[:], g_turned.bitcast(F32)]
         nc.scalar.copy(out=dx_early[0], in_=early[0][:, HALF:N])
         pairs = bank(1, [P, 2, P], "pairs")
         for u in range(2):
-            nc.tensor.transpose(pairs[:, u, :], g_turned[0].bitcast(F32)[:, P * u : P * (u + 1)], ident[:])
+            nc.tensor.transpose(pairs[:, u, :], g_turned.bitcast(F32)[:, P * u : P * (u + 1)], ident[:])
         nc.scalar.copy(
-            out=g_words[1][:, 0, :].bitcast(F32).rearrange("p (q u) -> p q u", u=2), in_=pairs[:].rearrange("p u q -> p q u")
+            out=g_second[:, 0, :].bitcast(F32).rearrange("p (q u) -> p q u", u=2), in_=pairs[:].rearrange("p u q -> p q u")
         )
         nc.scalar.copy(out=dx_early[1], in_=early[1][:, HALF:N])
 
@@ -287,7 +278,7 @@ def tile_attend_gml_nce_kernel(tc, xT, wd_words, wd_scales, wv_words, wv_scales,
             nc.vector.tensor_copy(out=window[j][:].indirect(entries(first, end)), in_=dx)
 
         scatter(0, dx_early[0], 0, HALF)
-        quantize_g(g_words[1][:].rearrange("p c n -> p (c n)"), HALF, N)
+        quantize_g(g_second[:].rearrange("p c n -> p (c n)"), HALF, N)
 
         dx_late = []
         for j, number in enumerate((3, 4, 5, 6)):

@@ -56,33 +56,25 @@ def tile_attend_gml_nce_kernel(tc, xT, wd_words, wd_scales, wv_words, wv_scales,
         cw4 = sb.tile([P, PACK], F32, name="cw4")
         rw_rows = sb.tile([P, P], F32, name="rw_rows", tag="rw_then_window")
         wd_in_words = sb.tile([P, 2 * V], U8, name="wd_in_words", align_bytes=64)
-        wd_in_scale = sb.tile([P, V], U8, name="wd_in_scale", tag="scale_then_x", align_bytes=64)
+        wd_in_scale = sb.tile([P, V], U8, name="wd_in_scale", tag="scale_then_back", align_bytes=64)
         wv_codes = sb.tile([P, 2 * D], U8, name="wv_codes", align_bytes=64)
-        wv_scale = sb.tile([P, D], U8, name="wv_scale", align_bytes=64)
-        g_codes = sb.tile([P, HALF + N], U32, name="g_codes", align_bytes=64)
-        g_scale = sb.tile([P, HALF + N], U8, name="g_scale", align_bytes=64)
         ident = sb.tile([P, P], F32, name="ident")
 
         nc.vector.memset(wd_in_scale[:].bitcast(I32), 0)
         nc.gpsimd.memset(rw_rows[:], 0.0)
         make_identity(nc, ident[:])
-        nc.gpsimd.memset(wv_scale[:].bitcast(I32), 0)
-        nc.gpsimd.memset(g_codes[:, 0:HALF], 0)
-        nc.gpsimd.memset(g_scale[:, 0:HALF].bitcast(I32), 0)
 
         nc.sync.dma_start(out=x_plane[0][:], in_=x_rows[:, 0, :])
-        load_scale_rows(nc, wd_in_scale, wd_scales)
         nc.sync.dma_start(offsets[:], offs)
+        load_scale_rows(nc, wd_in_scale, wd_scales)
         nc.sync.dma_start(out=x_plane[1][:], in_=x_rows[:, 1, :])
         nc.sync.dma_start(out=rw_rows[0 : N // P, :], in_=rw[0].rearrange("(c q) -> c q", q=P))
         nc.sync.dma_start(out=cw4[:], in_=cw.rearrange("(p r) o -> p (r o)", r=PACK))
         nc.sync.dma_start(out=x_plane[2][:], in_=x_rows[:, 2, :])
         nc.sync.dma_start(out=x_plane[3][:], in_=x_rows[:, 3, :])
         nc.sync.dma_start(out=wd_in_words[:].bitcast(I32), in_=wd_words[0].bitcast(I32))
-        load_scale_rows(nc, wv_scale, wv_scales)
         nc.sync.dma_start(out=y_half[0][:], in_=y_rows[:, :, 0:HALF])
         nc.sync.dma_start(out=y_half[1][:], in_=y_rows[:, :, HALF:N])
-        nc.sync.dma_start(out=wv_codes[:].bitcast(I32), in_=wv_words[0].bitcast(I32))
 
         window = [sb.tile([P, T], F32, name=f"window{j}") for j in range(2)]
         for j in range(2):
@@ -124,15 +116,24 @@ def tile_attend_gml_nce_kernel(tc, xT, wd_words, wd_scales, wv_words, wv_scales,
             scale=minus_rw[:, 2:3],
         )
 
-        wd_dealt = sb.tile([P, 3 * V], U8, name="wd_dealt", align_bytes=64)
-        wd_codes = wd_dealt[:, 0 : 2 * V]
-        wd_scale = wd_dealt[:, 2 * V : 3 * V]
-        nc.vector.tensor_copy(
-            out=wd_scale.rearrange("p (r s) -> p s r", r=PACK),
+        wd_codes = sb.tile([P, 2 * V], U8, name="wd_codes", align_bytes=64)
+        wd_scale = sb.tile([P, V], U8, name="wd_scale", align_bytes=64)
+        nc.gpsimd.tensor_copy(
+            out=wd_scale[:].rearrange("p (r s) -> p s r", r=PACK),
             in_=wd_in_scale[:].rearrange("p (s r) -> p s r", r=PACK),
         )
 
-        x_words = sb.tile([P, N, PACK], BF16, name="x_words", tag="scale_then_x", align_bytes=64)
+        g_columns = HALF + N
+        back_bytes = sb.tile([P, D + 5 * g_columns], U8, name="back_bytes", tag="scale_then_back", align_bytes=64)
+        wv_scale = back_bytes[:, 0:D]
+        g_scale = back_bytes[:, D : D + g_columns]
+        g_codes = back_bytes[:, D + g_columns :].bitcast(U32)
+        nc.gpsimd.memset(back_bytes[:, 0 : D + HALF].bitcast(I32), 0)
+        nc.gpsimd.memset(g_codes[:, 0:HALF], 0)
+        load_scale_rows(nc, wv_scale, wv_scales)
+        nc.sync.dma_start(out=wv_codes[:].bitcast(I32), in_=wv_words[0].bitcast(I32))
+
+        x_words = sb.tile([P, N, PACK], BF16, name="x_words", align_bytes=64)
         x_codes = [sb.tile([P, HALF], U32, name=f"x_codes{h}", align_bytes=64) for h in range(2)]
         x_scale = [wd_in_words[:, 2 * V - HALF :], sb.tile([P, HALF], U8, name="x_scale1", align_bytes=64)]
 
@@ -173,7 +174,7 @@ def tile_attend_gml_nce_kernel(tc, xT, wd_words, wd_scales, wv_words, wv_scales,
         under_chunk1 = P - P // (2 * PACK)
         for s in (slice(under_chunk1, P), slice(0, under_chunk1)):
             nc.vector.tensor_copy(
-                out=wd_codes.bitcast(U16).rearrange("p (r s) -> p r s", r=PACK)[:, :, s],
+                out=wd_codes[:].bitcast(U16).rearrange("p (r s) -> p r s", r=PACK)[:, :, s],
                 in_=wd_in_words[:].bitcast(U16).rearrange("p (s r) -> p r s", r=PACK)[:, :, s],
             )
         sig_first = [sb.tile([P, HALF], F32, name=f"sig_first{r}") for r in range(PACK)]

@@ -22,11 +22,11 @@ P = 128
 PACK = 4
 HALF = N // 2
 ENTRIES = 16
-EARLY_TILES = 2
 OVERLAP = 32
 RUN = 4
 SHARE = 40
 OWN = P - SHARE
+LAST_OWN = 96
 PLACE = (0, 2, 1, 3)
 LOW, HIGH, BOTH = slice(0, P), slice(P, HALF), slice(0, HALF)
 
@@ -56,11 +56,13 @@ def tile_attend_gml_nce_kernel(tc, xT, wd_words, wd_scales, wv_words, wv_scales,
         cw4 = sb.tile([P, PACK], F32, name="cw4")
         rw_rows = sb.tile([P, P], F32, name="rw_rows", tag="rw_then_window")
         wd_in_words = sb.tile([P, 2 * V], U8, name="wd_in_words", align_bytes=64)
-        wd_in_scale = sb.tile([P, V], U8, name="wd_in_scale", tag="scale_then_back", align_bytes=64)
+        wd_in_scale = sb.tile([P, V], U8, name="wd_in_scale", tag="scale_then_window", align_bytes=64)
+        wv_scale = sb.tile([P, D], U8, name="wv_scale", align_bytes=64)
         wv_codes = sb.tile([P, 2 * D], U8, name="wv_codes", align_bytes=64)
         ident = sb.tile([P, P], F32, name="ident")
 
         nc.vector.memset(wd_in_scale[:].bitcast(I32), 0)
+        nc.vector.memset(wv_scale[:].bitcast(I32), 0)
         nc.gpsimd.memset(rw_rows[:], 0.0)
         make_identity(nc, ident[:])
 
@@ -75,6 +77,8 @@ def tile_attend_gml_nce_kernel(tc, xT, wd_words, wd_scales, wv_words, wv_scales,
         nc.sync.dma_start(out=wd_in_words[:].bitcast(I32), in_=wd_words[0].bitcast(I32))
         nc.sync.dma_start(out=y_half[0][:], in_=y_rows[:, :, 0:HALF])
         nc.sync.dma_start(out=y_half[1][:], in_=y_rows[:, :, HALF:N])
+        load_scale_rows(nc, wv_scale, wv_scales)
+        nc.sync.dma_start(out=wv_codes[:].bitcast(I32), in_=wv_words[0].bitcast(I32))
 
         window = [sb.tile([P, T], F32, name=f"window{j}") for j in range(2)]
         for j in range(2):
@@ -92,22 +96,6 @@ def tile_attend_gml_nce_kernel(tc, xT, wd_words, wd_scales, wv_words, wv_scales,
             nc.tensor.transpose(cw_spread[:, PLACE[r], :], cw4[:, r : r + 1].to_broadcast([P, P]), ident[:])
         window.append(sb.tile([P, T], F32, name="window2", tag="rw_then_window"))
         nc.gpsimd.memset(window[2][:].bitcast(I32), 0)
-        window.append(window[0])
-        bank_weight = []
-        for c in range(2):
-            rows = sb.tile([P, PACK, P], F32, name=f"weight_rows{c}")
-            nc.scalar.activation(out=rows[:], in_=cw_spread[:], func=ACT.Copy, scale=minus_rw[:, c : c + 1])
-            bank_weight.append(bank(5 + c, [P, PACK, P], f"bank_weight{c}"))
-            for r in range(PACK):
-                nc.tensor.transpose(bank_weight[c][:, r, :], rows[:, PLACE[r], :], ident[:])
-        gpsimd_weight = sb.tile([P, PACK, SHARE + P], F32, name="gpsimd_weight")
-        for r in range(PACK):
-            nc.scalar.activation(
-                out=gpsimd_weight[:, r, :],
-                in_=rw_spread[:].rearrange("q c i -> q (c i)")[:, OWN : 2 * P],
-                func=ACT.Copy,
-                scale=cw4[:, r : r + 1],
-            )
         turned_weight = sb.tile([P, V], F32, name="turned_weight")
         nc.scalar.activation(
             out=turned_weight[:].rearrange("q (k e) -> q k e", e=2),
@@ -116,6 +104,22 @@ def tile_attend_gml_nce_kernel(tc, xT, wd_words, wd_scales, wv_words, wv_scales,
             scale=minus_rw[:, 2:3],
         )
 
+        bank_weight = {}
+        for c, number in ((0, 5), (1, 6), (3, 4)):
+            rows = sb.tile([P, PACK, P], F32, name=f"weight_rows{c}")
+            nc.scalar.activation(out=rows[:], in_=cw_spread[:], func=ACT.Copy, scale=minus_rw[:, c : c + 1])
+            bank_weight[c] = bank(number, [P, PACK, P], f"bank_weight{c}")
+            for r in range(PACK):
+                nc.tensor.transpose(bank_weight[c][:, r, :], rows[:, PLACE[r], :], ident[:])
+        gpsimd_weight = sb.tile([P, PACK, SHARE + P - LAST_OWN], F32, name="gpsimd_weight")
+        for r in range(PACK):
+            nc.scalar.activation(
+                out=gpsimd_weight[:, r, :],
+                in_=rw_spread[:].rearrange("q c i -> q (c i)")[:, OWN : 2 * P - LAST_OWN],
+                func=ACT.Copy,
+                scale=cw4[:, r : r + 1],
+            )
+
         wd_codes = sb.tile([P, 2 * V], U8, name="wd_codes", align_bytes=64)
         wd_scale = sb.tile([P, V], U8, name="wd_scale", align_bytes=64)
         nc.gpsimd.tensor_copy(
@@ -123,15 +127,11 @@ def tile_attend_gml_nce_kernel(tc, xT, wd_words, wd_scales, wv_words, wv_scales,
             in_=wd_in_scale[:].rearrange("p (s r) -> p s r", r=PACK),
         )
 
-        g_columns = HALF + N
-        back_bytes = sb.tile([P, D + 5 * g_columns], U8, name="back_bytes", tag="scale_then_back", align_bytes=64)
-        wv_scale = back_bytes[:, 0:D]
-        g_scale = back_bytes[:, D : D + g_columns]
-        g_codes = back_bytes[:, D + g_columns :].bitcast(U32)
-        nc.gpsimd.memset(back_bytes[:, 0 : D + HALF].bitcast(I32), 0)
-        nc.gpsimd.memset(g_codes[:, 0:HALF], 0)
-        load_scale_rows(nc, wv_scale, wv_scales)
-        nc.sync.dma_start(out=wv_codes[:].bitcast(I32), in_=wv_words[0].bitcast(I32))
+        window.append(sb.tile([P, T], F32, name="window3", tag="scale_then_window", align_bytes=64))
+        nc.gpsimd.memset(window[3][:].bitcast(I32), 0)
+
+        g_scale = sb.tile([P, N], U8, name="g_scale", align_bytes=64)
+        g_codes = sb.tile([P, N], U32, name="g_codes", align_bytes=64)
 
         x_words = sb.tile([P, N, PACK], BF16, name="x_words", align_bytes=64)
         x_codes = [sb.tile([P, HALF], U32, name=f"x_codes{h}", align_bytes=64) for h in range(2)]
@@ -189,8 +189,8 @@ def tile_attend_gml_nce_kernel(tc, xT, wd_words, wd_scales, wv_words, wv_scales,
         gather(PACK - 1, HALF - OVERLAP, N)
         quantize_x(1, BOTH)
         sig_second = sb.tile([P, PACK, HALF], F32, name="sig_second")
-        sigmoid(sig_second[:, 0:2, :], scores(1, [0, 1], BOTH, 4)[:], -1.0)
-        score = scores(1, [2, 3], BOTH, 7)
+        sigmoid(sig_second[:, 0:2, :], scores(1, [0, 1], BOTH, 1)[:], -1.0)
+        score = scores(1, [2, 3], BOTH, 2)
         for cols in (LOW, HIGH):
             sigmoid(sig_second[:, 2:4, cols], score[:, :, cols], -1.0)
 
@@ -223,38 +223,48 @@ def tile_attend_gml_nce_kernel(tc, xT, wd_words, wd_scales, wv_words, wv_scales,
             )
 
         def quantize_g(words, first, end):
-            cols = slice(HALF + first, HALF + end)
+            cols = slice(first, end)
             nc.vector.quantize_mx(out=g_codes[:, cols].bitcast(E5M2X4), scales=g_scale[:, cols], in_=words)
 
         for r in range(PACK - 1):
             subtract_plane(r, slice(0, 2))
         for c in (1, 0):
             subtract_plane(PACK - 1, slice(c, c + 1))
-        weigh(nc.gpsimd, g_first[:, 1, PACK * OWN :], diff[:, 1, :, OWN:P], gpsimd_weight[:, :, 0:SHARE])
-        weigh(nc.vector, g_first[:, 1, 0 : PACK * OWN], diff[:, 1, :, 0:OWN], bank_weight[1][:, :, 0:OWN])
-        weigh(nc.vector, g_first[:, 2, :], diff[:, 0, :, :], bank_weight[0][:])
+        weigh(nc.gpsimd, g_first[:, 0, PACK * OWN :], diff[:, 1, :, OWN:P], gpsimd_weight[:, :, 0:SHARE])
+        weigh(nc.vector, g_first[:, 0, 0 : PACK * OWN], diff[:, 1, :, 0:OWN], bank_weight[1][:, :, 0:OWN])
+        weigh(nc.vector, g_first[:, 1, :], diff[:, 0, :, :], bank_weight[0][:])
         for c in (1, 0):
-            quantize_g(g_first[:, 2 - c, :], P * c, P * (c + 1))
+            quantize_g(g_first[:, 1 - c, :], P * c, P * (c + 1))
 
-        def back(j, first, number):
+        def back(j, first, end, number):
             acc = bank(number, [P, N], f"acc{j}_{first}")
             nc.tensor.matmul_mx(
-                out=acc[:],
+                out=acc[:, 0 : end - first],
                 lhsT=wv_codes[:, 2 * P * j : 2 * P * (j + 1)].bitcast(E2M1X4),
                 lhsT_scale=wv_scale[:, P * j : P * (j + 1)],
-                rhs=g_codes[:, first : first + N].bitcast(E5M2X4),
-                rhs_scale=g_scale[:, first : first + N],
+                rhs=g_codes[:, first:end].bitcast(E5M2X4),
+                rhs_scale=g_scale[:, first:end],
                 start=True,
                 stop=True,
             )
             return acc
 
-        early = [back(j, 0, 1 + j) for j in range(EARLY_TILES)]
+        def scatter_vector(j, dx, first, end):
+            nc.vector.tensor_copy(out=window[j][:].indirect(entries(first, end)), in_=dx)
 
-        diff_last = g_first[:, 0:2, :].rearrange("p c n -> p (c n)").bitcast(F32).rearrange("p (r i) -> p r i", i=P)
-        nc.vector.scalar_tensor_tensor(diff_last, sig_second[:, :, HIGH], -1.0, y_half[1][:, :, HIGH], ALU.add, ALU.add)
-        weigh(nc.gpsimd, g_second[:, 1, :], diff_last, gpsimd_weight[:, :, SHARE:])
-        g_turned = g_first[:, 2, :]
+        def scatter_scalar(j, dx, first, end):
+            nc.scalar.activation(out=window[j][:].indirect(entries(first, end)), in_=dx, func=ACT.Copy)
+
+        def store(j):
+            nc.sync.dma_start(out=out[P * j : P * (j + 1), :], in_=window[j][:])
+
+        dx = [sb.tile([P, N], F32, name=f"dx{j}") for j in range(PACK)]
+        early0 = back(0, 0, HALF, 3)
+        early1 = back(1, 0, HALF, 6)
+        nc.scalar.copy(out=dx[0][:, 0:HALF], in_=early0[:, 0:HALF])
+        scatter_scalar(0, dx[0][:, 0:HALF], 0, HALF)
+
+        g_turned = g_first[:, 0, :]
         nc.vector.scalar_tensor_tensor(
             g_turned.rearrange("q (k e) -> q k e", e=2),
             sums[:].rearrange("q (e u) p -> q (u p) e", e=2),
@@ -264,32 +274,38 @@ def tile_attend_gml_nce_kernel(tc, xT, wd_words, wd_scales, wv_words, wv_scales,
             ALU.mult,
         )
 
-        dx_first = sb.tile([P, HALF], F32, name="dx_first")
-        dx_early = [dx_first[:], g_turned.bitcast(F32)]
-        nc.scalar.copy(out=dx_early[0], in_=early[0][:, HALF:N])
-        pairs = bank(1, [P, 2, P], "pairs")
+        diff_last = g_first[:, 1:3, :].rearrange("p c n -> p (c n)").bitcast(F32).rearrange("p (r i) -> p r i", i=P)
+        nc.vector.scalar_tensor_tensor(diff_last, sig_second[:, :, HIGH], -1.0, y_half[1][:, :, HIGH], ALU.add, ALU.add)
+        split = P - LAST_OWN
+        weigh(nc.gpsimd, g_second[:, 1, 0 : PACK * split], diff_last[:, :, 0:split], gpsimd_weight[:, :, SHARE:])
+        pairs = early1[:, HALF:N].rearrange("p (u q) -> p u q", u=2)
         for u in range(2):
             nc.tensor.transpose(pairs[:, u, :], g_turned.bitcast(F32)[:, P * u : P * (u + 1)], ident[:])
-        nc.scalar.copy(
-            out=g_second[:, 0, :].bitcast(F32).rearrange("p (q u) -> p q u", u=2), in_=pairs[:].rearrange("p u q -> p q u")
+        nc.vector.tensor_copy(
+            out=g_second[:, 0, :].bitcast(F32).rearrange("p (q u) -> p q u", u=2), in_=pairs.rearrange("p u q -> p q u")
         )
-        nc.scalar.copy(out=dx_early[1], in_=early[1][:, HALF:N])
-
-        def scatter(j, dx, first, end):
-            nc.vector.tensor_copy(out=window[j][:].indirect(entries(first, end)), in_=dx)
-
-        scatter(0, dx_early[0], 0, HALF)
+        weigh(nc.vector, g_second[:, 1, PACK * split :], diff_last[:, :, split:P], bank_weight[3][:, :, split:P])
         quantize_g(g_second[:].rearrange("p c n -> p (c n)"), HALF, N)
 
-        dx_late = []
-        for j, number in enumerate((3, 4, 5, 6)):
-            acc = back(j, HALF, number)
-            first = HALF if j < EARLY_TILES else 0
-            dx = sb.tile([P, N - first], F32, name=f"dx_late{j}")
-            nc.scalar.copy(out=dx[:], in_=acc[:, first:N])
-            dx_late.append((dx, first))
-
-        scatter(1, dx_early[1], 0, HALF)
-        for j, (dx, first) in enumerate(dx_late):
-            scatter(j, dx[:], first, N)
-            nc.sync.dma_start(out=out[P * j : P * (j + 1), :], in_=window[j][:])
+        late0 = back(0, HALF, N, 2)
+        late2 = back(2, HALF, N, 5)
+        late1 = back(1, HALF, N, 1)
+        first2 = back(2, 0, HALF, 4)
+        whole3 = back(3, 0, N, 0)
+        nc.scalar.copy(out=dx[0][:, HALF:N], in_=late0[:, 0:HALF])
+        scatter_scalar(0, dx[0][:, HALF:N], HALF, N)
+        store(0)
+        dx1_first = g_second[:, 0, :].bitcast(F32)
+        nc.vector.tensor_copy(out=dx1_first, in_=early1[:, 0:HALF])
+        scatter_vector(1, dx1_first, 0, HALF)
+        nc.vector.tensor_copy(out=dx[1][:, HALF:N], in_=late1[:, 0:HALF])
+        scatter_vector(1, dx[1][:, HALF:N], HALF, N)
+        store(1)
+        nc.scalar.copy(out=dx[0][:, 0:HALF], in_=late2[:, 0:HALF])
+        scatter_scalar(2, dx[0][:, 0:HALF], HALF, N)
+        nc.scalar.copy(out=dx[0][:, HALF:N], in_=first2[:, 0:HALF])
+        scatter_scalar(2, dx[0][:, HALF:N], 0, HALF)
+        store(2)
+        nc.vector.tensor_copy(out=dx[3][:], in_=whole3[:])
+        scatter_vector(3, dx[3][:], 0, N)
+        store(3)

@@ -26,8 +26,7 @@ OVERLAP = 32
 RUN = 4
 SHARE = 40
 OWN = P - SHARE
-LAST_OWN = 96
-PLACE = (0, 2, 1, 3)
+LAST_OWN = 88
 LOW, HIGH, BOTH = slice(0, P), slice(P, HALF), slice(0, HALF)
 
 
@@ -65,6 +64,8 @@ def tile_attend_gml_nce_kernel(tc, xT, wd_words, wd_scales, wv_words, wv_scales,
         nc.vector.memset(wv_scale[:].bitcast(I32), 0)
         nc.gpsimd.memset(rw_rows[:], 0.0)
         make_identity(nc, ident[:])
+        zeros = sb.tile([P, P], F32, name="zeros")
+        nc.gpsimd.memset(zeros[:], 0.0)
 
         nc.sync.dma_start(out=x_plane[0][:], in_=x_rows[:, 0, :])
         nc.sync.dma_start(offsets[:], offs)
@@ -84,33 +85,25 @@ def tile_attend_gml_nce_kernel(tc, xT, wd_words, wd_scales, wv_words, wv_scales,
         for j in range(2):
             nc.vector.memset(window[j][:].bitcast(I32), 0)
 
-        rw_turned = bank(5, [P, P], "rw_turned")
+        rw_turned = bank(0, [P, P], "rw_turned")
         nc.tensor.transpose(rw_turned[:], rw_rows[:], ident[:])
         minus_rw = sb.tile([P, N // P], F32, name="minus_rw")
         nc.scalar.activation(out=minus_rw[:], in_=rw_turned[:, 0 : N // P], func=ACT.Copy, scale=-1.0)
-        rw_spread = bank(7, [P, 2, P], "rw_spread")
+        rw_spread = bank(1, [P, 2, P], "rw_spread")
         for k, c in enumerate((1, 3)):
             nc.tensor.transpose(rw_spread[:, k, :], minus_rw[:, c : c + 1].to_broadcast([P, P]), ident[:])
-        cw_spread = bank(4, [P, PACK, P], "cw_spread")
+        cw_spread = bank(2, [P, PACK, P], "cw_spread")
         for r in range(PACK):
-            nc.tensor.transpose(cw_spread[:, PLACE[r], :], cw4[:, r : r + 1].to_broadcast([P, P]), ident[:])
+            nc.tensor.transpose(cw_spread[:, r, :], cw4[:, r : r + 1].to_broadcast([P, P]), ident[:])
         window.append(sb.tile([P, T], F32, name="window2", tag="rw_then_window"))
         nc.gpsimd.memset(window[2][:].bitcast(I32), 0)
-        turned_weight = sb.tile([P, V], F32, name="turned_weight")
-        nc.scalar.activation(
-            out=turned_weight[:].rearrange("q (k e) -> q k e", e=2),
-            in_=cw_spread[:].rearrange("q (e u) p -> q (u p) e", e=2),
-            func=ACT.Copy,
-            scale=minus_rw[:, 2:3],
-        )
-
-        bank_weight = {}
-        for c, number in ((0, 5), (1, 6), (3, 4)):
+        bank_weight = []
+        for c in range(N // P):
             rows = sb.tile([P, PACK, P], F32, name=f"weight_rows{c}")
             nc.scalar.activation(out=rows[:], in_=cw_spread[:], func=ACT.Copy, scale=minus_rw[:, c : c + 1])
-            bank_weight[c] = bank(number, [P, PACK, P], f"bank_weight{c}")
+            bank_weight.append(bank(4 + c, [P, PACK, P], f"bank_weight{c}"))
             for r in range(PACK):
-                nc.tensor.transpose(bank_weight[c][:, r, :], rows[:, PLACE[r], :], ident[:])
+                nc.tensor.transpose(bank_weight[c][:, r, :], rows[:, r, :], ident[:])
         gpsimd_weight = sb.tile([P, PACK, SHARE + P - LAST_OWN], F32, name="gpsimd_weight")
         for r in range(PACK):
             nc.scalar.activation(
@@ -164,8 +157,8 @@ def tile_attend_gml_nce_kernel(tc, xT, wd_words, wd_scales, wv_words, wv_scales,
                 )
             return score
 
-        def sigmoid(result, score, sign):
-            nc.scalar.activation(out=result, in_=score, func=ACT.Sigmoid, scale=sign)
+        def sigmoid(result, score):
+            nc.scalar.activation(out=result, in_=score, func=ACT.Sigmoid)
 
         for t in range(PACK - 1):
             gather(t, 0, N)
@@ -178,33 +171,25 @@ def tile_attend_gml_nce_kernel(tc, xT, wd_words, wd_scales, wv_words, wv_scales,
                 in_=wd_in_words[:].bitcast(U16).rearrange("p (s r) -> p r s", r=PACK)[:, :, s],
             )
         sig_first = [sb.tile([P, HALF], F32, name=f"sig_first{r}") for r in range(PACK)]
-        for cols, number in ((HIGH, 7), (LOW, 0)):
+        for cols, number in ((HIGH, 0), (LOW, 1)):
             quantize_x(0, cols)
-            sigmoid(sig_first[0][:, cols], scores(0, [0], cols, number)[:, 0, :], 1.0)
+            sigmoid(sig_first[0][:, cols], scores(0, [0], cols, number)[:, 0, :])
         for r in range(1, PACK - 1):
-            sigmoid(sig_first[r][:], scores(0, [r], BOTH, r)[:, 0, :], 1.0)
-        score = scores(0, [PACK - 1], BOTH, PACK - 1)
+            sigmoid(sig_first[r][:], scores(0, [r], BOTH, 1 + r)[:, 0, :])
+        score = scores(0, [PACK - 1], BOTH, 0)
         for cols in (HIGH, LOW):
-            sigmoid(sig_first[PACK - 1][:, cols], score[:, 0, cols], 1.0)
+            sigmoid(sig_first[PACK - 1][:, cols], score[:, 0, cols])
         gather(PACK - 1, HALF - OVERLAP, N)
         quantize_x(1, BOTH)
         sig_second = sb.tile([P, PACK, HALF], F32, name="sig_second")
-        sigmoid(sig_second[:, 0:2, :], scores(1, [0, 1], BOTH, 1)[:], -1.0)
+        sigmoid(sig_second[:, 0:2, :], scores(1, [0, 1], BOTH, 1)[:])
         score = scores(1, [2, 3], BOTH, 2)
         for cols in (LOW, HIGH):
-            sigmoid(sig_second[:, 2:4, cols], score[:, :, cols], -1.0)
+            sigmoid(sig_second[:, 2:4, cols], score[:, :, cols])
 
         diff = sb.tile([P, 2, PACK, P], F32, name="diff")
-        g_first = sb.tile([P, 3, P * PACK], BF16, name="g_first", align_bytes=64)
+        g_first = sb.tile([P, 4, P * PACK], BF16, name="g_first", align_bytes=64)
         g_second = sb.tile([P, 2, P * PACK], BF16, name="g_second", align_bytes=64)
-
-        sums = bank(0, [P, PACK, P], "sums")
-        for r in range(PACK):
-            nc.tensor.matmul(sums[:, PLACE[r], :], y_half[1][:, r, LOW], ident[:], is_transpose=True, start=r == 0, stop=False)
-        for r in range(PACK):
-            nc.tensor.matmul(
-                sums[:, PLACE[r], :], sig_second[:, r, LOW], ident[:], is_transpose=True, start=False, stop=r == PACK - 1
-            )
 
         def subtract_plane(r, chunks):
             nc.vector.tensor_tensor(
@@ -232,25 +217,30 @@ def tile_attend_gml_nce_kernel(tc, xT, wd_words, wd_scales, wv_words, wv_scales,
             subtract_plane(PACK - 1, slice(c, c + 1))
         weigh(nc.gpsimd, g_first[:, 0, PACK * OWN :], diff[:, 1, :, OWN:P], gpsimd_weight[:, :, 0:SHARE])
         weigh(nc.vector, g_first[:, 0, 0 : PACK * OWN], diff[:, 1, :, 0:OWN], bank_weight[1][:, :, 0:OWN])
-        weigh(nc.vector, g_first[:, 1, :], diff[:, 0, :, :], bank_weight[0][:])
+        weigh(nc.vector, g_first[:, 2, :], diff[:, 0, :, :], bank_weight[0][:])
         for c in (1, 0):
-            quantize_g(g_first[:, 1 - c, :], P * c, P * (c + 1))
+            quantize_g(g_first[:, 2 - 2 * c, :], P * c, P * (c + 1))
 
-        def back(j, first, end, number):
+        def back(j, first, end, number, width=N):
             acc = bank(number, [P, N], f"acc{j}_{first}")
-            nc.tensor.matmul_mx(
-                out=acc[:, 0 : end - first],
-                lhsT=wv_codes[:, 2 * P * j : 2 * P * (j + 1)].bitcast(E2M1X4),
-                lhsT_scale=wv_scale[:, P * j : P * (j + 1)],
-                rhs=g_codes[:, first:end].bitcast(E5M2X4),
-                rhs_scale=g_scale[:, first:end],
-                start=True,
-                stop=True,
-            )
+            for start in range(first, end, width):
+                stop = min(end, start + width)
+                nc.tensor.matmul_mx(
+                    out=acc[:, start - first : stop - first],
+                    lhsT=wv_codes[:, 2 * P * j : 2 * P * (j + 1)].bitcast(E2M1X4),
+                    lhsT_scale=wv_scale[:, P * j : P * (j + 1)],
+                    rhs=g_codes[:, start:stop].bitcast(E5M2X4),
+                    rhs_scale=g_scale[:, start:stop],
+                    start=True,
+                    stop=True,
+                )
             return acc
 
         def scatter_vector(j, dx, first, end):
             nc.vector.tensor_copy(out=window[j][:].indirect(entries(first, end)), in_=dx)
+
+        def scatter_chunk(j, dx, first):
+            nc.vector.tensor_tensor(window[j][:].indirect(entries(first, first + P)), dx, zeros[:], ALU.add)
 
         def scatter_scalar(j, dx, first, end):
             nc.scalar.activation(out=window[j][:].indirect(entries(first, end)), in_=dx, func=ACT.Copy)
@@ -258,54 +248,43 @@ def tile_attend_gml_nce_kernel(tc, xT, wd_words, wd_scales, wv_words, wv_scales,
         def store(j):
             nc.sync.dma_start(out=out[P * j : P * (j + 1), :], in_=window[j][:])
 
-        dx = [sb.tile([P, N], F32, name=f"dx{j}") for j in range(PACK)]
+        dx = [sb.tile([P, N], F32, name=f"dx{j}") for j in range(2)]
         early0 = back(0, 0, HALF, 3)
-        early1 = back(1, 0, HALF, 6)
+        early1 = back(1, 0, HALF, 0)
         nc.scalar.copy(out=dx[0][:, 0:HALF], in_=early0[:, 0:HALF])
         scatter_scalar(0, dx[0][:, 0:HALF], 0, HALF)
+        nc.scalar.copy(out=dx[1][:, 0:HALF], in_=early1[:, 0:HALF])
+        scatter_scalar(1, dx[1][:, 0:HALF], 0, HALF)
 
-        g_turned = g_first[:, 0, :]
-        nc.vector.scalar_tensor_tensor(
-            g_turned.rearrange("q (k e) -> q k e", e=2),
-            sums[:].rearrange("q (e u) p -> q (u p) e", e=2),
-            -1.0,
-            turned_weight[:].rearrange("q (k e) -> q k e", e=2),
-            ALU.add,
-            ALU.mult,
-        )
-
-        diff_last = g_first[:, 1:3, :].rearrange("p c n -> p (c n)").bitcast(F32).rearrange("p (r i) -> p r i", i=P)
-        nc.vector.scalar_tensor_tensor(diff_last, sig_second[:, :, HIGH], -1.0, y_half[1][:, :, HIGH], ALU.add, ALU.add)
+        diff_late = [
+            g_first[:, 2 * c : 2 * c + 2, :].rearrange("p c n -> p (c n)").bitcast(F32).rearrange("p (r i) -> p r i", i=P)
+            for c in range(2)
+        ]
+        for c, cols in enumerate((LOW, HIGH)):
+            nc.vector.tensor_tensor(diff_late[c], y_half[1][:, :, cols], sig_second[:, :, cols], ALU.subtract)
         split = P - LAST_OWN
-        weigh(nc.gpsimd, g_second[:, 1, 0 : PACK * split], diff_last[:, :, 0:split], gpsimd_weight[:, :, SHARE:])
-        pairs = early1[:, HALF:N].rearrange("p (u q) -> p u q", u=2)
-        for u in range(2):
-            nc.tensor.transpose(pairs[:, u, :], g_turned.bitcast(F32)[:, P * u : P * (u + 1)], ident[:])
-        nc.vector.tensor_copy(
-            out=g_second[:, 0, :].bitcast(F32).rearrange("p (q u) -> p q u", u=2), in_=pairs.rearrange("p u q -> p q u")
-        )
-        weigh(nc.vector, g_second[:, 1, PACK * split :], diff_last[:, :, split:P], bank_weight[3][:, :, split:P])
-        quantize_g(g_second[:].rearrange("p c n -> p (c n)"), HALF, N)
+        weigh(nc.gpsimd, g_second[:, 1, 0 : PACK * split], diff_late[1][:, :, 0:split], gpsimd_weight[:, :, SHARE:])
+        weigh(nc.vector, g_second[:, 0, :], diff_late[0], bank_weight[2][:])
+        weigh(nc.vector, g_second[:, 1, PACK * split :], diff_late[1][:, :, split:P], bank_weight[3][:, :, split:P])
+        for c in range(2):
+            quantize_g(g_second[:, c, :], HALF + P * c, HALF + P * (c + 1))
 
-        late0 = back(0, HALF, N, 2)
-        late2 = back(2, HALF, N, 5)
+        late0 = [back(0, HALF + P * c, HALF + P * (c + 1), number) for c, number in enumerate((2, 4))]
         late1 = back(1, HALF, N, 1)
-        first2 = back(2, 0, HALF, 4)
-        whole3 = back(3, 0, N, 0)
-        nc.scalar.copy(out=dx[0][:, HALF:N], in_=late0[:, 0:HALF])
-        scatter_scalar(0, dx[0][:, HALF:N], HALF, N)
+        whole2 = back(2, 0, N, 5)
+        whole3 = back(3, 0, N, 6)
+        for c in range(2):
+            nc.vector.tensor_copy(out=dx[0][:, HALF + P * c : HALF + P * (c + 1)], in_=late0[c][:, 0:P])
+        for c in range(2):
+            scatter_chunk(0, dx[0][:, HALF + P * c : HALF + P * (c + 1)], HALF + P * c)
         store(0)
-        dx1_first = g_second[:, 0, :].bitcast(F32)
-        nc.vector.tensor_copy(out=dx1_first, in_=early1[:, 0:HALF])
-        scatter_vector(1, dx1_first, 0, HALF)
-        nc.vector.tensor_copy(out=dx[1][:, HALF:N], in_=late1[:, 0:HALF])
-        scatter_vector(1, dx[1][:, HALF:N], HALF, N)
+        nc.scalar.copy(out=dx[1][:, HALF:N], in_=late1[:, 0:HALF])
+        scatter_scalar(1, dx[1][:, HALF:N], HALF, N)
         store(1)
-        nc.scalar.copy(out=dx[0][:, 0:HALF], in_=late2[:, 0:HALF])
-        scatter_scalar(2, dx[0][:, 0:HALF], HALF, N)
-        nc.scalar.copy(out=dx[0][:, HALF:N], in_=first2[:, 0:HALF])
-        scatter_scalar(2, dx[0][:, HALF:N], 0, HALF)
+        nc.vector.tensor_copy(out=dx[0][:], in_=whole2[:])
+        scatter_vector(2, dx[0][:], 0, N)
         store(2)
-        nc.vector.tensor_copy(out=dx[3][:], in_=whole3[:])
-        scatter_vector(3, dx[3][:], 0, N)
+        for first in (0, HALF):
+            nc.scalar.copy(out=dx[1][:, first : first + HALF], in_=whole3[:, first : first + HALF])
+            scatter_scalar(3, dx[1][:, first : first + HALF], first, first + HALF)
         store(3)

@@ -24,9 +24,6 @@ HALF = N // 2
 ENTRIES = 16
 OVERLAP = 32
 RUN = 4
-SHARE = 40
-OWN = P - SHARE
-LAST_OWN = 88
 LOW, HIGH, BOTH = slice(0, P), slice(P, HALF), slice(0, HALF)
 
 
@@ -89,29 +86,14 @@ def tile_attend_gml_nce_kernel(tc, xT, wd_words, wd_scales, wv_words, wv_scales,
         nc.tensor.transpose(rw_turned[:], rw_rows[:], ident[:])
         minus_rw = sb.tile([P, N // P], F32, name="minus_rw")
         nc.scalar.activation(out=minus_rw[:], in_=rw_turned[:, 0 : N // P], func=ACT.Copy, scale=-1.0)
-        rw_spread = bank(1, [P, 2, P], "rw_spread")
-        for k, c in enumerate((1, 3)):
-            nc.tensor.transpose(rw_spread[:, k, :], minus_rw[:, c : c + 1].to_broadcast([P, P]), ident[:])
-        cw_spread = bank(2, [P, PACK, P], "cw_spread")
-        for r in range(PACK):
-            nc.tensor.transpose(cw_spread[:, r, :], cw4[:, r : r + 1].to_broadcast([P, P]), ident[:])
+        rw_spread = bank(1, [P, N], "rw_spread")
+        for c in range(N // P):
+            nc.tensor.transpose(rw_spread[:, P * c : P * (c + 1)], minus_rw[:, c : c + 1].to_broadcast([P, P]), ident[:])
         window.append(sb.tile([P, T], F32, name="window2", tag="rw_then_window"))
         nc.gpsimd.memset(window[2][:].bitcast(I32), 0)
-        bank_weight = []
-        for c in range(N // P):
-            rows = sb.tile([P, PACK, P], F32, name=f"weight_rows{c}")
-            nc.scalar.activation(out=rows[:], in_=cw_spread[:], func=ACT.Copy, scale=minus_rw[:, c : c + 1])
-            bank_weight.append(bank(4 + c, [P, PACK, P], f"bank_weight{c}"))
-            for r in range(PACK):
-                nc.tensor.transpose(bank_weight[c][:, r, :], rows[:, r, :], ident[:])
-        gpsimd_weight = sb.tile([P, PACK, SHARE + P - LAST_OWN], F32, name="gpsimd_weight")
+        weight = sb.tile([P, PACK, N], F32, name="weight")
         for r in range(PACK):
-            nc.scalar.activation(
-                out=gpsimd_weight[:, r, :],
-                in_=rw_spread[:].rearrange("q c i -> q (c i)")[:, OWN : 2 * P - LAST_OWN],
-                func=ACT.Copy,
-                scale=cw4[:, r : r + 1],
-            )
+            nc.scalar.activation(out=weight[:, r, :], in_=rw_spread[:], func=ACT.Copy, scale=cw4[:, r : r + 1])
 
         wd_codes = sb.tile([P, 2 * V], U8, name="wd_codes", align_bytes=64)
         wd_scale = sb.tile([P, V], U8, name="wd_scale", align_bytes=64)
@@ -170,40 +152,39 @@ def tile_attend_gml_nce_kernel(tc, xT, wd_words, wd_scales, wv_words, wv_scales,
                 out=wd_codes[:].bitcast(U16).rearrange("p (r s) -> p r s", r=PACK)[:, :, s],
                 in_=wd_in_words[:].bitcast(U16).rearrange("p (s r) -> p r s", r=PACK)[:, :, s],
             )
-        sig_first = [sb.tile([P, HALF], F32, name=f"sig_first{r}") for r in range(PACK)]
-        for cols, number in ((HIGH, 0), (LOW, 1)):
+        sig_first = [sb.tile([P, PACK, P], F32, name=f"sig_first{c}") for c in range(2)]
+        for c, cols in ((1, HIGH), (0, LOW)):
             quantize_x(0, cols)
-            sigmoid(sig_first[0][:, cols], scores(0, [0], cols, number)[:, 0, :])
-        for r in range(1, PACK - 1):
-            sigmoid(sig_first[r][:], scores(0, [r], BOTH, 1 + r)[:, 0, :])
-        score = scores(0, [PACK - 1], BOTH, 0)
-        for cols in (HIGH, LOW):
-            sigmoid(sig_first[PACK - 1][:, cols], score[:, 0, cols])
+            for u in range(2):
+                sigmoid(sig_first[c][:, 2 * u : 2 * u + 2, :], scores(0, [2 * u, 2 * u + 1], cols, 2 * c + u)[:])
         gather(PACK - 1, HALF - OVERLAP, N)
         quantize_x(1, BOTH)
         sig_second = sb.tile([P, PACK, HALF], F32, name="sig_second")
-        sigmoid(sig_second[:, 0:2, :], scores(1, [0, 1], BOTH, 1)[:])
-        score = scores(1, [2, 3], BOTH, 2)
+        sigmoid(sig_second[:, 0:2, :], scores(1, [0, 1], BOTH, 4)[:])
+        score = scores(1, [2, 3], BOTH, 5)
         for cols in (LOW, HIGH):
             sigmoid(sig_second[:, 2:4, cols], score[:, :, cols])
 
-        diff = sb.tile([P, 2, PACK, P], F32, name="diff")
-        g_first = sb.tile([P, 4, P * PACK], BF16, name="g_first", align_bytes=64)
+        shared = sb.tile([P, 2 * N], F32, name="shared", align_bytes=64)
+        diff1 = sb.tile([P, N], F32, name="diff1")
+        diff = [
+            part.rearrange("p (r i) -> p r i", i=P)
+            for part in (shared[:, HALF : HALF + N], diff1[:], shared[:, 0:N], shared[:, N : 2 * N])
+        ]
+        g_first = [shared[:, N + HALF :].bitcast(BF16), shared[:, 0:HALF].bitcast(BF16)]
         g_second = sb.tile([P, 2, P * PACK], BF16, name="g_second", align_bytes=64)
 
-        def subtract_plane(r, chunks):
+        def subtract_pair(c, u):
+            planes = slice(2 * u, 2 * u + 2)
             nc.vector.tensor_tensor(
-                diff[:, chunks, r, :],
-                y_half[0][:, r, :].rearrange("p (c i) -> p c i", i=P)[:, chunks, :],
-                sig_first[r][:].rearrange("p (c i) -> p c i", i=P)[:, chunks, :],
-                ALU.subtract,
+                diff[c][:, planes, :], y_half[0][:, planes, P * c : P * (c + 1)], sig_first[c][:, planes, :], ALU.subtract
             )
 
-        def weigh(engine, words, differences, weights):
-            engine.tensor_tensor(
+        def weigh(words, differences, c):
+            nc.vector.tensor_tensor(
                 words.rearrange("p (k i r) -> p k r i", i=RUN, r=PACK),
                 differences.rearrange("p r (k i) -> p k r i", i=RUN),
-                weights.rearrange("p r (k i) -> p k r i", i=RUN),
+                weight[:, :, P * c : P * (c + 1)].rearrange("p r (k i) -> p k r i", i=RUN),
                 ALU.mult,
             )
 
@@ -211,29 +192,20 @@ def tile_attend_gml_nce_kernel(tc, xT, wd_words, wd_scales, wv_words, wv_scales,
             cols = slice(first, end)
             nc.vector.quantize_mx(out=g_codes[:, cols].bitcast(E5M2X4), scales=g_scale[:, cols], in_=words)
 
-        for r in range(PACK - 1):
-            subtract_plane(r, slice(0, 2))
-        for c in (1, 0):
-            subtract_plane(PACK - 1, slice(c, c + 1))
-        weigh(nc.gpsimd, g_first[:, 0, PACK * OWN :], diff[:, 1, :, OWN:P], gpsimd_weight[:, :, 0:SHARE])
-        weigh(nc.vector, g_first[:, 0, 0 : PACK * OWN], diff[:, 1, :, 0:OWN], bank_weight[1][:, :, 0:OWN])
-        weigh(nc.vector, g_first[:, 2, :], diff[:, 0, :, :], bank_weight[0][:])
-        for c in (1, 0):
-            quantize_g(g_first[:, 2 - 2 * c, :], P * c, P * (c + 1))
+        def back_into(acc, j, first, end):
+            nc.tensor.matmul_mx(
+                out=acc,
+                lhsT=wv_codes[:, 2 * P * j : 2 * P * (j + 1)].bitcast(E2M1X4),
+                lhsT_scale=wv_scale[:, P * j : P * (j + 1)],
+                rhs=g_codes[:, first:end].bitcast(E5M2X4),
+                rhs_scale=g_scale[:, first:end],
+                start=True,
+                stop=True,
+            )
 
-        def back(j, first, end, number, width=N):
+        def back(j, first, end, number):
             acc = bank(number, [P, N], f"acc{j}_{first}")
-            for start in range(first, end, width):
-                stop = min(end, start + width)
-                nc.tensor.matmul_mx(
-                    out=acc[:, start - first : stop - first],
-                    lhsT=wv_codes[:, 2 * P * j : 2 * P * (j + 1)].bitcast(E2M1X4),
-                    lhsT_scale=wv_scale[:, P * j : P * (j + 1)],
-                    rhs=g_codes[:, start:stop].bitcast(E5M2X4),
-                    rhs_scale=g_scale[:, start:stop],
-                    start=True,
-                    stop=True,
-                )
+            back_into(acc[:, 0 : end - first], j, first, end)
             return acc
 
         def scatter_vector(j, dx, first, end):
@@ -248,41 +220,62 @@ def tile_attend_gml_nce_kernel(tc, xT, wd_words, wd_scales, wv_words, wv_scales,
         def store(j):
             nc.sync.dma_start(out=out[P * j : P * (j + 1), :], in_=window[j][:])
 
-        dx = [sb.tile([P, N], F32, name=f"dx{j}") for j in range(2)]
-        early0 = back(0, 0, HALF, 3)
-        early1 = back(1, 0, HALF, 0)
-        nc.scalar.copy(out=dx[0][:, 0:HALF], in_=early0[:, 0:HALF])
+        dx01 = sb.tile([P, 2, N], F32, name="dx01")
+        dx = [dx01[:, 0, :], dx01[:, 1, :], sb.tile([P, N], F32, name="dx2")]
+
+        def subtract_late(c, u):
+            planes, cols = slice(2 * u, 2 * u + 2), slice(P * c, P * (c + 1))
+            nc.vector.tensor_tensor(
+                diff[2 + c][:, planes, :], y_half[1][:, planes, cols], sig_second[:, planes, cols], ALU.subtract
+            )
+
+        def last_piece(c):
+            return dx[2][:, P * c : P * (c + 1)]
+
+        subtract_pair(1, 0)
+        subtract_pair(1, 1)
+        subtract_pair(0, 0)
+        weigh(g_first[1], diff[1], 1)
+        subtract_pair(0, 1)
+        quantize_g(g_first[1], P, HALF)
+        both = back(0, P, HALF, 6)
+        back_into(both[:, P:HALF], 1, P, HALF)
+        nc.scalar.copy(out=dx01[:, :, P:HALF], in_=both[:, 0:HALF].rearrange("p (j i) -> p j i", j=2))
+        weigh(g_first[0], diff[0], 0)
+        subtract_late(0, 0)
+        quantize_g(g_first[0], 0, P)
+
+        early0 = back(0, 0, P, 0)
+        early1 = back(1, 0, P, 1)
+        nc.scalar.copy(out=dx[0][:, 0:P], in_=early0[:, 0:P])
         scatter_scalar(0, dx[0][:, 0:HALF], 0, HALF)
-        nc.scalar.copy(out=dx[1][:, 0:HALF], in_=early1[:, 0:HALF])
+        nc.scalar.copy(out=dx[1][:, 0:P], in_=early1[:, 0:P])
         scatter_scalar(1, dx[1][:, 0:HALF], 0, HALF)
 
-        diff_late = [
-            g_first[:, 2 * c : 2 * c + 2, :].rearrange("p c n -> p (c n)").bitcast(F32).rearrange("p (r i) -> p r i", i=P)
-            for c in range(2)
-        ]
-        for c, cols in enumerate((LOW, HIGH)):
-            nc.vector.tensor_tensor(diff_late[c], y_half[1][:, :, cols], sig_second[:, :, cols], ALU.subtract)
-        split = P - LAST_OWN
-        weigh(nc.gpsimd, g_second[:, 1, 0 : PACK * split], diff_late[1][:, :, 0:split], gpsimd_weight[:, :, SHARE:])
-        weigh(nc.vector, g_second[:, 0, :], diff_late[0], bank_weight[2][:])
-        weigh(nc.vector, g_second[:, 1, PACK * split :], diff_late[1][:, :, split:P], bank_weight[3][:, :, split:P])
-        for c in range(2):
-            quantize_g(g_second[:, c, :], HALF + P * c, HALF + P * (c + 1))
-
-        late0 = [back(0, HALF + P * c, HALF + P * (c + 1), number) for c, number in enumerate((2, 4))]
-        late1 = back(1, HALF, N, 1)
-        whole2 = back(2, 0, N, 5)
-        whole3 = back(3, 0, N, 6)
-        for c in range(2):
-            nc.vector.tensor_copy(out=dx[0][:, HALF + P * c : HALF + P * (c + 1)], in_=late0[c][:, 0:P])
-        for c in range(2):
-            scatter_chunk(0, dx[0][:, HALF + P * c : HALF + P * (c + 1)], HALF + P * c)
+        subtract_late(0, 1)
+        subtract_late(1, 0)
+        weigh(g_second[:, 0, :], diff[2], 2)
+        subtract_late(1, 1)
+        quantize_g(g_second[:, 0, :], 2 * P, 3 * P)
+        piece2 = back(0, 2 * P, 3 * P, 3)
+        weigh(g_second[:, 1, :], diff[3], 3)
+        nc.vector.tensor_copy(out=last_piece(2), in_=piece2[:, 0:P])
+        quantize_g(g_second[:, 1, :], 3 * P, N)
+        piece3 = back(0, 3 * P, N, 4)
+        back_into(piece3[:, HALF:N], 2, 0, HALF)
+        late1 = back(1, HALF, N, 5)
+        late2 = back(2, HALF, N, 6)
+        whole3 = back(3, 0, N, 7)
+        scatter_chunk(0, last_piece(2), 2 * P)
+        nc.vector.tensor_copy(out=last_piece(3), in_=piece3[:, 0:P])
+        nc.vector.tensor_copy(out=dx[2][:, 0:HALF], in_=piece3[:, HALF:N])
+        scatter_chunk(0, last_piece(3), 3 * P)
         store(0)
         nc.scalar.copy(out=dx[1][:, HALF:N], in_=late1[:, 0:HALF])
         scatter_scalar(1, dx[1][:, HALF:N], HALF, N)
         store(1)
-        nc.vector.tensor_copy(out=dx[0][:], in_=whole2[:])
-        scatter_vector(2, dx[0][:], 0, N)
+        nc.vector.tensor_copy(out=dx[2][:, HALF:N], in_=late2[:, 0:HALF])
+        scatter_vector(2, dx[2][:], 0, N)
         store(2)
         for first in (0, HALF):
             nc.scalar.copy(out=dx[1][:, first : first + HALF], in_=whole3[:, first : first + HALF])

@@ -221,7 +221,7 @@ def tile_attend_gml_nce_kernel(tc, xT, wd_words, wd_scales, wv_words, wv_scales,
             nc.sync.dma_start(out=out[P * j : P * (j + 1), :], in_=window[j][:])
 
         dx01 = sb.tile([P, 2, N], F32, name="dx01")
-        dx = [dx01[:, 0, :], dx01[:, 1, :], sb.tile([P, N], F32, name="dx2")]
+        dx = [dx01[:, 0, :], dx01[:, 1, :], sb.tile([P, N + HALF], F32, name="dx23")]
 
         def subtract_late(c, u):
             planes, cols = slice(2 * u, 2 * u + 2), slice(P * c, P * (c + 1))
@@ -274,10 +274,10 @@ def tile_attend_gml_nce_kernel(tc, xT, wd_words, wd_scales, wv_words, wv_scales,
         nc.scalar.copy(out=dx[1][:, HALF:N], in_=late1[:, 0:HALF])
         scatter_scalar(1, dx[1][:, HALF:N], HALF, N)
         store(1)
-        nc.vector.tensor_copy(out=dx[2][:, HALF:N], in_=late2[:, 0:HALF])
-        scatter_vector(2, dx[2][:], 0, N)
+        scatter_vector(2, dx[2][:, 0:HALF], 0, HALF)
+        nc.scalar.copy(out=dx[0][:, 0:HALF], in_=late2[:, 0:HALF])
+        scatter_scalar(2, dx[0][:, 0:HALF], HALF, N)
         store(2)
-        for first in (0, HALF):
-            nc.scalar.copy(out=dx[1][:, first : first + HALF], in_=whole3[:, first : first + HALF])
-            scatter_scalar(3, dx[1][:, first : first + HALF], first, first + HALF)
+        nc.vector.tensor_copy(out=dx[2][:, HALF:], in_=whole3[:])
+        scatter_vector(3, dx[2][:, HALF:], 0, N)
         store(3)

@@ -50,7 +50,7 @@ def tile_attend_gml_nce_kernel(tc, xT, wd_words, wd_scales, wv_words, wv_scales,
         y_half = [sb.tile([P, PACK, HALF], F32, name=f"y_half{h}") for h in range(2)]
         offsets = sb.tile([P, N // ENTRIES], U16, name="offsets")
         cw4 = sb.tile([P, PACK], F32, name="cw4")
-        rw_rows = sb.tile([P, P], F32, name="rw_rows", tag="rw_then_window")
+        rw_rows = sb.tile([P, P], F32, name="rw_rows")
         wd_in_words = sb.tile([P, 2 * V], U8, name="wd_in_words", align_bytes=64)
         wd_in_scale = sb.tile([P, V], U8, name="wd_in_scale", tag="scale_then_window", align_bytes=64)
         wv_scale = sb.tile([P, D], U8, name="wv_scale", align_bytes=64)
@@ -89,8 +89,6 @@ def tile_attend_gml_nce_kernel(tc, xT, wd_words, wd_scales, wv_words, wv_scales,
         rw_spread = bank(1, [P, N], "rw_spread")
         for c in range(N // P):
             nc.tensor.transpose(rw_spread[:, P * c : P * (c + 1)], minus_rw[:, c : c + 1].to_broadcast([P, P]), ident[:])
-        window.append(sb.tile([P, T], F32, name="window2", tag="rw_then_window"))
-        nc.gpsimd.memset(window[2][:].bitcast(I32), 0)
         weight = sb.tile([P, PACK, N], F32, name="weight")
         for r in range(PACK):
             nc.scalar.activation(out=weight[:, r, :], in_=rw_spread[:], func=ACT.Copy, scale=cw4[:, r : r + 1])
@@ -102,8 +100,8 @@ def tile_attend_gml_nce_kernel(tc, xT, wd_words, wd_scales, wv_words, wv_scales,
             in_=wd_in_scale[:].rearrange("p (s r) -> p s r", r=PACK),
         )
 
-        window.append(sb.tile([P, T], F32, name="window3", tag="scale_then_window", align_bytes=64))
-        nc.gpsimd.memset(window[3][:].bitcast(I32), 0)
+        window.append(sb.tile([P, T], F32, name="window2", tag="scale_then_window", align_bytes=64))
+        nc.gpsimd.memset(window[2][:].bitcast(I32), 0)
 
         g_scale = sb.tile([P, N], U8, name="g_scale", align_bytes=64)
         g_codes = sb.tile([P, N], U32, name="g_codes", align_bytes=64)
@@ -172,7 +170,7 @@ def tile_attend_gml_nce_kernel(tc, xT, wd_words, wd_scales, wv_words, wv_scales,
             for part in (shared[:, HALF : HALF + N], diff1[:], shared[:, 0:N], shared[:, N : 2 * N])
         ]
         g_first = [shared[:, N + HALF :].bitcast(BF16), shared[:, 0:HALF].bitcast(BF16)]
-        g_second = sb.tile([P, 2, P * PACK], BF16, name="g_second", align_bytes=64)
+        g_second = sb.tile([P, 2, P * PACK], BF16, name="g_second", tag="words_then_window", align_bytes=64)
 
         def subtract_pair(c, u):
             planes = slice(2 * u, 2 * u + 2)
@@ -261,6 +259,8 @@ def tile_attend_gml_nce_kernel(tc, xT, wd_words, wd_scales, wv_words, wv_scales,
         weigh(g_second[:, 1, :], diff[3], 3)
         nc.vector.tensor_copy(out=last_piece(2), in_=piece2[:, 0:P])
         quantize_g(g_second[:, 1, :], 3 * P, N)
+        window.append(sb.tile([P, T], F32, name="window3", tag="words_then_window", align_bytes=64))
+        nc.gpsimd.memset(window[3][:].bitcast(I32), 0)
         piece3 = back(0, 3 * P, N, 4)
         back_into(piece3[:, HALF:N], 2, 0, HALF)
         late1 = back(1, HALF, N, 5)

@@ -64,6 +64,9 @@ def tile_attend_gml_nce_kernel(tc, xT, wd_words, wd_scales, wv_words, wv_scales,
         zeros = sb.tile([P, P], F32, name="zeros")
         nc.gpsimd.memset(zeros[:], 0.0)
 
+        warm = sb.tile([P, 1], F32, name="warm")
+        nc.scalar.activation(out=warm[:], in_=zeros[:, 0:1], func=ACT.Sigmoid)
+
         nc.sync.dma_start(out=x_plane[0][:], in_=x_rows[:, 0, :])
         nc.sync.dma_start(offsets[:], offs)
         load_scale_rows(nc, wd_in_scale, wd_scales)
@@ -144,6 +147,8 @@ def tile_attend_gml_nce_kernel(tc, xT, wd_words, wd_scales, wv_words, wv_scales,
             gather(t, 0, N)
 
         gather(PACK - 1, 0, HALF)
+        picked = sb.tile([P, HALF + OVERLAP], BF16, name="picked", align_bytes=64)
+        nc.scalar.activation(out=picked[:], in_=x_plane[PACK - 1][:].indirect(entries(HALF - OVERLAP, N)), func=ACT.Copy)
         under_chunk1 = P - P // (2 * PACK)
         for s in (slice(under_chunk1, P), slice(0, under_chunk1)):
             nc.vector.tensor_copy(
@@ -155,7 +160,7 @@ def tile_attend_gml_nce_kernel(tc, xT, wd_words, wd_scales, wv_words, wv_scales,
             quantize_x(0, cols)
             for u in range(2):
                 sigmoid(sig_first[c][:, 2 * u : 2 * u + 2, :], scores(0, [2 * u, 2 * u + 1], cols, 2 * c + u)[:])
-        gather(PACK - 1, HALF - OVERLAP, N)
+        nc.vector.tensor_copy(out=x_words[:, HALF - OVERLAP : N, PACK - 1], in_=picked[:])
         quantize_x(1, BOTH)
         sig_second = sb.tile([P, PACK, HALF], F32, name="sig_second")
         sigmoid(sig_second[:, 0:2, :], scores(1, [0, 1], BOTH, 4)[:])
@@ -233,21 +238,20 @@ def tile_attend_gml_nce_kernel(tc, xT, wd_words, wd_scales, wv_words, wv_scales,
         subtract_pair(1, 0)
         subtract_pair(1, 1)
         subtract_pair(0, 0)
-        weigh(g_first[1], diff[1], 1)
         subtract_pair(0, 1)
-        quantize_g(g_first[1], P, HALF)
-        both = back(0, P, HALF, 6)
-        back_into(both[:, P:HALF], 1, P, HALF)
-        nc.scalar.copy(out=dx01[:, :, P:HALF], in_=both[:, 0:HALF].rearrange("p (j i) -> p j i", j=2))
+        weigh(g_first[1], diff[1], 1)
         weigh(g_first[0], diff[0], 0)
-        subtract_late(0, 0)
+        quantize_g(g_first[1], P, HALF)
         quantize_g(g_first[0], 0, P)
+        high0 = back(0, P, HALF, 6)
+        nc.scalar.copy(out=dx[0][:, P:HALF], in_=high0[:, 0:P])
+        subtract_late(0, 0)
 
         early0 = back(0, 0, P, 0)
-        early1 = back(1, 0, P, 1)
+        early1 = back(1, 0, HALF, 1)
         nc.scalar.copy(out=dx[0][:, 0:P], in_=early0[:, 0:P])
         scatter_scalar(0, dx[0][:, 0:HALF], 0, HALF)
-        nc.scalar.copy(out=dx[1][:, 0:P], in_=early1[:, 0:P])
+        nc.scalar.copy(out=dx[1][:, 0:HALF], in_=early1[:, 0:HALF])
         scatter_scalar(1, dx[1][:, 0:HALF], 0, HALF)
 
         subtract_late(0, 1)

@@ -96,7 +96,7 @@ def tile_attend_gml_nce_kernel(tc, xT, wd_words, wd_scales, wv_words, wv_scales,
         for r in range(PACK):
             nc.scalar.activation(out=weight[:, r, :], in_=rw_spread[:], func=ACT.Copy, scale=cw4[:, r : r + 1])
 
-        wd_codes = sb.tile([P, 2 * V], U8, name="wd_codes", align_bytes=64)
+        wd_codes = [sb.tile([P, V], U8, name=f"wd_codes{u}", align_bytes=64) for u in range(2)]
         wd_scale = sb.tile([P, V], U8, name="wd_scale", align_bytes=64)
         nc.gpsimd.tensor_copy(
             out=wd_scale[:].rearrange("p (r s) -> p s r", r=PACK),
@@ -111,7 +111,7 @@ def tile_attend_gml_nce_kernel(tc, xT, wd_words, wd_scales, wv_words, wv_scales,
 
         x_words = sb.tile([P, N, PACK], BF16, name="x_words", align_bytes=64)
         x_codes = [sb.tile([P, HALF], U32, name=f"x_codes{h}", align_bytes=64) for h in range(2)]
-        x_scale = [wd_in_words[:, 2 * V - HALF :], sb.tile([P, HALF], U8, name="x_scale1", align_bytes=64)]
+        x_scale = [sb.tile([P, HALF], U8, name=f"x_scale{h}", align_bytes=64) for h in range(2)]
 
         def entries(first, end):
             return offsets[:, first // ENTRIES : end // ENTRIES]
@@ -131,7 +131,7 @@ def tile_attend_gml_nce_kernel(tc, xT, wd_words, wd_scales, wv_words, wv_scales,
             for u, r in enumerate(planes):
                 nc.tensor.matmul_mx(
                     out=score[:, u, :],
-                    lhsT=wd_codes[:, 2 * P * r : 2 * P * (r + 1)].bitcast(E2M1X4),
+                    lhsT=wd_codes[r // 2][:, 2 * P * (r % 2) : 2 * P * (r % 2 + 1)].bitcast(E2M1X4),
                     lhsT_scale=wd_scale[:, P * r : P * (r + 1)],
                     rhs=x_codes[h][:, cols].bitcast(E4M3X4),
                     rhs_scale=x_scale[h][:, cols],
@@ -146,21 +146,25 @@ def tile_attend_gml_nce_kernel(tc, xT, wd_words, wd_scales, wv_words, wv_scales,
         for t in range(PACK - 1):
             gather(t, 0, N)
 
-        gather(PACK - 1, 0, HALF)
-        picked = sb.tile([P, HALF + OVERLAP], BF16, name="picked", align_bytes=64)
-        nc.scalar.activation(out=picked[:], in_=x_plane[PACK - 1][:].indirect(entries(HALF - OVERLAP, N)), func=ACT.Copy)
-        under_chunk1 = P - P // (2 * PACK)
-        for s in (slice(under_chunk1, P), slice(0, under_chunk1)):
-            nc.vector.tensor_copy(
-                out=wd_codes[:].bitcast(U16).rearrange("p (r s) -> p r s", r=PACK)[:, :, s],
-                in_=wd_in_words[:].bitcast(U16).rearrange("p (s r) -> p r s", r=PACK)[:, :, s],
+        last = x_plane[PACK - 1]
+        picked = [sb.tile([P, P], BF16, name=f"picked{c}", align_bytes=64) for c in range(2)]
+        picked_late = sb.tile([P, HALF + OVERLAP], BF16, name="picked_late", align_bytes=64)
+        for c in (1, 0):
+            nc.vector.tensor_copy(out=picked[c][:], in_=last[:].indirect(entries(P * c, P * (c + 1))))
+        nc.scalar.activation(out=picked_late[:], in_=last[:].indirect(entries(HALF - OVERLAP, N)), func=ACT.Copy)
+        for c in (1, 0):
+            nc.vector.tensor_copy(out=x_words[:, P * c : P * (c + 1), PACK - 1], in_=picked[c][:])
+        for u in range(2):
+            nc.scalar.copy(
+                out=wd_codes[u][:].bitcast(U16).rearrange("p (r s) -> p r s", r=2),
+                in_=wd_in_words[:].bitcast(U16).rearrange("p (s r) -> p r s", r=PACK)[:, 2 * u : 2 * u + 2, :],
             )
         sig_first = [sb.tile([P, PACK, P], F32, name=f"sig_first{c}") for c in range(2)]
         for c, cols in ((1, HIGH), (0, LOW)):
             quantize_x(0, cols)
             for u in range(2):
                 sigmoid(sig_first[c][:, 2 * u : 2 * u + 2, :], scores(0, [2 * u, 2 * u + 1], cols, 2 * c + u)[:])
-        nc.vector.tensor_copy(out=x_words[:, HALF - OVERLAP : N, PACK - 1], in_=picked[:])
+        nc.vector.tensor_copy(out=x_words[:, HALF - OVERLAP : N, PACK - 1], in_=picked_late[:])
         quantize_x(1, BOTH)
         sig_second = sb.tile([P, PACK, HALF], F32, name="sig_second")
         sigmoid(sig_second[:, 0:2, :], scores(1, [0, 1], BOTH, 4)[:])

from contextlib import ExitStack

import concourse.mybir as mybir
from concourse.masks import make_identity

N, T, D, V = 512, 2048, 512, 512
FLOPS = 2 * 2 * N * D * V

F32 = mybir.dt.float32
BF16 = mybir.dt.bfloat16
I32 = mybir.dt.int32
U32 = mybir.dt.uint32
U16 = mybir.dt.uint16
U8 = mybir.dt.uint8
E4M3X4 = mybir.dt.float8_e4m3fn_x4
E5M2X4 = mybir.dt.float8_e5m2_x4
E2M1X4 = mybir.dt.float4_e2m1fn_x4
ACT = mybir.ActivationFunctionType
ALU = mybir.AluOpType

P = 128
PACK = 4
HALF = N // 2
ENTRIES = 16
OVERLAP = 32
RUN = 4
LOW, HIGH, BOTH = slice(0, P), slice(P, HALF), slice(0, HALF)


def load_scale_rows(nc, tile, scales):
    for q in range(4):
        nc.sync.dma_start(
            out=tile[32 * q : 32 * q + 4, :].bitcast(I32),
            in_=scales[0, 4 * q : 4 * q + 4, :].bitcast(I32),
        )


def tile_attend_gml_nce_kernel(tc, xT, wd_words, wd_scales, wv_words, wv_scales, y, cw, rw, offs, out):
    nc = tc.nc
    with ExitStack() as ctx:
        sb = ctx.enter_context(tc.tile_pool(name="sb", bufs=1))
        ps = ctx.enter_context(tc.psum_pool(name="ps", bufs=1))

        def bank(number, shape, name):
            return ps.tile(shape, F32, name=name, tag=f"bank{number}")

        x_rows = xT.rearrange("(p t) n -> p t n", t=PACK)
        y_rows = y.rearrange("(p r) n -> p r n", r=PACK)
        x_plane = [sb.tile([P, T], F32, name=f"x_plane{t}", align_bytes=64) for t in range(PACK)]
        y_half = [sb.tile([P, PACK, HALF], F32, name=f"y_half{h}") for h in range(2)]
        offsets = sb.tile([P, N // ENTRIES], U16, name="offsets")
        cw4 = sb.tile([P, PACK], F32, name="cw4")
        rw_rows = sb.tile([P, P], F32, name="rw_rows")
        wd_in_words = sb.tile([P, 2 * V], U8, name="wd_in_words", align_bytes=64)
        wd_in_scale = sb.tile([P, V], U8, name="wd_in_scale", tag="scale_then_window", align_bytes=64)
        wv_scale = sb.tile([P, D], U8, name="wv_scale", align_bytes=64)
        wv_codes = sb.tile([P, 2 * D], U8, name="wv_codes", align_bytes=64)
        ident = sb.tile([P, P], F32, name="ident")

        nc.vector.memset(wd_in_scale[:].bitcast(I32), 0)
        nc.vector.memset(wv_scale[:].bitcast(I32), 0)
        nc.gpsimd.memset(rw_rows[:], 0.0)
        make_identity(nc, ident[:])
        zeros = sb.tile([P, P], F32, name="zeros")
        nc.gpsimd.memset(zeros[:], 0.0)

        warm = sb.tile([P, 1], F32, name="warm")
        nc.scalar.activation(out=warm[:], in_=zeros[:, 0:1], func=ACT.Sigmoid)

        nc.sync.dma_start(out=x_plane[0][:], in_=x_rows[:, 0, :])
        nc.sync.dma_start(offsets[:], offs)
        load_scale_rows(nc, wd_in_scale, wd_scales)
        nc.sync.dma_start(out=x_plane[1][:], in_=x_rows[:, 1, :])
        nc.sync.dma_start(out=rw_rows[0 : N // P, :], in_=rw[0].rearrange("(c q) -> c q", q=P))
        nc.sync.dma_start(out=cw4[:], in_=cw.rearrange("(p r) o -> p (r o)", r=PACK))
        nc.sync.dma_start(out=x_plane[2][:], in_=x_rows[:, 2, :])
        nc.sync.dma_start(out=x_plane[3][:], in_=x_rows[:, 3, :])
        nc.sync.dma_start(out=wd_in_words[:].bitcast(I32), in_=wd_words[0].bitcast(I32))
        nc.sync.dma_start(out=y_half[0][:], in_=y_rows[:, :, 0:HALF])
        nc.sync.dma_start(out=y_half[1][:], in_=y_rows[:, :, HALF:N])
        load_scale_rows(nc, wv_scale, wv_scales)
        nc.sync.dma_start(out=wv_codes[:].bitcast(I32), in_=wv_words[0].bitcast(I32))

        window = [sb.tile([P, T], F32, name=f"window{j}") for j in range(2)]
        for j in range(2):
            nc.vector.memset(window[j][:].bitcast(I32), 0)

        rw_turned = bank(0, [P, P], "rw_turned")
        nc.tensor.transpose(rw_turned[:], rw_rows[:], ident[:])
        minus_rw = sb.tile([P, N // P], F32, name="minus_rw")
        nc.scalar.activation(out=minus_rw[:], in_=rw_turned[:, 0 : N // P], func=ACT.Copy, scale=-1.0)
        rw_spread = bank(1, [P, N], "rw_spread")
        for c in range(N // P):
            nc.tensor.transpose(rw_spread[:, P * c : P * (c + 1)], minus_rw[:, c : c + 1].to_broadcast([P, P]), ident[:])
        weight = sb.tile([P, PACK, N], F32, name="weight")
        for r in range(PACK):
            nc.scalar.activation(out=weight[:, r, :], in_=rw_spread[:], func=ACT.Copy, scale=cw4[:, r : r + 1])

        wd_codes = [sb.tile([P, V], U8, name=f"wd_codes{u}", align_bytes=64) for u in range(2)]
        wd_scale = sb.tile([P, V], U8, name="wd_scale", align_bytes=64)
        nc.gpsimd.tensor_copy(
            out=wd_scale[:].rearrange("p (r s) -> p s r", r=PACK),
            in_=wd_in_scale[:].rearrange("p (s r) -> p s r", r=PACK),
        )

        window.append(sb.tile([P, T], F32, name="window2", tag="scale_then_window", align_bytes=64))
        nc.gpsimd.memset(window[2][:].bitcast(I32), 0)

        g_scale = sb.tile([P, N], U8, name="g_scale", align_bytes=64)
        g_codes = sb.tile([P, N], U32, name="g_codes", align_bytes=64)

        x_words = sb.tile([P, N, PACK], BF16, name="x_words", align_bytes=64)
        x_codes = [sb.tile([P, HALF], U32, name=f"x_codes{h}", align_bytes=64) for h in range(2)]
        x_scale = [sb.tile([P, HALF], U8, name=f"x_scale{h}", align_bytes=64) for h in range(2)]

        def entries(first, end):
            return offsets[:, first // ENTRIES : end // ENTRIES]

        def gather(t, first, end):
            nc.vector.tensor_copy(out=x_words[:, first:end, t], in_=x_plane[t][:].indirect(entries(first, end)))

        def quantize_x(h, cols):
            nc.vector.quantize_mx(
                out=x_codes[h][:, cols].bitcast(E4M3X4),
                scales=x_scale[h][:, cols],
                in_=x_words[:, HALF * h : HALF * (h + 1), :][:, cols, :].rearrange("p n t -> p (n t)"),
            )

        def scores(h, planes, cols, number):
            score = bank(number, [P, len(planes), cols.stop - cols.start], f"score{number}")
            for u, r in enumerate(planes):
                nc.tensor.matmul_mx(
                    out=score[:, u, :],
                    lhsT=wd_codes[r // 2][:, 2 * P * (r % 2) : 2 * P * (r % 2 + 1)].bitcast(E2M1X4),
                    lhsT_scale=wd_scale[:, P * r : P * (r + 1)],
                    rhs=x_codes[h][:, cols].bitcast(E4M3X4),
                    rhs_scale=x_scale[h][:, cols],
                    start=True,
                    stop=True,
                )
            return score

        def sigmoid(result, score):
            nc.scalar.activation(out=result, in_=score, func=ACT.Sigmoid)

        for t in range(PACK - 1):
            gather(t, 0, N)

        last = x_plane[PACK - 1]
        picked = [sb.tile([P, P], BF16, name=f"picked{c}", align_bytes=64) for c in range(2)]
        picked_late = sb.tile([P, HALF + OVERLAP], BF16, name="picked_late", align_bytes=64)
        for c in (1, 0):
            nc.vector.tensor_copy(out=picked[c][:], in_=last[:].indirect(entries(P * c, P * (c + 1))))
        nc.scalar.activation(out=picked_late[:], in_=last[:].indirect(entries(HALF - OVERLAP, N)), func=ACT.Copy)
        for c in (1, 0):
            nc.vector.tensor_copy(out=x_words[:, P * c : P * (c + 1), PACK - 1], in_=picked[c][:])
        for u in range(2):
            nc.scalar.copy(
                out=wd_codes[u][:].bitcast(U16).rearrange("p (r s) -> p r s", r=2),
                in_=wd_in_words[:].bitcast(U16).rearrange("p (s r) -> p r s", r=PACK)[:, 2 * u : 2 * u + 2, :],
            )
        sig_first = [sb.tile([P, PACK, P], F32, name=f"sig_first{c}") for c in range(2)]
        for c, cols in ((1, HIGH), (0, LOW)):
            quantize_x(0, cols)
            for u in range(2):
                sigmoid(sig_first[c][:, 2 * u : 2 * u + 2, :], scores(0, [2 * u, 2 * u + 1], cols, 2 * c + u)[:])
        nc.vector.tensor_copy(out=x_words[:, HALF - OVERLAP : N, PACK - 1], in_=picked_late[:])
        quantize_x(1, BOTH)
        sig_second = sb.tile([P, PACK, HALF], F32, name="sig_second")
        sigmoid(sig_second[:, 0:2, :], scores(1, [0, 1], BOTH, 4)[:])
        score = scores(1, [2, 3], BOTH, 5)
        for cols in (LOW, HIGH):
            sigmoid(sig_second[:, 2:4, cols], score[:, :, cols])

        shared = sb.tile([P, 2 * N], F32, name="shared", align_bytes=64)
        diff1 = sb.tile([P, N], F32, name="diff1")
        diff = [
            part.rearrange("p (r i) -> p r i", i=P)
            for part in (shared[:, HALF : HALF + N], diff1[:], shared[:, 0:N], shared[:, N : 2 * N])
        ]
        g_first = [shared[:, N + HALF :].bitcast(BF16), shared[:, 0:HALF].bitcast(BF16)]
        g_second = sb.tile([P, 2, P * PACK], BF16, name="g_second", tag="words_then_window", align_bytes=64)

        def subtract_pair(c, u):
            planes = slice(2 * u, 2 * u + 2)
            nc.vector.tensor_tensor(
                diff[c][:, planes, :], y_half[0][:, planes, P * c : P * (c + 1)], sig_first[c][:, planes, :], ALU.subtract
            )

        def weigh(words, differences, c):
            nc.vector.tensor_tensor(
                words.rearrange("p (k i r) -> p k r i", i=RUN, r=PACK),
                differences.rearrange("p r (k i) -> p k r i", i=RUN),
                weight[:, :, P * c : P * (c + 1)].rearrange("p r (k i) -> p k r i", i=RUN),
                ALU.mult,
            )

        def quantize_g(words, first, end):
            cols = slice(first, end)
            nc.vector.quantize_mx(out=g_codes[:, cols].bitcast(E5M2X4), scales=g_scale[:, cols], in_=words)

        def back_into(acc, j, first, end):
            nc.tensor.matmul_mx(
                out=acc,
                lhsT=wv_codes[:, 2 * P * j : 2 * P * (j + 1)].bitcast(E2M1X4),
                lhsT_scale=wv_scale[:, P * j : P * (j + 1)],
                rhs=g_codes[:, first:end].bitcast(E5M2X4),
                rhs_scale=g_scale[:, first:end],
                start=True,
                stop=True,
            )

        def back(j, first, end, number):
            acc = bank(number, [P, N], f"acc{j}_{first}")
            back_into(acc[:, 0 : end - first], j, first, end)
            return acc

        def scatter_vector(j, dx, first, end):
            nc.vector.tensor_copy(out=window[j][:].indirect(entries(first, end)), in_=dx)

        def scatter_chunk(j, dx, first):
            nc.vector.tensor_tensor(window[j][:].indirect(entries(first, first + P)), dx, zeros[:], ALU.add)

        def scatter_scalar(j, dx, first, end):
            nc.scalar.activation(out=window[j][:].indirect(entries(first, end)), in_=dx, func=ACT.Copy)

        def store(j):
            nc.sync.dma_start(out=out[P * j : P * (j + 1), :], in_=window[j][:])

        dx01 = sb.tile([P, 2, N], F32, name="dx01")
        dx = [dx01[:, 0, :], dx01[:, 1, :], sb.tile([P, N + HALF], F32, name="dx23")]

        def subtract_late(c, u):
            planes, cols = slice(2 * u, 2 * u + 2), slice(P * c, P * (c + 1))
            nc.vector.tensor_tensor(
                diff[2 + c][:, planes, :], y_half[1][:, planes, cols], sig_second[:, planes, cols], ALU.subtract
            )

        def last_piece(c):
            return dx[2][:, P * c : P * (c + 1)]

        subtract_pair(1, 0)
        subtract_pair(1, 1)
        subtract_pair(0, 0)
        subtract_pair(0, 1)
        weigh(g_first[1], diff[1], 1)
        weigh(g_first[0], diff[0], 0)
        quantize_g(g_first[1], P, HALF)
        quantize_g(g_first[0], 0, P)
        high0 = back(0, P, HALF, 6)
        nc.scalar.copy(out=dx[0][:, P:HALF], in_=high0[:, 0:P])
        subtract_late(0, 0)

        early0 = back(0, 0, P, 0)
        early1 = back(1, 0, HALF, 1)
        nc.scalar.copy(out=dx[0][:, 0:P], in_=early0[:, 0:P])
        scatter_scalar(0, dx[0][:, 0:HALF], 0, HALF)
        nc.scalar.copy(out=dx[1][:, 0:HALF], in_=early1[:, 0:HALF])
        scatter_scalar(1, dx[1][:, 0:HALF], 0, HALF)

        subtract_late(0, 1)
        subtract_late(1, 0)
        weigh(g_second[:, 0, :], diff[2], 2)
        subtract_late(1, 1)
        quantize_g(g_second[:, 0, :], 2 * P, 3 * P)
        piece2 = back(0, 2 * P, 3 * P, 3)
        weigh(g_second[:, 1, :], diff[3], 3)
        nc.vector.tensor_copy(out=last_piece(2), in_=piece2[:, 0:P])
        quantize_g(g_second[:, 1, :], 3 * P, N)
        window.append(sb.tile([P, T], F32, name="window3", tag="words_then_window", align_bytes=64))
        nc.gpsimd.memset(window[3][:].bitcast(I32), 0)
        piece3 = back(0, 3 * P, N, 4)
        back_into(piece3[:, HALF:N], 2, 0, HALF)
        late1 = back(1, HALF, N, 5)
        late2 = back(2, HALF, N, 6)
        whole3 = back(3, 0, N, 7)
        scatter_chunk(0, last_piece(2), 2 * P)
        nc.vector.tensor_copy(out=last_piece(3), in_=piece3[:, 0:P])
        nc.vector.tensor_copy(out=dx[2][:, 0:HALF], in_=piece3[:, HALF:N])
        scatter_chunk(0, last_piece(3), 3 * P)
        store(0)
        nc.scalar.copy(out=dx[1][:, HALF:N], in_=late1[:, 0:HALF])
        scatter_scalar(1, dx[1][:, HALF:N], HALF, N)
        store(1)
        scatter_vector(2, dx[2][:, 0:HALF], 0, HALF)
        nc.scalar.copy(out=dx[0][:, 0:HALF], in_=late2[:, 0:HALF])
        scatter_scalar(2, dx[0][:, 0:HALF], HALF, N)
        store(2)
        nc.vector.tensor_copy(out=dx[2][:, HALF:], in_=whole3[:])
        scatter_vector(3, dx[2][:, HALF:], 0, N)
        store(3)
